import numpy as np, ml_dtypes
CORES = [5,29,101,125,133,157,229,253]
N = 8
BF = ml_dtypes.bfloat16
def gentries(a):
    return np.ascontiguousarray(a.reshape(8, 16, -1).transpose(0, 2, 1)).reshape(8, -1)
def gtable(e):
    e = np.asarray(e); return np.ascontiguousarray(e.reshape(8, -1, 16).transpose(0, 2, 1)).reshape(128, -1).astype(np.int32)
V, WN, M, S, RO, LIM, PEN, T0 = 2048, 1024, 256, 4, 2, 28, 33, 34816
H = WN // 2
def parts(rng):
    return rng.integers(0, 256, (N, 8, 16, V)), rng.integers(0, V, (N, 8, 16, WN)), rng.integers(0, V, (N, 8, M)), rng.integers(0, 256, (N, 8, 16, M))
def pack(X, O, v, z):
    return {"tracks": np.ascontiguousarray(X.reshape(N, 128, V)).astype(np.float32).astype(BF),
            "nb": np.ascontiguousarray((O[..., :H] + V * O[..., H:]).reshape(N, 128, H)).astype(np.int32),
            "v": np.stack([gtable(a) for a in v]), "z": np.ascontiguousarray(z.reshape(N, 128, M)).astype(np.float32).astype(BF)}
def bits(b):
    return 255 * ((np.asarray(b)[..., None] >> (15 - np.arange(16))) & 1)
def tune(b, goal):
    t = bits(b); t = t - LIM * (t > 0); need = int((goal - np.add.reduce((2 * np.arange(16) + 1) * t)) % V)
    for p in range(15, -1, -1):
        d = min(LIM, need // (2 * p + 1)); t[p] += d; need -= d * (2 * p + 1)
    return t
def ladder(z):
    t = np.tile(np.where(np.abs(z - 128) > 64, 128, 0), (3, 1)); t[:, 0] = z[0]
    for j in (1, 2, 3): t[j - 1, 4 - j] = z[4 - j] + (LIM + j) * (1 if z[4 - j] < 128 else -1)
    return t
def setup_inputs(rng):
    X, O, v, z = parts(rng)
    few = np.take_along_axis(rng.integers(0, V, (N, 8, 16)), rng.integers(0, 16, (N, 8, M)), 2)
    return pack(X, O, np.where(rng.random((N, 8, M)) < 0.25, few, v), z)
def uneven(rng, n):
    a = np.minimum((np.exp2(8 * rng.random((N, 8, 1, n))) * rng.random((N, 8, 16, n))).astype(np.int64), 255)
    return np.where(rng.random(a.shape) < 0.5, 255 - a, a)
def setup_inputs_spread(rng):
    O = np.minimum((V * rng.random((N, 8, 16, WN)) ** 3).astype(np.int64), V - 1); v = np.minimum((V * rng.random((N, 8, M)) ** 2).astype(np.int64), V - 1)
    return pack(uneven(rng, V), O, v, uneven(rng, M))
def setup_inputs_ends(rng):
    X, O, v, z = parts(rng)
    X = 255 * rng.integers(0, 2, X.shape); z = 255 * rng.integers(0, 2, z.shape)
    e = (V - 1) * rng.integers(0, 2, (N, 8, 16, H)); keep = rng.random((N, 8, 16, H)) < 0.75
    keep[..., 0] = True; keep[..., H - 1] = True; e[:, :, 14, H - 1] = V - 1; e[:, :, 15, H - 1] = 0; e[:, :, 14, 0] = 0; e[:, :, 15, 0] = V - 1
    O = np.concatenate([np.where(keep, e, O[..., :H]), np.where(keep, e, O[..., H:])], axis=3)
    v = np.where(rng.random(v.shape) < 0.75, (V - 1) * rng.integers(0, 2, v.shape), v)
    X[:, 1::2, :, V - 1] = X[:, 1::2, :, 0]
    z[..., M // 2:M // 2 + 8] = 255
    v[:, :, M - 2:] = V - 1; z[..., M - 1] = X[..., V - 1]; z[..., M - 2] = 255 - X[..., V - 1]
    v[:, :, :2] = 0; z[..., 0] = X[..., 0]; z[..., 1] = 255 - X[..., 0]
    return pack(X, O, v, z)
def setup_inputs_ties(rng):
    X, O, v, z = parts(rng)
    B = np.broadcast_to(rng.integers(60, 196, (1, 8, 16, 6)), (N, 8, 16, 6)); jog = np.array([LIM, LIM + 1, LIM + 2, LIM + 3, LIM + 4, -LIM, -LIM - 1, -LIM - 2])
    X = np.take_along_axis(B, np.broadcast_to(rng.integers(0, 6, (N, 8, 1, V)), X.shape), 3)
    X = np.where((rng.random((N, 8, 1, V)) < 0.5) & (rng.random(X.shape) < 0.15), X + rng.choice(jog, X.shape), X)
    z = np.take_along_axis(B, np.broadcast_to(rng.integers(0, 6, (N, 8, 1, M)), z.shape), 3)
    z = np.where(rng.random(z.shape) < 0.3, z + rng.choice(jog, z.shape), z)
    O[:, ::2] = np.tile(O[:, ::2, :4], (1, 1, 4, 1))
    return pack(X, O, v, z)
def calm(rng, X, O, v, z, g, low):
    for r in range(N):
        t = rng.integers(0, 256, 16); B = rng.permutation(V)[:5]; f, n, L = int(B[0]), int(B[1]), B[2:]
        w = rng.permutation(np.setdiff1d(np.arange(WN), np.array([f & (WN - 1)])))[:2]; go, end = int(w[0]), int(w[1])
        X[r, g][:, f] = t; X[r, g][:, n] = np.where(np.abs(t - 128) > 64, 128, 0); X[r, g][:, L] = ladder(t).T
        O[r, g][:, go] = f; O[r, g][:, end] = n; O[r, g][:, f & (WN - 1)] = L[rng.permutation(16) % 3]
        stay = np.ones(M, bool); z[r, g] = t[:, None]
        if r in low: stay = np.isin(np.arange(M), rng.permutation(M)[:low[r]])
        else: z[r, g][1:] = rng.integers(0, 256, (15, M))
        v[r, g] = np.where(stay, end, go) + WN * rng.integers(0, V // WN, M)
def setup_inputs_corners(rng):
    X, O, v, z = parts(rng); C = min(M // 4, WN // (4 * N)); own = 1 + np.arange(3 * N * C).reshape(N, 3, C); top = 3 * N * C + 1
    O[..., 0] = rng.choice(np.array([0, V - 1]), (N, 8, 16)); O[..., WN - 1] = rng.choice(np.array([0, V - 1]), (N, 8, 16))
    for r in range(N):
        for g in range(8):
            o = rng.permutation(M); rest = o[3 * C:]
            v[r, g, rest[::2]] = rng.choice(np.array([0, V - 1]), len(rest[::2]))
            for j in range(3):
                E = own[r, j]; ln = o[j * C:(j + 1) * C]; b = rng.integers(0, 65536, C); d = rng.integers(1, 1000, C)
                v[r, g, ln] = E + WN * rng.integers(0, V // WN, C); z[r, g][:, ln] = bits(b).T
                for s in range((S, 1, 2)[j]):
                    q = (r + s) % N
                    t = 65535 - (S - 1 - s) * d if j == 0 else np.full(C, T0 + j - 1)
                    b = b ^ (65535 - t); X[q, g][:, E] = bits(b).T
                    if j == 0:
                        O[q, g][:, E] = rng.integers(top, V, (16, C)); O[q, g][rng.integers(0, 16, C), E] = E
                    else: O[q, g][:, E] = E
    two = rng.permutation(8)[:2]; few = rng.permutation(4)
    for i in range(2): calm(rng, X, O, v, z, int(two[i]), {(i + 2 * j) % N: int(few[(i * (N // 2) + j) % 4]) for j in range(N // 2)})
    return pack(X, O, v, z)
def apart(rng, X, O, v, z, g, q, b):
    K = (S - 1) * M; E = rng.permutation(WN - 1)[:K]; E[K - 1] = WN - 1
    B = E + WN * rng.integers(0, V // WN, K); B[K - 1] = V - 1; B2 = (B[:M] + WN) % V
    left = int(np.setdiff1d(np.arange(WN), E)[0]); X[:, g, :, left] = 128
    for r in range(N):
        k = rng.integers(0, 16, K); k[K - 1] = 15
        X[r, g][:, B] = bits(int(b[r]))[:, None]; O[r, g][:, E] = left; O[r, g][k, E] = B
        if r == q:
            X[r, g][:, B2] = bits(65535 - int(b[q]))[:, None]; O[r, g][(k[:M] + 1 + rng.integers(0, 15, M)) % 16, E[:M]] = B2
    for s in range(1, S):
        r = (q - s) % N; v[r, g] = B[(s - 1) * M:s * M]
        for i in range(M): z[r, g, :, i] = tune(int(b[r]) ^ (65534 - T0), int(rng.integers(1, V)))
    v[q, g] = B2; z[q, g] = bits(65535 - int(b[q]))[:, None]
def setup_inputs_crowd(rng):
    X, O, v, z = parts(rng)
    v = np.take_along_axis(rng.integers(0, V, (N, 8, 3)), rng.integers(0, 3, (N, 8, M)), 2)
    o = rng.permutation(8)
    for i in range(7):
        g = int(o[i]); q = int(rng.integers(0, N)); a = int((V - 1, 0, WN, rng.integers(1, V - 1), V - 1, rng.integers(1, V - 1), 0)[i]); first = q - S + (2 if i < 2 else 1)
        t = np.sort(T0 + 2 + rng.permutation(65534 - T0)[:S - 1]); b = rng.integers(0, 65536, N)
        if i in (2, 3): t[S - 2] = t[S - 3]
        if i >= 4: t[S - 2] = 65535
        for j in range(1, S): b[(first + j) % N] = b[(first + j - 1) % N] ^ (65535 - int(t[j - 1]))
        b = b ^ (int(b[q]) ^ int(rng.integers(1, 65535)))
        if i == 6:
            apart(rng, X, O, v, z, g, q, b); continue
        for r in range(N): X[r, g, :, a] = bits(int(b[r]))
        O[:, g, :, a & (WN - 1)] = a
        if i == 0: X[:, g, :, 0] = 128; O[:, g, :15, a & (WN - 1)] = 0
        v[:, g] = (a + WN * rng.integers(0, V // WN, (N, M))) % V
        for r in range(N):
            m = T0 + 1
            if i in (2, 3) and r == q: m = T0
            if i in (2, 3) and r == (q - 1) % N: m = int(t[S - 2])
            if i >= 4 and r == q: m = 65535
            z[r, g] = tune(int(b[r]) ^ (65535 - m), V - 1)[:, None]
        if i in (2, 3):
            e = (a + 1 + np.arange(3)) % V
            X[q, g][:, e] = ladder(z[q, g, :, 0]).T; O[q, g, :, (a - 1) & (WN - 1)] = e[rng.permutation(16) % 3]
        if i == 2:
            y = tune(int(b[q]) ^ (65535 - T0), V - 2); z[q, g, :, 1::2] = y[:, None]
            f = (a + 4) % V; nx = (q + 1) % N; x = np.full(16, 128); x[[0, 4, 15]] = y[[0, 4, 15]]
            X[q, g, :, f] = x; O[q, g, :, (a - 2) & (WN - 1)] = f
            X[nx, g][:, e] = ladder(x).T; O[nx, g, :, f & (WN - 1)] = e[rng.permutation(16) % 3]
        if i == 1: z[q, g, :, M - 1] = bits(65535 - int(b[q]))
        if i == 3: z[q, g, :, M - 1] = bits(int(b[q]))
        if i == 5: z[q, g, :, M - max(1, S * M - 1024):] = bits(65535 - int(b[q]))[:, None]
    return pack(X, O, v, z)
def check_inputs(d):
    bad = []
    for k, hi in (("tracks", 255), ("nb", V * V - 1), ("v", V - 1), ("z", 255)):
        a = np.asarray(d[k]).astype(np.float64)
        if not np.all((a >= 0) & (a <= hi) & (a == np.floor(a))): bad.append("range of " + k)
    return bad
def reference(tracks, nb, v, z):
    X = np.ascontiguousarray(tracks.astype(np.float32).astype(np.int16).reshape(N, 8, 16, V).transpose(0, 1, 3, 2))
    a = nb.astype(np.int64).reshape(N, 8, 16, H)
    O = np.ascontiguousarray(np.concatenate([a & (V - 1), a // V], axis=3).transpose(0, 1, 3, 2))
    bo = np.stack([gentries(e) for e in v]).astype(np.int64)
    tr = np.ascontiguousarray(z.astype(np.float32).astype(np.int16).reshape(N, 8, 16, M).transpose(0, 1, 3, 2))
    r = np.arange(N)[:, None, None]; g = np.arange(8)[None, :, None]
    two = (1 << (15 - np.arange(16))).astype(np.int32); odd = 2 * np.arange(16) + 1
    settled = np.zeros((N, 8), np.int64)
    for rnd in range(RO):
        u = np.add.reduce(tr * odd, axis=-1) & (V - 1)
        vs, zs, mark, live, c, trail = bo, tr, np.full((N, 8, M), T0), np.ones((N, 8, M), bool), np.zeros((N, 8, M), np.int64), []
        for s in range(S):
            q = (r + s) % N; w = vs & (WN - 1)
            P = O[q, g, w]
            x = X[q[..., None], g[..., None], P]
            near = np.abs(x - zs[:, :, :, None, :]) <= LIM + (settled[q, g] & 3)[..., None, None]
            T = np.add.reduce(np.where(near, two, 0), axis=-1)
            k = np.argmax(T, axis=-1); best = np.max(T, axis=-1)
            go = live & (best > mark)
            nv = np.take_along_axis(P, k[..., None], 3)[..., 0]; nz = np.take_along_axis(x, k[..., None, None], 3)[:, :, :, 0]
            trail.append((w, k, nv))
            vs = np.where(go, nv, vs); zs = np.where(go[..., None], nz, zs); mark = np.where(go, best, mark); c = c + go; live = go
            if s == 0: z1 = zs
        hit = np.zeros((N, 8, V), bool); more = np.zeros((N, 8, WN, 16), np.int64); settled = np.zeros((N, 8), np.int64)
        G = np.broadcast_to(g, (N, 8, M))
        for s in range(S):
            w, k, nv = trail[s]; Q = np.broadcast_to((r + s) % N, (N, 8, M))
            e = c == s + 1; hit[Q[e], G[e], nv[e]] = True
            e = c > s + 1; np.add.at(more, (Q[e], G[e], w[e], k[e]), u[e])
            e = (c == s) if s < S - 1 else (c >= s)
            settled = settled + np.roll(np.add.reduce(e.astype(np.int64), axis=2), s, axis=0)
        X = np.where(hit[..., None], np.maximum(X - PEN, 0), X).astype(np.int16); O = (O + more) & (V - 1)
        bo = np.where(c > 0, vs, (bo + u) & (V - 1)); tr = np.where((c > 0)[..., None], (tr + z1) >> 1, tr).astype(np.int16)
    o = O.transpose(0, 1, 3, 2)
    return {"yx": np.ascontiguousarray(X.transpose(0, 1, 3, 2)).reshape(N, 128, V).astype(np.float32).astype(BF),
            "yn": np.ascontiguousarray(o[..., :H] + V * o[..., H:]).reshape(N, 128, H).astype(np.float32),
            "yv": np.stack([gtable(e) for e in bo]).astype(np.float32),
            "yz": np.ascontiguousarray(tr.transpose(0, 1, 3, 2)).reshape(N, 128, M).astype(np.float32).astype(BF)}

@@ -1,0 +1,598 @@
+import numpy as np
+from concourse.bass import DstId, RemoteDMATransfer
+from concourse.mybir import AluOpType, AxisListType, ActivationFunctionType
+
+ALU, ACT = AluOpType, ActivationFunctionType
+NR, NS = 2, 4
+BIGN, BIG2, BIG3, BIG4, BIG0 = 1.5 * 2.0 ** 29, 1.5 * 2.0 ** 34, 1.5 * 2.0 ** 30, 1.5 * 2.0 ** 25, 1.5 * 2.0 ** 23
+OFF = 1023.5
+NOH = 16
+F32, BF, F16, I32, U16 = "float32", "bfloat16", "float16", "int32", "uint16"
+
+
+def _sb(shape, dt):
+    return ("sbuf", [128] + list(shape), dt)
+
+
+SCRATCH = {
+    "XZ": _sb([2304], BF), "OW": _sb([2304], F32), "nbi": _sb([512], I32), "vi": _sb([16], I32), "vw": _sb([16], I32),
+    "Xg": _sb([4096], BF), "near": _sb([4096], BF), "Pu": _sb([256], U16), "Pf": _sb([256], F32), "zT": _sb([256], F16),
+    "zin": _sb([12 * 128], BF), "zout": _sb([12 * 128], BF), "lin": _sb([96], U16), "lout": _sb([96], U16), "l0": _sb([32], U16),
+    "MO": _sb([16, 32], F32), "MI": _sb([12, 24], F32), "BI": _sb([12, 16], F32), "BFn": _sb([4, 16], F32),
+    "Mx": _sb([272], F32), "eq": _sb([272], F32), "val": _sb([272], F32), "Qs": _sb([272], F32),
+    "Rs": _sb([16, 8], F32), "Yw": _sb([24 * 8], F32), "tn": _sb([64, 8], F32), "bt": _sb([4 * 64], F16),
+    "U": _sb([4, 8], F32), "V0": _sb([6, 8], F32), "hp": _sb([512, 8], F32),
+    "OA": _sb([NOH * 128], BF), "OB": _sb([NOH * 144], F16),
+    "exs": _sb([1024], F32), "Rm": _sb([1024], F32), "hit": _sb([128], F16), "hitT": _sb([128], BF),
+    "zt": _sb([256], F32), "fl": _sb([96], BF), "cn": _sb([32], F32), "ynb": _sb([512], F32), "yvb": _sb([16], F32),
+    "iJ": _sb([240], F32), "pi": _sb([4], I32), "pf": _sb([16], F32), "it": _sb([352], F32),
+    "Ib": _sb([128], BF), "If": _sb([128], F32), "hI": _sb([128], BF), "sI": _sb([128], BF), "nsI": _sb([128], BF),
+    "BTs": _sb([240], F16), "Perm": _sb([136], F32), "m8": _sb([8], F32), "M16": _sb([16], F32), "seg": _sb([136], F32),
+    "BM": _sb([64], F32), "BL": _sb([4], U16), "BL2": _sb([4], U16), "o17": _sb([136], F32), "age": _sb([272], F32), "blk": _sb([128], BF), "Sel": _sb([2048], BF), "Rr": _sb([2048], BF),
+    "pw": _sb([64], F32), "W": _sb([8], BF), "Wu": _sb([8], BF), "cI0": _sb([16], F32), "cm": _sb([16], BF),
+    "one": _sb([384], BF), "iA": _sb([128], BF), "nA": _sb([128], BF),
+    "Dt": _sb([128], F32), "Dm": _sb([128], F32), "Dh": _sb([128], F16), "iB": _sb([144], BF),
+    "d0": ("psum", [128, 512], F32), "d1": ("psum", [128, 512], F32), "d2": ("psum", [128, 512], F32),
+    "key": ("psum", [128, 512], F32), "msc": ("psum", [128, 512], F32),
+    "ex0": ("psum", [128, 512], F32), "ex1": ("psum", [128, 512], F32), "pen": ("psum", [128, 512], F32),
+}
+NDMA = 20
+SEMAPHORES = (["cV", "cS", "cP", "cG", "sent"] + ["dm%d" % i for i in range(NDMA)]
+              + ["%s%d" % (k, j) for k in "zlmb" for j in range(12)] + ["f%d" % j for j in range(4)] + ["u0", "u1"])
+IO = {"tracks": [128, 2048], "nb": [128, 512], "v": [128, 16], "z": [128, 256],
+      "yx": [128, 2048], "yn": [128, 512], "yv": [128, 16], "yz": [128, 256]}
+
+CY, PCY, GA, SYNC, HOP, ISSUE = 1.0, 0.5, 1.55, 90.0, 3800.0, 500.0
+XUP, XV = [8000, 7000, 6000, 5000], [3]
+NSC = [8, 8, 8, 8, 8, 3, 8, 8]
+FIXV, FIXP = 30.0, 15.0
+OPT = {"vg": 0, "zv": 1, "tv": 0, "lift": 16000, "rs": 12, "pre": 20000, "tup": [12000, 7500]}
+BLK = [512, 512, 512, 384, 128]
+
+
+def A(name, *idx):
+    shape = (SCRATCH[name][1] if name in SCRATCH else IO[name])[1:]
+    cols = np.arange(int(np.prod(shape))).reshape(shape)[idx]
+    psum = name in SCRATCH and SCRATCH[name][0] == "psum"
+    dt = SCRATCH[name][2] if name in SCRATCH else None
+    return {"n": name, "i": idx, "lo": int(np.min(cols)), "hi": int(np.max(cols)) + 1, "k": int(np.size(cols)), "ps": psum, "dt": dt, "ind": None}
+
+
+def S(a, b, c=None):
+    return slice(a, b, c)
+
+
+def C(name, a, n):
+    return A(name, S(a, a + n))
+
+
+def IND(win, off):
+    d = dict(win); d["ind"] = off; d["k"] = off["k"] * 16
+    return d
+
+
+def build_ops():
+    ops = []; seq = [99]
+
+    def add(e, call, args, w, r, busy, lat=0.0, kw=None, **x):
+        rr = []
+        for a in r:
+            if isinstance(a, dict):
+                rr.append(a)
+                if a["ind"] is not None: rr.append(a["ind"])
+        op = {"e": e, "call": call, "args": args, "kw": kw or {}, "w": w, "r": rr, "busy": busy, "lat": lat, "id": len(ops), "seq": seq[0]}
+        op.update(x); ops.append(op)
+        return op
+
+    def two(*a):
+        return all(x["dt"] in (BF, F16, U16) for x in a)
+
+    def vcost(out, in0, per):
+        if in0["ind"] is not None: return 50 + in0["k"] * GA * CY
+        return FIXV + max(64, out["k"] * per) * CY
+
+    def ts(out, in0, s1, op0, s2=None, op1=None):
+        args = [out, in0, s1, s2, op0] + ([op1] if op1 is not None else [])
+        return add("V", "ts", args, [out], [in0, s1, s2], vcost(out, in0, 0.5 if two(out, in0) else 1))
+
+    def tt(out, a, b, op):
+        return add("V", "tt", [out, a, b, op], [out], [a, b], vcost(out, a, 1 if a["ps"] or b["ps"] else 2))
+
+    def cp(out, a):
+        return add("V", "cp", [out, a], [out], [a], vcost(out, a, 0.5 if two(out, a) else 1))
+
+    def scan(out, d0, d1, init, op0, op1):
+        return add("V", "scan", [out, d0, d1, init, op0, op1], [out], [d0, d1], vcost(out, d0, 1))
+
+    def ms(out, val):
+        return add("V", "ms", [out, val], [out], [], 30 + max(64, out["k"] * 0.5) * CY)
+
+    def act(out, a, bias=None, scale=None):
+        kw = {}
+        if bias is not None: kw["bias"] = bias
+        if scale is not None: kw["scale"] = scale
+        c = 65 + a["k"] * GA * CY if a["ind"] is not None else 60 + max(64, a["k"]) * CY
+        return add("S", "act", [out, a, ACT.Identity if kw else ACT.Copy], [out], [a, bias, scale], c, kw=kw)
+
+    def mm(out, l, r, start=True, stop=True):
+        return add("P", "mm", [out, l, r, start, stop], [out], [l, r], FIXP + max(64, r["k"]) * PCY * (4 if l["dt"] == F32 else 1), lat=60)
+
+    def iota(out, pat, base, cm):
+        kw = {} if out["dt"] == I32 else {"allow_small_or_imprecise_dtypes": True}
+        return add("G", "iota", [out, pat, base, cm], [out], [], 130 + 2 * out["k"] * CY, kw=kw)
+
+    nd = [0]; prev = [None]
+
+    def dma(q, out, a, nbytes):
+        nd[0] += 1
+        return add(q, "dma", [out, a], [out], [a], 80, lat=1800 + nbytes / 150.0, sem="dm%d" % (nd[0] - 1), cnt=16)
+
+    def send(stream, src, outs):
+        o = add("G", "send", [src], [], [src], ISSUE, stream=stream, outs=outs, behind=prev[0] if stream != 1 else None)
+        prev[0] = o["id"]
+        for dst, sem, dist in outs:
+            add(None, "arrive", [], [dst], [], 0, lat=HOP + src["k"] * 3, after=o["id"], sem=sem, dist=dist, nout=len(outs))
+
+    E, GE, GT, LT = ALU.is_equal, ALU.is_ge, ALU.is_gt, ALU.is_lt
+    AD, SU, MU, MX, MN = ALU.add, ALU.subtract, ALU.mult, ALU.max, ALU.min
+    W_ = lambda n: A(n, S(None, None))
+
+    dma("Y", C("nbi", 0, 256), C("nb", 0, 256), 131072)
+    dma("S", C("nbi", 256, 256), C("nb", 256, 256), 262144)
+    dma("Y", W_("vi"), W_("v"), 8192)
+    dma("S", C("XZ", 2048, 256), W_("z"), 65536)
+    dma("Y", C("XZ", 0, 1024), C("tracks", 0, 1024), 500000)
+    dma("S", C("XZ", 1024, 1024), C("tracks", 1024, 1024), 600000)
+    iota(C("pi", 0, 1), [[0, 1]], 0, 1)
+    iota(W_("iJ"), [[1, 240]], 0, 0)
+    iota(C("it", 0, 64), [[0, 8], [1, 8]], 0, 0)
+    iota(C("it", 64, 136), [[0, 8], [1, 17]], 0, 0)
+    iota(W_("cI0"), [[128, 2], [0, 8]], 2048, 1)
+    iota(C("iB", 0, 16), [[128, 16]], -1024, 0)
+    iota(C("iB", 16, 128), [[-1024, 16], [128, 8]], 16384, 0)
+    iota(C("it", 224, 128), [[1, 8], [0, 16]], 0, 0)
+    ts(C("pi", 1, 1), C("pi", 0, 1), 15, ALU.bitwise_and)
+    ts(C("pi", 2, 1), C("pi", 0, 1), 4, ALU.logical_shift_right)
+    cp(C("pf", 0, 3), C("pi", 0, 3))
+    pc, pm, pd = C("pf", 0, 1), C("pf", 1, 1), C("pf", 2, 1)
+    ts(C("pf", 3, 1), pd, 17.0, MU, 15.0, AD)
+    tt(C("pf", 4, 1), C("pf", 3, 1), pm, SU)
+    ts(C("pf", 5, 1), pm, 8.0, GE)
+    ts(C("pf", 6, 1), pm, 2.0, MU, 1.0, AD)
+    J = lambda n: C("iJ", 0, n)
+    ts(W_("Ib"), J(128), pc, E); ts(W_("If"), J(128), pc, E)
+    ts(W_("hI"), J(128), pc, E, 0.5, MU)
+    ts(W_("sI"), J(128), pc, E, 32 / 28.5, MU); ts(W_("nsI"), J(128), pc, E, -32 / 28.5, MU)
+    ts(W_("BTs"), J(240), -112.0, AD, pm, E)
+    ts(W_("Perm"), J(136), C("pf", 4, 1), E)
+    ts(W_("m8"), J(8), pd, E); ts(W_("M16"), J(16), pm, E)
+    ts(W_("seg"), C("it", 64, 136), 0.0, GT)
+    ts(W_("BM"), C("it", 0, 64), pd, E)
+    ts(W_("BL"), J(4), 2.0, MU, C("pf", 5, 1), AD)
+    ts(C("pf", 7, 1), C("pf", 5, 1), 17.0, MU, 16.0, AD); ts(W_("BL2"), J(4), 34.0, MU, C("pf", 7, 1), AD)
+    ms(W_("o17"), 1.0)
+    ts(W_("blk"), C("it", 224, 128), pd, E, -33.0, MU)
+    ms(C("pw", 0, 16), 0.5); ms(C("pw", 16, 16), 0.0)
+    scan(C("pw", 32, 16), C("pw", 0, 16), C("pw", 16, 16), 65536.0 * 4096, MU, AD)
+    tt(C("pw", 48, 16), C("pw", 32, 16), W_("M16"), MU)
+    add("V", "red", [C("pf", 8, 1), C("pw", 48, 16), AxisListType.X, AD], [C("pf", 8, 1)], [C("pw", 48, 16)], 100)
+    ts(W_("W"), W_("m8"), C("pf", 8, 1), MU); ts(W_("Wu"), W_("m8"), C("pf", 6, 1), MU)
+    ms(C("cm", 8, 8), 34816.0 * 4096)
+    ms(C("one", 0, 128), 1.0); ms(C("one", 128, 128), -1.0); ms(C("one", 256, 128), 0.0)
+    ts(W_("iA"), J(128), -63.5, AD); ts(W_("nA"), J(128), -1.0, MU, 63.0, AD)
+    ts(W_("Dt"), J(128), -1.0, AD, pc, E); tt(W_("Dm"), W_("Dt"), W_("If"), SU)
+    ts(C("pf", 9, 1), pc, 127.0, E); tt(C("Dm", 0, 1), C("Dm", 0, 1), C("pf", 9, 1), SU); cp(W_("Dh"), W_("Dm"))
+    for k in range(16): (act if k < OPT["rs"] else cp)(A("Rr", S(k, 2048, 16)), W_("Ib"))
+    for b in range(16): act(C("Sel", 128 * b, 128), W_("blk"), scale=C("M16", b, 1))
+    ms(C("OW", 2048, 256), -OFF)
+    for h in range(2):
+        y, R = C("d0", 256 * h, 256), C("Rm", 256 * h, 256)
+        ts(y, C("nbi", 256 * h, 256), -OFF, AD); ts(R, y, BIG2, AD, BIG2, SU)
+        tt(C("OW", 256 * h, 256), y, R, SU)
+        act(C("OW", 512 + 256 * h, 256), R, bias=-OFF, scale=1 / 2048.0)
+    for h in range(2): act(C("OW", 1024 + 512 * h, 512), C("OW", 512 * h, 512))
+
+    cnt = {"d": 0, "tn": 0, "bt": 0, "y": 0, "oh": 0, "hp": 0}
+
+    def nxt(k, m, step=1):
+        v = cnt[k]; cnt[k] = (v + step) % m
+        return v
+
+    def turn(win, lst="BL"):
+        b = nxt("bt", 4)
+        tt(C("bt", 64 * b, 64), IND(win, W_(lst)), W_("BM"), MU)
+        for gi in range(8):
+            mm(C("msc", 0, 8), C("BTs", 112 - 16 * gi, 128), C("bt", 64 * b + 8 * gi, 8), gi == 0, gi == 7)
+        return C("msc", 0, 8)
+
+    ts(W_("vw"), W_("vi"), 1023, ALU.bitwise_and); cp(C("l0", 0, 16), W_("vw"))
+    cp(C("Yw", 0, 16), W_("vi")); cnt["y"] = 2
+    for c in range(2):
+        act(A("V0", c, S(0, 8)), turn(C("Yw", 8 * c, 8)))
+
+    def station(r, s, c):
+        jo, ji = r * 8 + s * 2 + c, r * 6 + (s - 1) * 2 + c
+        j = r * 6 + s * 2 + c; seq[0] = jo
+        L = C("l0", 16 * r + 8 * c, 8) if s == 0 else C("lin", 8 * ji, 8)
+        Z = C("XZ", 2048 + 128 * c, 128) if s == 0 else C("zin", 128 * ji, 128)
+        ow = IND(W_("OW") if s else C("OW", 0, 1024), L)
+        ts(C("Pu", 128 * c, 128), ow, OFF, AD)
+        d = "d%d" % nxt("d", 3)
+        mm(C(d, 0, 128), Z, W_("nsI"))
+        (cp if OPT["tv"] else act)(C("zT", 128 * c, 128), C(d, 0, 128))
+        b = 0
+        for n in BLK:
+            o = 2048 * c + b
+            (cp if b < OPT["vg"] else act)(C("Xg", o, n), IND(C("XZ", 0, 2048), C("Pu", o // 16, n // 16)))
+            if b == 0: act(C("Pf", 128 * c, 128), ow, bias=OFF)
+            d = C("d%d" % nxt("d", 3), 0, n)
+            mm(d, C("zT", 128 * c, 128), C("Rr", b, n), True, False)
+            mm(d, W_("sI"), C("Xg", o, n), False, True)
+            ts(C("near", o, n), d, BIGN, AD, BIGN, E)
+            b += n
+        mk, mq = A("key", S(16, 136, 17)), A("key", S(136 + 16, 272, 17))
+        mm(C("key", 136, 136), C("Pf", 128 * c, 128), W_("Perm"), True, False)
+        if s == 0:
+            mm(mq, W_("If"), C("cI0", 8 * c, 8), False, True)
+            mm(mk, W_("Ib"), C("cm", 8, 8))
+        else:
+            mm(mq, W_("If"), A("MI", ji, S(0, 8)), False, True)
+            mm(mk, W_("If"), A("MI", ji, S(8, 16)))
+        for k in range(16):
+            mm(A("key", S(15 - k, 136, 17)), A("near", S(2048 * c + k, 2048 * c + 2048, 16)), W_("W"))
+        o = 136 * c
+        scan(C("Mx", o, 136), W_("seg"), C("key", 0, 136), 0.0, MU, MX)
+        D = C("eq", o, 136)
+        tt(D, C("Mx", o, 136), C("key", 0, 136), SU)
+        tt(C("val", o, 136), C("key", 136, 136), D, SU)
+        scan(C("Qs", o, 136), D, C("val", o, 136), 0.0, MN, MX)
+        scan(C("age", o, 136), D, W_("o17"), 0.0, MN, AD)
+        Q, G = A("Qs", S(o + 16, o + 136, 17)), A("age", S(o + 16, o + 136, 17))
+        go, vn = A("MO", jo, S(0, 8)), A("MO", jo, S(8, 16))
+        if s == 0: ts(vn, Q, 2047.0, MN)
+        else: (cp if s == 3 else act)(vn, Q)
+        ts(go, G, 1.5, GT)
+        if s < 3: act(A("Rs", jo, S(0, 8)), G, bias=19 * 1024.0, scale=-1024.0)
+        back = [(A("BI", ji, S(0, 16)), "b%d" % ji, -1)] if s else None
+        if s == 3:
+            send(3, A("MO", jo, S(0, 16)), back + [(A("BFn", 2 * r + c, S(0, 16)), "f%d" % (2 * r + c), -3)])
+            seq[0] = 99
+            return
+        lo = C("lout", 8 * j, 8)
+        if s == 0:
+            y = C("Yw", 8 * nxt("y", 24), 8)
+            ts(y, Q, -1152.0, AD); ts(lo, turn(y), 1152.0, AD)
+        else:
+            cp(lo, turn(C("Qs", o, 136), "BL2"))
+        send(1, lo, [(C("lin", 8 * j, 8), "l%d" % j, 1)])
+        (cp if OPT["zv"] else act)(C("zout", 128 * j, 128), IND(W_("XZ"), lo))
+        send(0, C("zout", 128 * j, 128), [(C("zin", 128 * j, 128), "z%d" % j, 1)])
+        t = A("tn", nxt("tn", 64), S(0, 8))
+        act(t, go, bias=2.0 ** 30, scale=-2.0 ** 30)
+        tt(A("MO", jo, S(16, 24)), A("Mx", S(o + 16, o + 136, 17)), t, MX)
+        n = 16
+        if s < 2 and (r or s):
+            act(A("MO", jo, S(24, 32)), A("U", 2 * r + c, S(0, 8)) if s == 0 else A("MI", ji, S(16, 24))); n = 24
+        send(2, A("MO", jo, S(8, 8 + n)), [(A("MI", j, S(0, n)), "m%d" % j, 1)])
+        if s: send(3, A("MO", jo, S(0, 16)), back)
+        seq[0] = 99
+
+    def hp2():
+        h = nxt("hp", 512, 2)
+        return h
+
+    def H(h, cs):
+        return A("hp", S(h + cs[0], h + cs[-1] + 1), S(0, 8))
+
+    def hist_pre(r, s, b=(0, 1)):
+        jo, ji = r * 8 + s * 2, r * 6 + (s - 1) * 2
+        go, vn, R = A("MO", S(jo, jo + 2), S(0, 8)), A("MO", S(jo, jo + 2), S(8, 16)), A("Rs", S(jo, jo + 2), S(0, 8))
+        base = hp2()
+        act(H(base, b), A("MO", S(jo + b[0], jo + b[-1] + 1), S(8, 16)), bias=-1087.5)
+        if s == 3: return (base,)
+        vin = A("V0", S(2 * r, 2 * r + 2), S(0, 8)) if s == 0 else A("MI", S(ji, ji + 2), S(0, 8))
+        u = A("U", S(2 * r, 2 * r + 2), S(0, 8)) if s == 0 else A("MI", S(ji, ji + 2), S(16, 24))
+        h, w, x, d, du = [hp2() for _ in range(5)]
+        ts(H(h, b), vin, 1024.0, GE, -1024.0, MU); tt(H(w, b), vin, H(h, b), AD)
+        tt(H(x, b), H(w, b), R, AD); tt(H(d, b), H(x, b), vn, SU); tt(H(du, b), u, go, SU)
+        return base, d, du
+
+    def hist_post(r, s, pre, cs, last):
+        jo = r * 8 + s * 2; cl = S(cs[0], cs[-1] + 1)
+        go = A("MO", S(jo + cs[0], jo + cs[-1] + 1), S(0, 8))
+        if s == 3:
+            code = pre[0]; wt = None
+        else:
+            base, d, du = pre; jb = r * 6 + s * 2
+            gon = A("BI", S(jb + cs[0], jb + cs[-1] + 1), S(0, 8))
+            t1, code, t2, wt = [hp2() for _ in range(4)]
+            tt(H(t1, cs), gon, H(d, cs), MU); tt(H(code, cs), H(t1, cs), H(base, cs), AD)
+            tt(H(t2, cs), gon, H(du, cs), MU); tt(H(wt, cs), H(t2, cs), go, AD)
+        bR, a = hp2(), hp2()
+        ts(H(bR, cs), H(code, cs), BIG3, AD, BIG3, SU); tt(H(a, cs), H(code, cs), H(bR, cs), SU)
+        ns = NSC[2 * s + cs[0]]
+        if ns:
+            wh = hp2(); act(H(wh, cs), go if s == 3 else H(wt, cs), scale=0.5)
+        for c in cs:
+            for gi in range(8):
+                o = nxt("oh", NOH); col = S(gi, gi + 1); n = 16 if s == 3 else 144
+                oa, ac = C("OA", 128 * o, 128), A("hp", a + c, col)
+                if gi >= 8 - ns:
+                    add("S", "act", [oa, W_("nA"), ACT.Sign], [oa], [W_("nA"), ac], 60 + 128 * CY, kw={"bias": ac})
+                    wc = A("hp", wh + c, col)
+                else:
+                    ts(oa, W_("iA"), ac, LT, 0.5, SU)
+                    wc = A("MO", jo + c, col) if s == 3 else A("hp", wt + c, col)
+                ts(C("OB", 144 * o, n), C("iB", 0, n), A("hp", bR + c, col), E, wc, MU)
+                end = last and c == cs[-1]
+                if s < 3:
+                    mm(C("ex%d" % (gi // 4), 128 * (gi % 4), 128), C("OA", 128 * o, 128), C("OB", 144 * o + 16, 128), False, end and gi % 4 == 3)
+                mm(C("pen", 16 * gi, 16), C("OA", 128 * o, 128), C("OB", 144 * o, 16), False, end and gi == 7)
+
+    b2 = (0, 1)
+    for r in range(NR):
+        last = r == NR - 1
+        for c in range(2): mm(C("msc", 8 * c, 8), C("XZ", 2048 + 128 * c, 128), W_("Wu"))
+        h1, h2 = hp2(), hp2()
+        ts(H(h1, b2), C("msc", 0, 16), -OFF, AD, BIG2, AD); act(H(h2, b2), H(h1, b2), bias=-BIG2)
+        U = A("U", S(2 * r, 2 * r + 2), S(0, 8))
+        tt(U, C("msc", 0, 16), H(h2, b2), SU)
+        if r == 0:
+            seq[0] = 0
+            for c in range(2): send(1 - c, A("U", c, S(0, 8)), [(A("MI", c, S(16, 24)), "u%d" % c, 1)])
+            seq[0] = 99; ops[-1]["lift"] = ops[-3]["lift"] = OPT["lift"]
+        station(r, 0, 0); station(r, 0, 1)
+        for bk, n in (("ex0", 512), ("ex1", 512), ("pen", 128)):
+            mm(C(bk, 0, n), C("one", 256, 128), C("Rr", 0, n), True, False)
+        V0 = A("V0", S(2 * r, 2 * r + 2), S(0, 8)); h1, h2, alt = hp2(), hp2(), hp2()
+        tt(H(h1, b2), V0, U, AD); ts(H(h2, b2), H(h1, b2), 2048.0, GE, -2048.0, MU); tt(H(alt, b2), H(h1, b2), H(h2, b2), AD)
+        pre0 = hist_pre(r, 0)
+        station(r, 1, 0)
+        mm(C("msc", 0, 256), W_("hI"), C("XZ", 2048, 256), True, False)
+        mm(C("msc", 0, 256), W_("hI"), C("zout", 768 * r, 256), False, True)
+        ts(W_("zt"), C("msc", 0, 256), -0.25, AD, BIG0, AD)
+        act(C("XZ", 2048, 256), W_("zt"), bias=-BIG0)
+        if last: dma("Y", W_("yz"), C("XZ", 2048, 256), 65536)
+        station(r, 1, 1)
+        pre1 = hist_pre(r, 1)
+        hist_post(r, 0, pre0, (0,), False)
+        station(r, 2, 0)
+        hist_post(r, 0, pre0, (1,), False)
+        station(r, 2, 1)
+        pre2 = hist_pre(r, 2)
+        hist_post(r, 1, pre1, (0,), False)
+        station(r, 3, 0)
+        hist_post(r, 1, pre1, (1,), False)
+        hist_post(r, 3, hist_pre(r, 3, (0,)), (0,), False)
+        station(r, 3, 1)
+        if not last:
+            for s in range(3):
+                ts(C("fl", 16 * s, 16), A("MI", S(r * 6 + 2 * s, r * 6 + 2 * s + 2), S(8, 16)), 2.0 ** 29, LT)
+                act(C("fl", 48 + 16 * s, 16), A("MO", S(r * 8 + 2 * s, r * 8 + 2 * s + 2), S(0, 8)))
+            for s in range(6): mm(C("msc", 0, 16), C("one", 128 * (s // 3), 128), C("fl", 16 * s, 16), s == 0, s == 5)
+            tt(C("cn", 0, 16), C("msc", 0, 16), C("BM", 0, 16), MU)
+            add("V", "red", [C("cn", 16, 1), C("cn", 0, 16), AxisListType.X, AD], [C("cn", 16, 1)], [C("cn", 0, 16)], 100)
+            ts(C("cn", 17, 1), C("cn", 16, 1), -1.5, AD, BIG4, AD)
+            ts(C("cn", 18, 1), C("cn", 17, 1), BIG4, SU, -28.5, AD)
+            ts(C("cn", 19, 1), C("cn", 16, 1), C("cn", 18, 1), SU, 1 / 32.0, MU)
+            add("V", "rcp", [C("cn", 20, 1), C("cn", 19, 1)], [C("cn", 20, 1)], [C("cn", 19, 1)], 250)
+            ts(W_("sI"), W_("Ib"), C("cn", 20, 1), MU); ts(W_("nsI"), W_("Ib"), C("cn", 20, 1), MU, -1.0, MU)
+        for c in range(2):
+            hist_post(r, 2, pre2, (c,), c == 1)
+            if c == 0: hist_post(r, 3, hist_pre(r, 3, (1,)), (1,), False)
+            h1, h2 = hp2(), hp2(); cs = (c,)
+            vnew = A("V0", 2 * r + 2 + c, S(0, 8)); y = C("Yw", 8 * nxt("y", 24), 8)
+            tt(H(h1, cs), A("BFn", S(2 * r + c, 2 * r + c + 1), S(8, 16)), H(alt, cs), SU)
+            tt(H(h2, cs), H(h1, cs), A("MO", S(r * 8 + c, r * 8 + c + 1), S(0, 8)), MU)
+            tt(y, H(h2, cs), H(alt, cs), AD)
+            if not last:
+                act(vnew, y); h3 = hp2(); y0 = y; y = C("Yw", 8 * nxt("y", 24), 8)
+                ts(H(h3, cs), y0, 1024.0, GE, -1024.0, MU); tt(y, y0, H(h3, cs), AD)
+            cp(C("yvb", 8 * c, 8) if last else C("l0", 16 * (r + 1) + 8 * c, 8), turn(y))
+        if last: dma("Y", W_("yv"), W_("yvb"), 8192)
+        for h in range(2): mm(W_("d%d" % h), W_("If"), C("OW", 512 * h, 512), True, False)["up"] = OPT["pre"]
+        cp(C("exs", 0, 512), W_("ex0")); act(C("exs", 512, 512), W_("ex1"))
+        t0 = len(ops)
+        act(W_("hit"), C("pen", 0, 128))
+        mm(C("pen", 128, 128), W_("hit"), W_("Dh")); ts(W_("hitT"), C("pen", 128, 128), 0.5, GT)
+        for x in ops[t0:]: x["up"] = 9000
+        for x in range(8):
+            o, a = C("d%d" % (x // 4), 128 * (x % 4), 128), A("exs", S(x, 1024, 8))
+            mm(o, a, W_("Dm"), False, x % 4 == 3)["up"] = OPT["tup"][x // 4]
+        for h in range(2):
+            d = W_("d%d" % h); ow = C("OW", 512 * h, 512)
+            ts(C("Rm", 512 * h, 512), d, BIG2, AD, BIG2, SU); tt(ow, d, C("Rm", 512 * h, 512), SU)
+            if not last: act(C("OW", 1024 + 512 * h, 512), ow)
+        if last:
+            act(C("exs", 0, 512), C("OW", 512, 512), bias=OFF * 2049, scale=2048.0)
+            for h in range(2):
+                tt(C("ynb", 256 * h, 256), C("exs", 256 * h, 256), C("OW", 256 * h, 256), AD)
+                dma("Y", C("yn", 256 * h, 256), C("ynb", 256 * h, 256), 131072)
+        for q, bk in enumerate(("key", "d2", "ex0", "ex1")):
+            xb = C("XZ", 512 * q, 512)
+            mm(W_(bk), W_("Ib"), xb, True, False)["up"] = 15000
+            for i in range(4): mm(C(bk, 128 * i, 128), C("Sel", 128 * (4 * q + i), 128), W_("hitT"), False, i == 3)["up"] = XUP[q]
+            if q in XV: ts(xb, W_(bk), 0.0, MX)["up"] = XUP[q]
+            else: add("S", "act", [xb, W_(bk), ACT.Relu], [xb], [W_(bk)], 60 + 512 * CY)
+            if last: dma("Y", C("yx", 512 * q, 512), xb, 131072)
+        cnt["d"] = 0
+    return ops
+
+
+def plan_order(WIN=200, FILL=60, SEED=1, AMP=0.0):
+    ops = build_ops(); acc = {}
+    for op in ops:
+        deps = {}
+        e = op["e"]; eng = e if op["call"] != "dma" else None
+        if "after" in op: deps[op["after"]] = "msg"
+        if op.get("behind") is not None: deps[op["behind"]] = "order"
+        for a, wr in [(a, False) for a in op["r"]] + [(a, True) for a in op["w"]]:
+            lo, hi = (0, 512) if a["ps"] else (a["lo"], a["hi"])
+            for (p, plo, phi, pwr, pe) in acc.get(a["n"], []):
+                if p == op["id"] or phi <= lo or hi <= plo: continue
+                if a["n"] == "Rr" and wr and pwr: continue
+                same = pe is not None and pe == eng
+                if not (wr or pwr or (a["ps"] and not same)): continue
+                if same and eng == "P":
+                    deps.setdefault(p, "order")
+                else:
+                    deps[p] = "sem"
+        for a, wr in [(a, False) for a in op["r"]] + [(a, True) for a in op["w"]]:
+            lo, hi = (0, 512) if a["ps"] else (a["lo"], a["hi"])
+            lst = acc.setdefault(a["n"], [])
+            if wr and not a["ps"] and a["k"] == hi - lo: lst[:] = [x for x in lst if x[0] == op["id"] or not (lo <= x[1] and x[2] <= hi)]
+            if a["ps"]:
+                lst[:] = ([x for x in lst if x[3]][-1:] + [x for x in lst if not x[3]][-1:]) if not wr else []
+            lst.append((op["id"], lo, hi, wr, eng))
+        op["deps"] = deps
+    n = len(ops); succ = [[] for _ in range(n)]
+    for op in ops:
+        for p in op["deps"]: succ[p].append(op["id"])
+    lev = [0.0] * n
+    for op in reversed(ops):
+        i = op["id"]; m = 0.0
+        for s in succ[i]: m = max(m, lev[s] + (0 if ops[s]["deps"][i] == "order" else op["lat"] + SYNC))
+        lev[i] = m + op["busy"] + (op["lat"] if not succ[i] else 0) + op.get("lift", 0)
+    sq = [op["seq"] for op in ops]
+    for op in reversed(ops):
+        for p in op["deps"]: sq[p] = min(sq[p], sq[op["id"]])
+    x = SEED
+    for i in range(n):
+        x = (x * 1103515245 + 12345) % 2147483648
+        lev[i] += ops[i].get("up", 0) - 1e6 * sq[i] + AMP * x / 2147483648.0
+    left = [len(op["deps"]) for op in ops]; ready = {}; rt = [0.0] * n; st = [0.0] * n; fin = [0.0] * n
+    free = {}; order = []
+    pool = [i for i in range(n) if left[i] == 0]
+    while pool:
+        best = None
+        tmin = {}
+        for i in pool:
+            e = ops[i]["e"]; t = max(rt[i], free.get(e, 0.0)) if e else rt[i]
+            tmin[e] = min(tmin.get(e, 1e18), t)
+        e0 = min(tmin, key=lambda k: tmin[k])
+        for i in pool:
+            if ops[i]["e"] != e0: continue
+            t = max(rt[i], free.get(e0, 0.0)) if e0 else rt[i]
+            if t <= tmin[e0] + WIN and (best is None or lev[i] > lev[best]): best = i
+        if e0 and rt[best] > tmin[e0]:
+            fill = [i for i in pool if ops[i]["e"] == e0 and max(rt[i], tmin[e0]) + ops[i]["busy"] <= rt[best] + FILL]
+            if fill: best = max(fill, key=lambda i: lev[i])
+        i = best; pool.remove(i); op = ops[i]
+        st[i] = max(rt[i], free.get(e0, 0.0)) if e0 else rt[i]
+        if e0: free[e0] = st[i] + op["busy"]
+        fin[i] = st[i] + op["busy"] + op["lat"]; order.append(i)
+        for s in succ[i]:
+            k = ops[s]["deps"][i]
+            rt[s] = max(rt[s], st[i] if k == "order" else fin[i] + (SYNC if k == "sem" else 0))
+            left[s] -= 1
+            if left[s] == 0: pool.append(s)
+    pos = {}; cntq = {}
+    for i in order:
+        op = ops[i]
+        if "sem" in op: op["clk"] = (op["sem"], 1)
+        else:
+            cntq[op["e"]] = cntq.get(op["e"], 0) + 1; op["clk"] = (op["e"], cntq[op["e"]])
+    know = {}; need = set()
+    for i in order:
+        op = ops[i]; op["waits"] = []
+        if op["e"] is None:
+            op["know"] = {}; continue
+        kn = know.setdefault(op["e"], {})
+        for p in sorted((p for p, k in op["deps"].items() if k == "sem"), key=lambda p: -fin[p]):
+            key, val = ops[p]["clk"]
+            if kn.get(key, 0) >= val: continue
+            op["waits"].append(p); need.add(p); kn[key] = val
+            for a, b in ops[p]["know"].items():
+                if kn.get(a, 0) < b: kn[a] = b
+        op["know"] = dict(kn)
+    num = {}
+    for i in order:
+        op = ops[i]
+        if "sem" not in op and i in need:
+            num[op["e"]] = num.get(op["e"], 0) + 1; op["sig"] = ("c" + op["e"], num[op["e"]])
+    return {"ops": ops, "order": order, "need": need, "span": max(fin), "st": st, "fin": fin}
+
+
+PLAN = {}
+
+
+def view(T, a):
+    if not isinstance(a, dict): return a
+    v = T[a["n"]][(slice(None),) + tuple(a["i"])]
+    if a["ind"] is not None: v = v.indirect(view(T, a["ind"]))
+    return v
+
+
+def helpers(T, topo, rank):
+    me = T.cores[rank]; n = len(T.cores)
+    far = [T.cores[(rank + k) % n] for k in (1, -1, -3)]
+    ok = [c for c in topo.cores_of(me) if c != me and T.rank_of(c) is None and all(topo.may_write(c, f) for f in far)]
+    ok.sort(key=lambda c: topo.die(c) != topo.die(me))
+    return [ok[k % len(ok)] for k in range(4)]
+
+
+def split_mask(engs, nout, k):
+    m = len(engs) // nout
+    return sum(1 << e for e in engs[k * m:(k + 1) * m]), m
+
+
+def rank_program(g, core, T, topo):
+    if not PLAN: PLAN.update(plan_order())
+    ops, order = PLAN["ops"], PLAN["order"]
+    n = len(T.cores); rank = T.rank_of(core)
+    if rank is None:
+        for rk in range(n):
+            hs = helpers(T, topo, rk)
+            if core not in hs: continue
+            sent = 0
+            for i in order:
+                op = ops[i]
+                if op["call"] != "send" or hs[op["stream"]] != core: continue
+                outs = op["outs"]; src = view(T, outs[0][0])
+                g.wait_ge(T.sem[outs[0][1]], len(topo.engines(T.cores[rk], core)))
+                trs = []
+                for k, (dst, sem, dist) in enumerate(outs):
+                    to = T.cores[(rk + dist) % n]; rid, pid = topo.addr(to, core)
+                    mask, m = split_mask(topo.engines(core, to), len(outs), k); sent += m
+                    if len(outs) == 1: g.remote_dma(view(T, dst), src, T.sem[sem], T.sem.sent, pid, rid, mask)
+                    else: trs.append(RemoteDMATransfer(dst_ids=[DstId(rid=rid, pnc=pid)], dma_engine_mask=mask, remote_sem=T.sem[sem], src=src, dst=view(T, dst)))
+                if trs: g.remote_dma_fused(trs, local_sem=T.sem.sent)
+            g.wait_ge(T.sem.sent, sent)
+        return
+    hs = helpers(T, topo, rank)
+    Q = {"V": g.vector, "S": g.scalar, "P": g.tensor, "G": g, "Y": g.sync}
+    sent = 0
+    for i in order:
+        op = ops[i]
+        if op["e"] is None: continue
+        q = Q[op["e"]]
+        for p in op["waits"]:
+            o = ops[p]
+            if o["call"] == "arrive":
+                frm = (rank - o["dist"]) % n
+                h = helpers(T, topo, frm)[ops[o["after"]]["stream"]]
+                q.wait_ge(T.sem[o["sem"]], len(topo.engines(h, core)) // o["nout"])
+            elif o["call"] == "dma": q.wait_ge(T.sem[o["sem"]], 16)
+            else: q.wait_ge(T.sem[o["sig"][0]], o["sig"][1])
+        a = [view(T, x) for x in op["args"]]; kw = {k: view(T, x) for k, x in op["kw"].items()}; c = op["call"]
+        if c == "send":
+            h = hs[op["stream"]]; rid, pid = topo.addr(h, core); dst, sem, _d = op["outs"][0]
+            g.remote_dma(view(T, dst), a[0], T.sem[sem], T.sem.sent, pid, rid, topo.mask(core, h))
+            sent += len(topo.engines(core, h)); continue
+        if c == "dma":
+            q.dma_start(a[0], a[1]).then_inc(T.sem[op["sem"]], 16); continue
+        if c == "ts": ins = q.tensor_scalar(*a)
+        elif c == "tt": ins = q.tensor_tensor(*a)
+        elif c == "cp": ins = q.tensor_copy(*a)
+        elif c == "scan": ins = q.tensor_tensor_scan(*a)
+        elif c == "ms": ins = q.memset(*a)
+        elif c == "red": ins = q.tensor_reduce(*a)
+        elif c == "rcp": ins = q.reciprocal(*a)
+        elif c == "act": ins = q.activation(*a, **kw)
+        elif c == "mm": ins = q.matmul(*a)
+        elif c == "tr": ins = q.transpose(*a)
+        else: ins = q.iota(*a, **kw)
+        if "sig" in op: ins.then_inc(T.sem[op["sig"][0]], 1)
+    g.wait_ge(T.sem.sent, sent)
+    for i in order:
+        if ops[i]["call"] == "dma" and i not in PLAN["need"]: g.sync.wait_ge(T.sem[ops[i]["sem"]], 16)

@@ -42,12 +42,13 @@ SEMAPHORES = (["cV", "cS", "cP", "cG", "sent"] + ["dm%d" % i for i in range(NDMA
 IO = {"tracks": [128, 2048], "nb": [128, 512], "v": [128, 16], "z": [128, 256],
       "yx": [128, 2048], "yn": [128, 512], "yv": [128, 16], "yz": [128, 256]}
 
-CY, PCY, GA, SYNC, HOP, ISSUE = 1.0, 0.5, 1.55, 90.0, 3800.0, 500.0
+CY, PCY, GA, SYNC, HOP, ISSUE = 0.85, 0.4, 1.4, 90.0, 2800.0, 900.0
 XUP, XV = [8000, 7000, 6000, 5000], [3]
 NSC = [8, 8, 8, 8, 8, 3, 8, 8]
 FIXV, FIXP = 30.0, 15.0
-OPT = {"vg": 0, "zv": 1, "tv": 0, "lift": 16000, "rs": 12, "pre": 20000, "tup": [12000, 7500]}
-BLK = [512, 512, 512, 384, 128]
+OPT = {"vg": 256, "zv": 0, "tv": 0, "lift": 16000, "rs": 12, "pre": 20000, "tup": [12000, 7500],
+       "b0": 1, "b1": 0, "pv": 0, "pup": 0, "tp": [(0, 128)]}
+BLK = [256, 512, 512, 512, 256]
 
 
 def A(name, *idx):
@@ -127,11 +128,12 @@ def build_ops():
         nd[0] += 1
         return add(q, "dma", [out, a], [out], [a], 80, lat=1800 + nbytes / 150.0, sem="dm%d" % (nd[0] - 1), cnt=16)
 
-    def send(stream, src, outs):
-        o = add("G", "send", [src], [], [src], ISSUE, stream=stream, outs=outs, behind=prev[0] if stream != 1 else None)
+    def send(stream, src, outs, parts=None):
+        o = add("G", "send", [src], [], [src], ISSUE, stream=stream, outs=outs, parts=parts, behind=prev[0] if stream != 1 else None)
         prev[0] = o["id"]
-        for dst, sem, dist in outs:
-            add(None, "arrive", [], [dst], [], 0, lat=HOP + src["k"] * 3, after=o["id"], sem=sem, dist=dist, nout=len(outs))
+        for k, (dst, sem, dist) in enumerate(outs):
+            add(None, "arrive", [], [dst], [], 0, lat=HOP + src["k"] * 3 + (k * ISSUE if parts else 0), after=o["id"], sem=sem, dist=dist,
+                nout=1 if parts else len(outs))
 
     E, GE, GT, LT = ALU.is_equal, ALU.is_ge, ALU.is_gt, ALU.is_lt
     AD, SU, MU, MX, MN = ALU.add, ALU.subtract, ALU.mult, ALU.max, ALU.min
@@ -198,17 +200,19 @@ def build_ops():
         v = cnt[k]; cnt[k] = (v + step) % m
         return v
 
-    def turn(win, lst="BL"):
+    KEY = ("key", "msc")
+
+    def turn(win, c, lst="BL"):
         b = nxt("bt", 4)
         tt(C("bt", 64 * b, 64), IND(win, W_(lst)), W_("BM"), MU)
         for gi in range(8):
-            mm(C("msc", 0, 8), C("BTs", 112 - 16 * gi, 128), C("bt", 64 * b + 8 * gi, 8), gi == 0, gi == 7)
-        return C("msc", 0, 8)
+            mm(C(KEY[c], 272, 8), C("BTs", 112 - 16 * gi, 128), C("bt", 64 * b + 8 * gi, 8), gi == 0, gi == 7)
+        return C(KEY[c], 272, 8)
 
     ts(W_("vw"), W_("vi"), 1023, ALU.bitwise_and); cp(C("l0", 0, 16), W_("vw"))
     cp(C("Yw", 0, 16), W_("vi")); cnt["y"] = 2
     for c in range(2):
-        act(A("V0", c, S(0, 8)), turn(C("Yw", 8 * c, 8)))
+        act(A("V0", c, S(0, 8)), turn(C("Yw", 8 * c, 8), c))
 
     def station(r, s, c):
         jo, ji = r * 8 + s * 2 + c, r * 6 + (s - 1) * 2 + c
@@ -224,27 +228,33 @@ def build_ops():
         for n in BLK:
             o = 2048 * c + b
             (cp if b < OPT["vg"] else act)(C("Xg", o, n), IND(C("XZ", 0, 2048), C("Pu", o // 16, n // 16)))
-            if b == 0: act(C("Pf", 128 * c, 128), ow, bias=OFF)
+            if b == 0:
+                if OPT["pv"]: cp(C("Pf", 128 * c, 128), C("Pu", 128 * c, 128))
+                else: act(C("Pf", 128 * c, 128), ow, bias=OFF)["up"] = OPT["pup"]
             d = C("d%d" % nxt("d", 3), 0, n)
             mm(d, C("zT", 128 * c, 128), C("Rr", b, n), True, False)
             mm(d, W_("sI"), C("Xg", o, n), False, True)
             ts(C("near", o, n), d, BIGN, AD, BIGN, E)
             b += n
-        mk, mq = A("key", S(16, 136, 17)), A("key", S(136 + 16, 272, 17))
-        mm(C("key", 136, 136), C("Pf", 128 * c, 128), W_("Perm"), True, False)
+        key = KEY[c]
+        mk, mq = A(key, S(16, 136, 17)), A(key, S(136 + 16, 272, 17))
+        mm(C(key, 136, 136), C("Pf", 128 * c, 128), W_("Perm"), True, False)
         if s == 0:
             mm(mq, W_("If"), C("cI0", 8 * c, 8), False, True)
             mm(mk, W_("Ib"), C("cm", 8, 8))
         else:
             mm(mq, W_("If"), A("MI", ji, S(0, 8)), False, True)
             mm(mk, W_("If"), A("MI", ji, S(8, 16)))
-        for k in range(16):
-            mm(A("key", S(15 - k, 136, 17)), A("near", S(2048 * c + k, 2048 * c + 2048, 16)), W_("W"))
+        for p0, p1 in OPT["tp"]:
+            for k in range(16):
+                out = dict(A(key, S(15 - k, 136, 17))); out["p"] = (p0, p1)
+                x = mm(out, A("near", S(2048 * c + 16 * p0 + k, 2048 * c + 16 * p1, 16)), W_("W"))
+                x["busy"] = FIXP + min(64, p1 - p0) * PCY
         o = 136 * c
-        scan(C("Mx", o, 136), W_("seg"), C("key", 0, 136), 0.0, MU, MX)
+        scan(C("Mx", o, 136), W_("seg"), C(key, 0, 136), 0.0, MU, MX)
         D = C("eq", o, 136)
-        tt(D, C("Mx", o, 136), C("key", 0, 136), SU)
-        tt(C("val", o, 136), C("key", 136, 136), D, SU)
+        tt(D, C("Mx", o, 136), C(key, 0, 136), SU)
+        tt(C("val", o, 136), C(key, 136, 136), D, SU)
         scan(C("Qs", o, 136), D, C("val", o, 136), 0.0, MN, MX)
         scan(C("age", o, 136), D, W_("o17"), 0.0, MN, AD)
         Q, G = A("Qs", S(o + 16, o + 136, 17)), A("age", S(o + 16, o + 136, 17))
@@ -261,9 +271,9 @@ def build_ops():
         lo = C("lout", 8 * j, 8)
         if s == 0:
             y = C("Yw", 8 * nxt("y", 24), 8)
-            ts(y, Q, -1152.0, AD); ts(lo, turn(y), 1152.0, AD)
+            ts(y, Q, -1152.0, AD); ts(lo, turn(y, c), 1152.0, AD)
         else:
-            cp(lo, turn(C("Qs", o, 136), "BL2"))
+            cp(lo, turn(C("Qs", o, 136), c, "BL2"))
         send(1, lo, [(C("lin", 8 * j, 8), "l%d" % j, 1)])
         (cp if OPT["zv"] else act)(C("zout", 128 * j, 128), IND(W_("XZ"), lo))
         send(0, C("zout", 128 * j, 128), [(C("zin", 128 * j, 128), "z%d" % j, 1)])
@@ -273,8 +283,9 @@ def build_ops():
         n = 16
         if s < 2 and (r or s):
             act(A("MO", jo, S(24, 32)), A("U", 2 * r + c, S(0, 8)) if s == 0 else A("MI", ji, S(16, 24))); n = 24
-        send(2, A("MO", jo, S(8, 8 + n)), [(A("MI", j, S(0, n)), "m%d" % j, 1)])
-        if s: send(3, A("MO", jo, S(0, 16)), back)
+        meta, fwd = A("MO", jo, S(8, 8 + n)), [(A("MI", j, S(0, n)), "m%d" % j, 1)]
+        if s: send(2, A("MO", jo, S(0, 8 + n)), fwd + back, [meta, A("MO", jo, S(0, 16))])
+        else: send(2, meta, fwd)
         seq[0] = 99
 
     def hp2():
@@ -355,14 +366,14 @@ def build_ops():
         if last: dma("Y", W_("yz"), C("XZ", 2048, 256), 65536)
         station(r, 1, 1)
         pre1 = hist_pre(r, 1)
-        hist_post(r, 0, pre0, (0,), False)
+        if not OPT["b0"]: hist_post(r, 0, pre0, (0,), False)
         station(r, 2, 0)
-        hist_post(r, 0, pre0, (1,), False)
+        hist_post(r, 0, pre0, b2 if OPT["b0"] else (1,), False)
         station(r, 2, 1)
         pre2 = hist_pre(r, 2)
-        hist_post(r, 1, pre1, (0,), False)
+        if not OPT["b1"]: hist_post(r, 1, pre1, (0,), False)
         station(r, 3, 0)
-        hist_post(r, 1, pre1, (1,), False)
+        hist_post(r, 1, pre1, b2 if OPT["b1"] else (1,), False)
         hist_post(r, 3, hist_pre(r, 3, (0,)), (0,), False)
         station(r, 3, 1)
         if not last:
@@ -388,7 +399,7 @@ def build_ops():
             if not last:
                 act(vnew, y); h3 = hp2(); y0 = y; y = C("Yw", 8 * nxt("y", 24), 8)
                 ts(H(h3, cs), y0, 1024.0, GE, -1024.0, MU); tt(y, y0, H(h3, cs), AD)
-            cp(C("yvb", 8 * c, 8) if last else C("l0", 16 * (r + 1) + 8 * c, 8), turn(y))
+            cp(C("yvb", 8 * c, 8) if last else C("l0", 16 * (r + 1) + 8 * c, 8), turn(y, 1))
         if last: dma("Y", W_("yv"), W_("yvb"), 8192)
         for h in range(2): mm(W_("d%d" % h), W_("If"), C("OW", 512 * h, 512), True, False)["up"] = OPT["pre"]
         cp(C("exs", 0, 512), W_("ex0")); act(C("exs", 512, 512), W_("ex1"))
@@ -419,7 +430,7 @@ def build_ops():
     return ops
 
 
-def plan_order(WIN=200, FILL=60, SEED=1, AMP=0.0):
+def plan_order(WIN=150, FILL=60, SEED=1, AMP=0.0):
     ops = build_ops(); acc = {}
     for op in ops:
         deps = {}
@@ -518,7 +529,7 @@ PLAN = {}
 
 def view(T, a):
     if not isinstance(a, dict): return a
-    v = T[a["n"]][(slice(None),) + tuple(a["i"])]
+    v = T[a["n"]][(slice(*a["p"]) if "p" in a else slice(None),) + tuple(a["i"])]
     if a["ind"] is not None: v = v.indirect(view(T, a["ind"]))
     return v
 
@@ -550,11 +561,12 @@ def rank_program(g, core, T, topo):
                 if op["call"] != "send" or hs[op["stream"]] != core: continue
                 outs = op["outs"]; src = view(T, outs[0][0])
                 g.wait_ge(T.sem[outs[0][1]], len(topo.engines(T.cores[rk], core)))
-                trs = []
+                trs = []; parts = op["parts"]
                 for k, (dst, sem, dist) in enumerate(outs):
                     to = T.cores[(rk + dist) % n]; rid, pid = topo.addr(to, core)
-                    mask, m = split_mask(topo.engines(core, to), len(outs), k); sent += m
-                    if len(outs) == 1: g.remote_dma(view(T, dst), src, T.sem[sem], T.sem.sent, pid, rid, mask)
+                    mask, m = split_mask(topo.engines(core, to), 1 if parts else len(outs), 0 if parts else k); sent += m
+                    if parts: src = view(T, parts[k])
+                    if parts or len(outs) == 1: g.remote_dma(view(T, dst), src, T.sem[sem], T.sem.sent, pid, rid, mask)
                     else: trs.append(RemoteDMATransfer(dst_ids=[DstId(rid=rid, pnc=pid)], dma_engine_mask=mask, remote_sem=T.sem[sem], src=src, dst=view(T, dst)))
                 if trs: g.remote_dma_fused(trs, local_sem=T.sem.sent)
             g.wait_ge(T.sem.sent, sent)
@@ -577,7 +589,7 @@ def rank_program(g, core, T, topo):
         a = [view(T, x) for x in op["args"]]; kw = {k: view(T, x) for k, x in op["kw"].items()}; c = op["call"]
         if c == "send":
             h = hs[op["stream"]]; rid, pid = topo.addr(h, core); dst, sem, _d = op["outs"][0]
-            g.remote_dma(view(T, dst), a[0], T.sem[sem], T.sem.sent, pid, rid, topo.mask(core, h))
+            g.remote_dma(a[0] if op["parts"] else view(T, dst), a[0], T.sem[sem], T.sem.sent, pid, rid, topo.mask(core, h))
             sent += len(topo.engines(core, h)); continue
         if c == "dma":
             q.dma_start(a[0], a[1]).then_inc(T.sem[op["sem"]], 16); continue

@@ -4,9 +4,11 @@ from concourse.mybir import AluOpType, AxisListType, ActivationFunctionType
 
 ALU, ACT = AluOpType, ActivationFunctionType
 NR, NS = 2, 4
-BIGN, BIG2, BIG3, BIG4, BIG0 = 1.5 * 2.0 ** 29, 1.5 * 2.0 ** 34, 1.5 * 2.0 ** 30, 1.5 * 2.0 ** 25, 1.5 * 2.0 ** 23
-OFF = 1023.5
+BIGN, BIG2, BIG3, BIG4, BIG0, BIGP = 1.5 * 2.0 ** 29, 1.5 * 2.0 ** 34, 1.5 * 2.0 ** 30, 1.5 * 2.0 ** 25, 1.5 * 2.0 ** 23, 1.5 * 2.0 ** 35
+OFF, PO = 1023.5, 1087.5
+KS, DEAD = 2.0 ** 17, 2.0 ** 34
 NOH = 16
+OWN = 1032
 F32, BF, F16, I32, U16 = "float32", "bfloat16", "float16", "int32", "uint16"
 
 
@@ -15,22 +17,23 @@ def _sb(shape, dt):
 
 
 SCRATCH = {
-    "XZ": _sb([2304], BF), "OW": _sb([2304], F32), "nbi": _sb([512], I32), "vi": _sb([16], I32), "vw": _sb([16], I32),
-    "Xg": _sb([4096], BF), "near": _sb([4096], BF), "Pu": _sb([256], U16), "Pf": _sb([256], F32), "zT": _sb([256], F16),
-    "zin": _sb([12 * 128], BF), "zout": _sb([12 * 128], BF), "lin": _sb([96], U16), "lout": _sb([96], U16), "l0": _sb([32], U16),
-    "MO": _sb([16, 32], F32), "MI": _sb([12, 24], F32), "BI": _sb([12, 16], F32), "BFn": _sb([4, 16], F32),
-    "Mx": _sb([272], F32), "eq": _sb([272], F32), "val": _sb([272], F32), "Qs": _sb([272], F32),
-    "Rs": _sb([16, 8], F32), "Yw": _sb([24 * 8], F32), "tn": _sb([64, 8], F32), "bt": _sb([4 * 64], F16),
-    "U": _sb([4, 8], F32), "V0": _sb([6, 8], F32), "hp": _sb([512, 8], F32),
+    "XA": _sb([2304], BF), "XB0": _sb([2304], BF), "XB1": _sb([2304], BF),
+    "OWA": _sb([1280], F32), "OWB0": _sb([1280], F32), "OWB1": _sb([1280], F32),
+    "nbi": _sb([512], I32), "vi": _sb([16], I32), "vw": _sb([16], I32),
+    "Xg": _sb([4096], BF), "near": _sb([4096], BF), "Pu": _sb([256], U16), "Pf": _sb([256], F16), "zT": _sb([256], F16),
+    "zl": _sb([12 * 128], BF), "zin": _sb([4 * 128], BF), "LS": _sb([12 * 16], U16), "lin": _sb([32], U16), "l0": _sb([32], U16),
+    "MO": _sb([16, 56], F32), "MI": _sb([4, 48], F32), "EO": _sb([4, 16], F32), "E1": _sb([4, 16], F32), "E3": _sb([4, 32], F32),
+    "FI": _sb([4, 8], F32), "Mx": _sb([272], F32), "Qs": _sb([272], F32), "r2": _sb([16, 8], F32),
+    "VV": _sb([4, 24], F32), "WW": _sb([2, 24], F32), "bt": _sb([4 * 128], F16), "U": _sb([4, 8], F32), "hp": _sb([512, 8], F32),
     "OA": _sb([NOH * 128], BF), "OB": _sb([NOH * 144], F16),
     "exs": _sb([1024], F32), "Rm": _sb([1024], F32), "hit": _sb([128], F16), "hitT": _sb([128], BF),
-    "zt": _sb([256], F32), "fl": _sb([96], BF), "cn": _sb([32], F32), "ynb": _sb([512], F32), "yvb": _sb([16], F32),
-    "iJ": _sb([240], F32), "pi": _sb([4], I32), "pf": _sb([16], F32), "it": _sb([352], F32),
-    "Ib": _sb([128], BF), "If": _sb([128], F32), "hI": _sb([128], BF), "sI": _sb([128], BF), "nsI": _sb([128], BF),
-    "BTs": _sb([240], F16), "Perm": _sb([136], F32), "m8": _sb([8], F32), "M16": _sb([16], F32), "seg": _sb([136], F32),
-    "BM": _sb([64], F32), "BL": _sb([4], U16), "BL2": _sb([4], U16), "o17": _sb([136], F32), "age": _sb([272], F32), "blk": _sb([128], BF), "Sel": _sb([2048], BF), "Rr": _sb([2048], BF),
-    "pw": _sb([64], F32), "W": _sb([8], BF), "Wu": _sb([8], BF), "cI0": _sb([16], F32), "cm": _sb([16], BF),
-    "one": _sb([384], BF), "iA": _sb([128], BF), "nA": _sb([128], BF),
+    "zt": _sb([256], F32), "cn": _sb([32], F32), "ynb": _sb([512], F32), "yvb": _sb([16], F32),
+    "iJ": _sb([240], F32), "pi": _sb([4], I32), "pf": _sb([24], F32), "it": _sb([152], F32), "ct": _sb([272], F32),
+    "Ib": _sb([128], BF), "If": _sb([128], F32), "nBig": _sb([128], F32), "hI": _sb([128], BF),
+    "sI": _sb([6 * 128], BF), "BTs": _sb([240], F16), "Perm": _sb([136], F16), "m8": _sb([8], F32), "M16": _sb([16], F32),
+    "seg": _sb([136], F32), "cm": _sb([408], BF), "Dq": _sb([272], F32), "BM": _sb([16], F32), "BL": _sb([8], U16),
+    "Sel": _sb([2048], BF), "Rr": _sb([2048], BF), "pw": _sb([64], F32), "W": _sb([8], BF), "Wu": _sb([8], BF), "cI0": _sb([16], F32),
+    "one": _sb([256], BF), "oneF": _sb([256], F32), "iA": _sb([128], BF), "nA": _sb([128], BF),
     "Dt": _sb([128], F32), "Dm": _sb([128], F32), "Dh": _sb([128], F16), "iB": _sb([144], BF),
     "d0": ("psum", [128, 512], F32), "d1": ("psum", [128, 512], F32), "d2": ("psum", [128, 512], F32),
     "key": ("psum", [128, 512], F32), "msc": ("psum", [128, 512], F32),
@@ -38,16 +41,16 @@ SCRATCH = {
 }
 NDMA = 20
 SEMAPHORES = (["cV", "cS", "cP", "cG", "sent"] + ["dm%d" % i for i in range(NDMA)]
-              + ["%s%d" % (k, j) for k in "zlmb" for j in range(12)] + ["f%d" % j for j in range(4)] + ["u0", "u1"])
+              + ["%s%d" % (k, j) for k in "zlmabf" for j in range(4)]
+              + ["%s%d" % (k, j) for k in ("bo", "bx", "so", "sx", "sy") for j in range(2)])
 IO = {"tracks": [128, 2048], "nb": [128, 512], "v": [128, 16], "z": [128, 256],
       "yx": [128, 2048], "yn": [128, 512], "yv": [128, 16], "yz": [128, 256]}
 
-CY, PCY, GA, SYNC, HOP, ISSUE = 0.85, 0.4, 1.4, 90.0, 2800.0, 900.0
-XUP, XV = [8000, 7000, 6000, 5000], [3]
-NSC = [8, 8, 8, 8, 8, 3, 8, 8]
-FIXV, FIXP = 30.0, 15.0
-OPT = {"vg": 256, "zv": 0, "tv": 0, "lift": 16000, "rs": 12, "pre": 20000, "tup": [12000, 7500],
-       "b0": 1, "b1": 0, "pv": 0, "pup": 0, "tp": [(0, 128)]}
+COST = {"CY": 0.87, "PCY": 0.42, "GA": 1.56, "SYNC": 90.0, "RELAY": 4200.0, "DIRECT": 2200.0, "ISSUE": 900.0, "FIXV": 30.0, "FIXP": 15.0,
+        "BULK": 6500.0}
+OPT = {"vg": [512, 0, 256, 0, 512, 0, 0, 0],
+       "nsc": [2, 6, 2, 4, 5, 5, 4, 6],
+       "xv": [1, 3], "rs": 14, "e0": 1, "e1": 0, "pre": 0}
 BLK = [256, 512, 512, 512, 256]
 
 
@@ -56,7 +59,8 @@ def A(name, *idx):
     cols = np.arange(int(np.prod(shape))).reshape(shape)[idx]
     psum = name in SCRATCH and SCRATCH[name][0] == "psum"
     dt = SCRATCH[name][2] if name in SCRATCH else None
-    return {"n": name, "i": idx, "lo": int(np.min(cols)), "hi": int(np.max(cols)) + 1, "k": int(np.size(cols)), "ps": psum, "dt": dt, "ind": None}
+    return {"n": name, "i": idx, "lo": int(np.min(cols)), "hi": int(np.max(cols)) + 1, "k": int(np.size(cols)), "ps": psum, "dt": dt,
+            "ind": None, "set": frozenset(np.ravel(cols).tolist()) if len(shape) > 1 else None}
 
 
 def S(a, b, c=None):
@@ -72,8 +76,9 @@ def IND(win, off):
     return d
 
 
-def build_ops():
+def build_ops(K, O):
     ops = []; seq = [99]
+    CY, PCY, GA, FIXV, FIXP = K["CY"], K["PCY"], K["GA"], K["FIXV"], K["FIXP"]
 
     def add(e, call, args, w, r, busy, lat=0.0, kw=None, **x):
         rr = []
@@ -106,14 +111,14 @@ def build_ops():
         return add("V", "scan", [out, d0, d1, init, op0, op1], [out], [d0, d1], vcost(out, d0, 1))
 
     def ms(out, val):
-        return add("V", "ms", [out, val], [out], [], 30 + max(64, out["k"] * 0.5) * CY)
+        return add("V", "ms", [out, val], [out], [], FIXV + max(64, out["k"] * (0.5 if two(out) else 1)) * CY)
 
-    def act(out, a, bias=None, scale=None):
+    def act(out, a, bias=None, scale=None, fn=None):
         kw = {}
         if bias is not None: kw["bias"] = bias
         if scale is not None: kw["scale"] = scale
         c = 65 + a["k"] * GA * CY if a["ind"] is not None else 60 + max(64, a["k"]) * CY
-        return add("S", "act", [out, a, ACT.Identity if kw else ACT.Copy], [out], [a, bias, scale], c, kw=kw)
+        return add("S", "act", [out, a, fn if fn is not None else ACT.Identity if kw else ACT.Copy], [out], [a, bias, scale], c, kw=kw)
 
     def mm(out, l, r, start=True, stop=True):
         return add("P", "mm", [out, l, r, start, stop], [out], [l, r], FIXP + max(64, r["k"]) * PCY * (4 if l["dt"] == F32 else 1), lat=60)
@@ -128,333 +133,336 @@ def build_ops():
         nd[0] += 1
         return add(q, "dma", [out, a], [out], [a], 80, lat=1800 + nbytes / 150.0, sem="dm%d" % (nd[0] - 1), cnt=16)
 
-    def send(stream, src, outs, parts=None):
-        o = add("G", "send", [src], [], [src], ISSUE, stream=stream, outs=outs, parts=parts, behind=prev[0] if stream != 1 else None)
+    def send(src, dst, sem, dist, via=None):
+        o = add("G", "send", [src], [], [src], K["ISSUE"], pieces=[(via, src, dst)], rsem=sem, dist=dist, behind=prev[0])
         prev[0] = o["id"]
-        for k, (dst, sem, dist) in enumerate(outs):
-            add(None, "arrive", [], [dst], [], 0, lat=HOP + src["k"] * 3 + (k * ISSUE if parts else 0), after=o["id"], sem=sem, dist=dist,
-                nout=1 if parts else len(outs))
+        add(None, "arrive", [], [dst], [], 0, lat=K["DIRECT" if via is None else "RELAY"] + src["k"] * 3, after=[o["id"]], sem=sem)
+
+    def bulk(src, dst, a, n, vias, sem, loc):
+        m = n // len(vias)
+        o = add("G", "send", [C(src, a, n)], [], [C(src, a, n)], K["ISSUE"], lat=2500, rsem=sem, dist=-1, sem=loc, behind=prev[0],
+                pieces=[(h, C(src, a + m * k, m), C(dst, a + m * k, m)) for k, h in enumerate(vias)])
+        prev[0] = o["id"]
+        return o["id"]
+
+    def landed(dst, n, sem, after):
+        add(None, "arrive", [], [C(dst, 0, n)], [], 0, lat=K["BULK"] - 2500, after=after, sem=sem)
 
     E, GE, GT, LT = ALU.is_equal, ALU.is_ge, ALU.is_gt, ALU.is_lt
     AD, SU, MU, MX, MN = ALU.add, ALU.subtract, ALU.mult, ALU.max, ALU.min
-    W_ = lambda n: A(n, S(None, None))
+    W_ = lambda n: A(n, *[S(None, None)] * (len((SCRATCH[n][1] if n in SCRATCH else IO[n])) - 1))
 
     dma("Y", C("nbi", 0, 256), C("nb", 0, 256), 131072)
     dma("S", C("nbi", 256, 256), C("nb", 256, 256), 262144)
     dma("Y", W_("vi"), W_("v"), 8192)
-    dma("S", C("XZ", 2048, 256), W_("z"), 65536)
-    dma("Y", C("XZ", 0, 1024), C("tracks", 0, 1024), 500000)
-    dma("S", C("XZ", 1024, 1024), C("tracks", 1024, 1024), 600000)
+    dma("S", C("XA", 2048, 256), W_("z"), 65536)
+    dma("Y", C("XA", 0, 1024), C("tracks", 0, 1024), 500000)
+    dma("S", C("XA", 1024, 1024), C("tracks", 1024, 1024), 600000)
     iota(C("pi", 0, 1), [[0, 1]], 0, 1)
     iota(W_("iJ"), [[1, 240]], 0, 0)
-    iota(C("it", 0, 64), [[0, 8], [1, 8]], 0, 0)
-    iota(C("it", 64, 136), [[0, 8], [1, 17]], 0, 0)
-    iota(W_("cI0"), [[128, 2], [0, 8]], 2048, 1)
+    iota(C("it", 0, 16), [[0, 2], [1, 8]], 0, 0)
+    iota(C("it", 16, 136), [[0, 8], [1, 17]], 1, 0)
+    iota(W_("cI0"), [[128, 2], [0, 8]], 960, 1)
     iota(C("iB", 0, 16), [[128, 16]], -1024, 0)
     iota(C("iB", 16, 128), [[-1024, 16], [128, 8]], 16384, 0)
-    iota(C("it", 224, 128), [[1, 8], [0, 16]], 0, 0)
     ts(C("pi", 1, 1), C("pi", 0, 1), 15, ALU.bitwise_and)
     ts(C("pi", 2, 1), C("pi", 0, 1), 4, ALU.logical_shift_right)
-    cp(C("pf", 0, 3), C("pi", 0, 3))
-    pc, pm, pd = C("pf", 0, 1), C("pf", 1, 1), C("pf", 2, 1)
-    ts(C("pf", 3, 1), pd, 17.0, MU, 15.0, AD)
-    tt(C("pf", 4, 1), C("pf", 3, 1), pm, SU)
-    ts(C("pf", 5, 1), pm, 8.0, GE)
-    ts(C("pf", 6, 1), pm, 2.0, MU, 1.0, AD)
+    ts(C("pi", 3, 1), C("pi", 0, 1), 7, ALU.bitwise_and)
+    cp(C("pf", 0, 4), C("pi", 0, 4))
+    pf = lambda j: C("pf", j, 1)
+    pc, pm, pd, p8 = pf(0), pf(1), pf(2), pf(3)
     J = lambda n: C("iJ", 0, n)
-    ts(W_("Ib"), J(128), pc, E); ts(W_("If"), J(128), pc, E)
-    ts(W_("hI"), J(128), pc, E, 0.5, MU)
-    ts(W_("sI"), J(128), pc, E, 32 / 28.5, MU); ts(W_("nsI"), J(128), pc, E, -32 / 28.5, MU)
+    ts(W_("Ib"), J(128), pc, E)
+    ts(C("sI", 0, 128), W_("Ib"), 32 / 28.5, MU); ts(C("sI", 128, 128), W_("Ib"), -32 / 28.5, MU); ts(W_("hI"), W_("Ib"), 0.5, MU)
+    act(W_("If"), W_("Ib")); act(W_("nBig"), W_("Ib"), scale=-DEAD)
+    ts(pf(4), pd, 17.0, MU, 15.0, AD); tt(pf(5), pf(4), pm, SU); ts(W_("Perm"), J(136), pf(5), E)
     ts(W_("BTs"), J(240), -112.0, AD, pm, E)
-    ts(W_("Perm"), J(136), C("pf", 4, 1), E)
     ts(W_("m8"), J(8), pd, E); ts(W_("M16"), J(16), pm, E)
-    ts(W_("seg"), C("it", 64, 136), 0.0, GT)
-    ts(W_("BM"), C("it", 0, 64), pd, E)
-    ts(W_("BL"), J(4), 2.0, MU, C("pf", 5, 1), AD)
-    ts(C("pf", 7, 1), C("pf", 5, 1), 17.0, MU, 16.0, AD); ts(W_("BL2"), J(4), 34.0, MU, C("pf", 7, 1), AD)
-    ms(W_("o17"), 1.0)
-    ts(W_("blk"), C("it", 224, 128), pd, E, -33.0, MU)
+    pos = C("it", 16, 136)
+    ts(W_("seg"), pos, 1.5, GT)
+    ts(C("cm", 0, 136), pos, 17.0, E, 34816.0 * KS / 128, MU); ts(C("cm", 272, 136), pos, 17.0, E, DEAD / 128, MU)
+    ts(pf(6), pc, 0.0, E, 4096.0, MU); ts(pf(7), pc, 1.0, E, -1088.0, MU); ts(pf(8), pc, 2.0, E, 0.5, MU); tt(pf(9), pf(7), pf(8), AD)
+    ts(C("ct", 0, 136), pos, 16.5, LT, pf(9), MU); ts(C("ct", 136, 136), pos, -18.0, AD, pf(6), MU)
+    tt(C("cm", 136, 136), C("ct", 0, 136), C("ct", 136, 136), AD)
+    ts(W_("cI0"), W_("cI0"), 0.5, AD)
+    ts(W_("BM"), C("it", 0, 16), pd, E)
+    tt(pf(10), p8, pd, E); ts(pf(11), pm, 8.0, GE, 8.0, MU); ts(pf(12), pf(11), 8.0, AD); ts(W_("BL"), J(8), pf(12), AD, pf(10), MU)
     ms(C("pw", 0, 16), 0.5); ms(C("pw", 16, 16), 0.0)
-    scan(C("pw", 32, 16), C("pw", 0, 16), C("pw", 16, 16), 65536.0 * 4096, MU, AD)
+    scan(C("pw", 32, 16), C("pw", 0, 16), C("pw", 16, 16), 65536.0 * KS, MU, AD)
     tt(C("pw", 48, 16), C("pw", 32, 16), W_("M16"), MU)
-    add("V", "red", [C("pf", 8, 1), C("pw", 48, 16), AxisListType.X, AD], [C("pf", 8, 1)], [C("pw", 48, 16)], 100)
-    ts(W_("W"), W_("m8"), C("pf", 8, 1), MU); ts(W_("Wu"), W_("m8"), C("pf", 6, 1), MU)
-    ms(C("cm", 8, 8), 34816.0 * 4096)
-    ms(C("one", 0, 128), 1.0); ms(C("one", 128, 128), -1.0); ms(C("one", 256, 128), 0.0)
+    add("V", "red", [pf(13), C("pw", 48, 16), AxisListType.X, AD], [pf(13)], [C("pw", 48, 16)], 100)
+    ts(pf(14), pm, 2.0, MU, 1.0, AD)
+    ts(W_("W"), W_("m8"), pf(13), MU); ts(W_("Wu"), W_("m8"), pf(14), MU)
+    ms(C("one", 0, 128), 1.0); ms(C("one", 128, 128), 0.0)
+    ms(C("oneF", 0, 128), 1.0); ms(C("oneF", 128, 128), -1.0)
     ts(W_("iA"), J(128), -63.5, AD); ts(W_("nA"), J(128), -1.0, MU, 63.0, AD)
     ts(W_("Dt"), J(128), -1.0, AD, pc, E); tt(W_("Dm"), W_("Dt"), W_("If"), SU)
-    ts(C("pf", 9, 1), pc, 127.0, E); tt(C("Dm", 0, 1), C("Dm", 0, 1), C("pf", 9, 1), SU); cp(W_("Dh"), W_("Dm"))
-    for k in range(16): (act if k < OPT["rs"] else cp)(A("Rr", S(k, 2048, 16)), W_("Ib"))
-    for b in range(16): act(C("Sel", 128 * b, 128), W_("blk"), scale=C("M16", b, 1))
-    ms(C("OW", 2048, 256), -OFF)
+    ts(pf(15), pc, 127.0, E); tt(C("Dm", 0, 1), C("Dm", 0, 1), pf(15), SU); cp(W_("Dh"), W_("Dm"))
+    for k in range(16): (act if k < O["rs"] else cp)(A("Rr", S(k, 2048, 16)), W_("Ib"))
+    ms(A("MO", S(0, 16), S(0, 8)), -63.5); ms(A("VV", S(0, 4), S(0, 8)), -63.5); ms(A("WW", S(0, 2), S(0, 8)), -63.5)
+    ms(C("OWA", 1024, 256), -OFF)
+    for r in range(NR):
+        ms(C("OWB%d" % r, OWN, 1280 - OWN), -OFF); ms(C("XB%d" % r, 2048, 256), 0.0)
     for h in range(2):
         y, R = C("d0", 256 * h, 256), C("Rm", 256 * h, 256)
         ts(y, C("nbi", 256 * h, 256), -OFF, AD); ts(R, y, BIG2, AD, BIG2, SU)
-        tt(C("OW", 256 * h, 256), y, R, SU)
-        act(C("OW", 512 + 256 * h, 256), R, bias=-OFF, scale=1 / 2048.0)
-    for h in range(2): act(C("OW", 1024 + 512 * h, 512), C("OW", 512 * h, 512))
+        tt(C("OWA", 256 * h, 256), y, R, SU)
+        act(C("OWA", 512 + 256 * h, 256), R, bias=-OFF, scale=1 / 2048.0)
 
-    cnt = {"d": 0, "tn": 0, "bt": 0, "y": 0, "oh": 0, "hp": 0}
+    def copies(r, what):
+        seq[0] = 8 * r + 2
+        if what == "o": landed("OWB%d" % r, OWN, "bo%d" % r, [bulk("OWA", "OWB%d" % r, 0, OWN, [0, 2, 1, 3], "bo%d" % r, "so%d" % r)])
+        else: landed("XB%d" % r, 2048, "bx%d" % r, [bulk("XA", "XB%d" % r, 0, 1024, [0, 2], "bx%d" % r, "sx%d" % r),
+                                                      bulk("XA", "XB%d" % r, 1024, 1024, [1, 3], "bx%d" % r, "sy%d" % r)])
+        seq[0] = 99
+
+    copies(0, "o"); copies(0, "x")
+    o = iota(W_("Sel"), [[0, 2048]], -33, 0); o["behind"] = prev[0]
+    add("G", "sel", [W_("Sel"), W_("Sel"), [[-1, 16], [-16, 8], [0, 16]], E, 0.0, 0, 1], [W_("Sel")], [W_("Sel")], 170 + 2 * 2048 * CY)
+
+    cnt = {"d": 0, "bt": 0, "oh": 0, "hp": 0}
 
     def nxt(k, m, step=1):
         v = cnt[k]; cnt[k] = (v + step) % m
         return v
 
-    KEY = ("key", "msc")
-
-    def turn(win, c, lst="BL"):
-        b = nxt("bt", 4)
-        tt(C("bt", 64 * b, 64), IND(win, W_(lst)), W_("BM"), MU)
-        for gi in range(8):
-            mm(C(KEY[c], 272, 8), C("BTs", 112 - 16 * gi, 128), C("bt", 64 * b + 8 * gi, 8), gi == 0, gi == 7)
-        return C(KEY[c], 272, 8)
-
-    ts(W_("vw"), W_("vi"), 1023, ALU.bitwise_and); cp(C("l0", 0, 16), W_("vw"))
-    cp(C("Yw", 0, 16), W_("vi")); cnt["y"] = 2
-    for c in range(2):
-        act(A("V0", c, S(0, 8)), turn(C("Yw", 8 * c, 8), c))
-
-    def station(r, s, c):
-        jo, ji = r * 8 + s * 2 + c, r * 6 + (s - 1) * 2 + c
-        j = r * 6 + s * 2 + c; seq[0] = jo
-        L = C("l0", 16 * r + 8 * c, 8) if s == 0 else C("lin", 8 * ji, 8)
-        Z = C("XZ", 2048 + 128 * c, 128) if s == 0 else C("zin", 128 * ji, 128)
-        ow = IND(W_("OW") if s else C("OW", 0, 1024), L)
-        ts(C("Pu", 128 * c, 128), ow, OFF, AD)
-        d = "d%d" % nxt("d", 3)
-        mm(C(d, 0, 128), Z, W_("nsI"))
-        (cp if OPT["tv"] else act)(C("zT", 128 * c, 128), C(d, 0, 128))
-        b = 0
-        for n in BLK:
-            o = 2048 * c + b
-            (cp if b < OPT["vg"] else act)(C("Xg", o, n), IND(C("XZ", 0, 2048), C("Pu", o // 16, n // 16)))
-            if b == 0:
-                if OPT["pv"]: cp(C("Pf", 128 * c, 128), C("Pu", 128 * c, 128))
-                else: act(C("Pf", 128 * c, 128), ow, bias=OFF)["up"] = OPT["pup"]
-            d = C("d%d" % nxt("d", 3), 0, n)
-            mm(d, C("zT", 128 * c, 128), C("Rr", b, n), True, False)
-            mm(d, W_("sI"), C("Xg", o, n), False, True)
-            ts(C("near", o, n), d, BIGN, AD, BIGN, E)
-            b += n
-        key = KEY[c]
-        mk, mq = A(key, S(16, 136, 17)), A(key, S(136 + 16, 272, 17))
-        mm(C(key, 136, 136), C("Pf", 128 * c, 128), W_("Perm"), True, False)
-        if s == 0:
-            mm(mq, W_("If"), C("cI0", 8 * c, 8), False, True)
-            mm(mk, W_("Ib"), C("cm", 8, 8))
-        else:
-            mm(mq, W_("If"), A("MI", ji, S(0, 8)), False, True)
-            mm(mk, W_("If"), A("MI", ji, S(8, 16)))
-        for p0, p1 in OPT["tp"]:
-            for k in range(16):
-                out = dict(A(key, S(15 - k, 136, 17))); out["p"] = (p0, p1)
-                x = mm(out, A("near", S(2048 * c + 16 * p0 + k, 2048 * c + 16 * p1, 16)), W_("W"))
-                x["busy"] = FIXP + min(64, p1 - p0) * PCY
-        o = 136 * c
-        scan(C("Mx", o, 136), W_("seg"), C(key, 0, 136), 0.0, MU, MX)
-        D = C("eq", o, 136)
-        tt(D, C("Mx", o, 136), C(key, 0, 136), SU)
-        tt(C("val", o, 136), C(key, 136, 136), D, SU)
-        scan(C("Qs", o, 136), D, C("val", o, 136), 0.0, MN, MX)
-        scan(C("age", o, 136), D, W_("o17"), 0.0, MN, AD)
-        Q, G = A("Qs", S(o + 16, o + 136, 17)), A("age", S(o + 16, o + 136, 17))
-        go, vn = A("MO", jo, S(0, 8)), A("MO", jo, S(8, 16))
-        if s == 0: ts(vn, Q, 2047.0, MN)
-        else: (cp if s == 3 else act)(vn, Q)
-        ts(go, G, 1.5, GT)
-        if s < 3: act(A("Rs", jo, S(0, 8)), G, bias=19 * 1024.0, scale=-1024.0)
-        back = [(A("BI", ji, S(0, 16)), "b%d" % ji, -1)] if s else None
-        if s == 3:
-            send(3, A("MO", jo, S(0, 16)), back + [(A("BFn", 2 * r + c, S(0, 16)), "f%d" % (2 * r + c), -3)])
-            seq[0] = 99
-            return
-        lo = C("lout", 8 * j, 8)
-        if s == 0:
-            y = C("Yw", 8 * nxt("y", 24), 8)
-            ts(y, Q, -1152.0, AD); ts(lo, turn(y, c), 1152.0, AD)
-        else:
-            cp(lo, turn(C("Qs", o, 136), c, "BL2"))
-        send(1, lo, [(C("lin", 8 * j, 8), "l%d" % j, 1)])
-        (cp if OPT["zv"] else act)(C("zout", 128 * j, 128), IND(W_("XZ"), lo))
-        send(0, C("zout", 128 * j, 128), [(C("zin", 128 * j, 128), "z%d" % j, 1)])
-        t = A("tn", nxt("tn", 64), S(0, 8))
-        act(t, go, bias=2.0 ** 30, scale=-2.0 ** 30)
-        tt(A("MO", jo, S(16, 24)), A("Mx", S(o + 16, o + 136, 17)), t, MX)
-        n = 16
-        if s < 2 and (r or s):
-            act(A("MO", jo, S(24, 32)), A("U", 2 * r + c, S(0, 8)) if s == 0 else A("MI", ji, S(16, 24))); n = 24
-        meta, fwd = A("MO", jo, S(8, 8 + n)), [(A("MI", j, S(0, n)), "m%d" % j, 1)]
-        if s: send(2, A("MO", jo, S(0, 8 + n)), fwd + back, [meta, A("MO", jo, S(0, 16))])
-        else: send(2, meta, fwd)
-        seq[0] = 99
-
     def hp2():
-        h = nxt("hp", 512, 2)
-        return h
+        return nxt("hp", 512, 2)
 
-    def H(h, cs):
+    def H(h, cs=(0, 1)):
         return A("hp", S(h + cs[0], h + cs[-1] + 1), S(0, 8))
 
-    def hist_pre(r, s, b=(0, 1)):
-        jo, ji = r * 8 + s * 2, r * 6 + (s - 1) * 2
-        go, vn, R = A("MO", S(jo, jo + 2), S(0, 8)), A("MO", S(jo, jo + 2), S(8, 16)), A("Rs", S(jo, jo + 2), S(0, 8))
-        base = hp2()
-        act(H(base, b), A("MO", S(jo + b[0], jo + b[-1] + 1), S(8, 16)), bias=-1087.5)
-        if s == 3: return (base,)
-        vin = A("V0", S(2 * r, 2 * r + 2), S(0, 8)) if s == 0 else A("MI", S(ji, ji + 2), S(0, 8))
-        u = A("U", S(2 * r, 2 * r + 2), S(0, 8)) if s == 0 else A("MI", S(ji, ji + 2), S(16, 24))
-        h, w, x, d, du = [hp2() for _ in range(5)]
-        ts(H(h, b), vin, 1024.0, GE, -1024.0, MU); tt(H(w, b), vin, H(h, b), AD)
-        tt(H(x, b), H(w, b), R, AD); tt(H(d, b), H(x, b), vn, SU); tt(H(du, b), u, go, SU)
-        return base, d, du
+    KEY = ("key", "msc")
 
-    def hist_post(r, s, pre, cs, last):
-        jo = r * 8 + s * 2; cl = S(cs[0], cs[-1] + 1)
-        go = A("MO", S(jo + cs[0], jo + cs[-1] + 1), S(0, 8))
+    def turn(win, c):
+        b = nxt("bt", 4)
+        act(C("bt", 128 * b, 128), IND(win, W_("BL")), bias=63.5)
+        for gi in range(8):
+            mm(C(KEY[c], 272, 16), C("BTs", 112 - 16 * gi, 128), C("bt", 128 * b + 16 * gi, 16), gi == 0, gi == 7)
+        return C(KEY[c], 272, 16)
+
+    def low(out, v, cs):
+        h = hp2(); ts(H(h, cs), v, 1024.0 - PO, GE, -1024.0, MU); tt(out, v, H(h, cs), AD)
+
+    M = lambda r, s, cs, a, n=8: A("MO", S(r * 8 + s * 2 + cs[0], r * 8 + s * 2 + cs[-1] + 1), S(a, a + n))
+    MI = lambda r, cs, a, n=8: A("MI", S(r * 2 + cs[0], r * 2 + cs[-1] + 1), S(a, a + n))
+    R2 = lambda r, s, cs: A("r2", S(r * 8 + s * 2 + cs[0], r * 8 + s * 2 + cs[-1] + 1), S(0, 8))
+    GO = lambda r, s, cs: M(r, s, cs, 16 if s == 3 else 24)
+    b2 = (0, 1)
+
+    def both(n, j, cs=b2):
+        return A(n, j, S(8 + 8 * cs[0], 16 + 8 * cs[-1]))
+
+    def station(r, s, c):
+        jo = r * 8 + s * 2 + c; j = r * 6 + s * 2 + c; seq[0] = jo; cs = (c,)
+        tb = "B%d" % r if s % 2 else "A"; si = 2 * (1 + s % 2) if r else 0
+        L = C("l0", 16 * r + 8 * c, 8) if s == 0 else C("lin", 8 * (2 * r + c), 8) if s == 2 else C("LS", 16 * (j - 2) + 8, 8)
+        Z = C("XA", 2048 + 128 * c, 128) if s == 0 else C("zin", 128 * (2 * r + c), 128) if s == 2 else C("zl", 128 * (j - 2), 128)
+        Pf, Pu = C("Pf", 128 * c, 128), C("Pu", 128 * c, 128)
+        act(Pf, IND(W_("OW" + tb) if s else C("OWA", 0, 1024), L), bias=OFF); cp(Pu, Pf)
+        d = "d%d" % nxt("d", 3)
+        mm(C(d, 0, 128), Z, C("sI", 128 * si + 128, 128)); act(C("zT", 128 * c, 128), C(d, 0, 128))
+        b = 0; vg = O["vg"][2 * s + c]
+        for n in BLK:
+            o = 2048 * c + b
+            (cp if vg >= n else act)(C("Xg", o, n), IND(C("X" + tb, 0, 2048), C("Pu", o // 16, n // 16)))
+            if vg >= n: vg -= n
+            d = C("d%d" % nxt("d", 3), 0, n)
+            mm(d, C("zT", 128 * c, 128), C("Rr", b, n), True, False)
+            mm(d, C("sI", 128 * si, 128), C("Xg", o, n), False, True)
+            ts(C("near", o, n), d, BIGN, AD, BIGN, E)
+            b += n
+        key = KEY[c]; ko = 136 if s else 0; po = 136 - ko; o = 136 * c
+        kk, mk, pay = C(key, ko, 136), A(key, S(ko + 16, ko + 136, 17)), C(key, po, 136)
+        Mx = A("Mx", S(o + 16, o + 136, 17))
+        mm(C(key, 0, 272), C("one", 0, 128), C("cm", ko, 272), True, False)
+        mm(pay, Pf, W_("Perm"), False, False)
+        mm(A(key, S(po + 16, po + 136, 17)), W_("If"), C("cI0", 8 * c, 8) if s == 0 else MI(r, cs, 0) if s == 2 else M(r, s - 1, cs, 8), False, False)
+        if s:
+            mm(mk, W_("If"), MI(r, cs, 24) if s == 2 else Mx, False, False)
+            mm(mk, W_("nBig"), MI(r, cs, 16) if s == 2 else GO(r, s - 1, cs), False, False)
+        for k in range(16):
+            mm(A(key, S(ko + 15 - k, ko + 136, 17)), A("near", S(2048 * c + k, 2048 * c + 2048, 16)), W_("W"), False, k == 15)
+        scan(C("Mx", o, 136), W_("seg"), kk, 0.0, MU, MX)
+        tt(C("Dq", o, 136), kk, C("Mx", o, 136), SU)
+        scan(C("Qs", o, 136), C("Dq", o, 136), pay, 0.0, MX, MN)
+        Q, P = A("Qs", S(o + 16, o + 136, 17)), M(r, s, cs, 8)
+        ts(R2(r, s, cs), Q, BIGP, AD, BIGP, SU); tt(P, Q, R2(r, s, cs), SU)
         if s == 3:
-            code = pre[0]; wt = None
-        else:
-            base, d, du = pre; jb = r * 6 + s * 2
-            gon = A("BI", S(jb + cs[0], jb + cs[-1] + 1), S(0, 8))
-            t1, code, t2, wt = [hp2() for _ in range(4)]
-            tt(H(t1, cs), gon, H(d, cs), MU); tt(H(code, cs), H(t1, cs), H(base, cs), AD)
-            tt(H(t2, cs), gon, H(du, cs), MU); tt(H(wt, cs), H(t2, cs), go, AD)
+            ts(GO(r, s, cs), R2(r, s, cs), -5000.0, LT)
+            n = 32 if c == 0 and r < NR - 1 else 16
+            send(A("MO", jo, S(8, 8 + n)), A("E3", 2 * r + c, S(0, n)), "b%d" % (2 * r + c), 1, 0)
+            send(A("MO", jo, S(8, 16)), A("FI", 2 * r + c, S(0, 8)), "f%d" % (2 * r + c), -2)
+            seq[0] = 99
+            return
+        low(M(r, s, cs, 16), P, cs)
+        ts(C("LS", 16 * j, 16), turn(A("MO", jo, S(0, 24)), c), 1024.0, AD)
+        ts(GO(r, s, cs), R2(r, s, cs), -5000.0, LT)
+        if s == 1: send(C("LS", 16 * j + 8, 8), C("lin", 8 * (2 * r + c), 8), "l%d" % (2 * r + c), 2)
+        act(C("zl", 128 * j, 128), IND(W_("X" + tb), C("LS", 16 * j, 8)))
+        if s == 1:
+            send(C("zl", 128 * j, 128), C("zin", 128 * (2 * r + c), 128), "z%d" % (2 * r + c), 2)
+            act(M(r, s, cs, 32), Mx); diff(r, s, cs)
+            send(A("MO", jo, S(8, 56)), A("MI", 2 * r + c, S(0, 48)), "m%d" % (2 * r + c), 2)
+        seq[0] = 99
+
+    def diff(r, s, cs):
+        w = both("WW", r, cs) if s == 0 else M(r, 0, cs, 16) if s == 1 else MI(r, cs, 8)
+        e1, e2 = hp2(), hp2()
+        act(H(e1, cs), R2(r, s, cs), bias=19456.0, scale=0.25); tt(H(e2, cs), w, M(r, s, cs, 8), SU)
+        tt(M(r, s, cs, 40), H(e1, cs), H(e2, cs), AD)
+
+    def event(code, wt, cs, gon, P, go, d, um1):
+        t1, t2 = hp2(), hp2()
+        tt(H(t1, cs), gon, d, MU); tt(code, H(t1, cs), P, AD); tt(H(t2, cs), gon, um1, MU); tt(wt, H(t2, cs), go, AD)
+
+    def local_event(r, s, cs):
+        code, wt = hp2(), hp2()
+        event(H(code, cs), H(wt, cs), cs, GO(r, s + 1, cs), M(r, s, cs, 8), GO(r, s, cs), M(r, s, cs, 40), M(r, 1, cs, 48) if s == 0 else MI(r, cs, 40))
+        hist(s, cs, H(code, cs), H(wt, cs), lambda c, g: A("hp", wt + c, S(g, g + 1)))
+
+    def hist(s, cs, code, wt, wcol):
         bR, a = hp2(), hp2()
-        ts(H(bR, cs), H(code, cs), BIG3, AD, BIG3, SU); tt(H(a, cs), H(code, cs), H(bR, cs), SU)
-        ns = NSC[2 * s + cs[0]]
-        if ns:
-            wh = hp2(); act(H(wh, cs), go if s == 3 else H(wt, cs), scale=0.5)
+        ts(H(bR, cs), code, BIG3, AD, BIG3, SU); tt(H(a, cs), code, H(bR, cs), SU)
+        wh = hp2()
+        if any(O["nsc"][2 * s + c] for c in cs): act(H(wh, cs), wt, scale=0.5)
         for c in cs:
             for gi in range(8):
                 o = nxt("oh", NOH); col = S(gi, gi + 1); n = 16 if s == 3 else 144
                 oa, ac = C("OA", 128 * o, 128), A("hp", a + c, col)
-                if gi >= 8 - ns:
-                    add("S", "act", [oa, W_("nA"), ACT.Sign], [oa], [W_("nA"), ac], 60 + 128 * CY, kw={"bias": ac})
-                    wc = A("hp", wh + c, col)
+                if gi >= 8 - O["nsc"][2 * s + c]:
+                    act(oa, W_("nA"), bias=ac, fn=ACT.Sign); wc = A("hp", wh + c, col)
                 else:
-                    ts(oa, W_("iA"), ac, LT, 0.5, SU)
-                    wc = A("MO", jo + c, col) if s == 3 else A("hp", wt + c, col)
+                    ts(oa, W_("iA"), ac, LT, 0.5, SU); wc = wcol(c, gi)
                 ts(C("OB", 144 * o, n), C("iB", 0, n), A("hp", bR + c, col), E, wc, MU)
-                end = last and c == cs[-1]
-                if s < 3:
-                    mm(C("ex%d" % (gi // 4), 128 * (gi % 4), 128), C("OA", 128 * o, 128), C("OB", 144 * o + 16, 128), False, end and gi % 4 == 3)
-                mm(C("pen", 16 * gi, 16), C("OA", 128 * o, 128), C("OB", 144 * o, 16), False, end and gi == 7)
+                if s < 3: mm(C("ex%d" % (gi // 4), 128 * (gi % 4), 128), oa, C("OB", 144 * o + 16, 128), False, (s, c, gi % 4) == (2, 1, 3))
+                mm(C("pen", 16 * gi, 16), oa, C("OB", 144 * o, 16), False, (s, c, gi) == (3, 1, 7))
 
-    b2 = (0, 1)
+    def far_hist(r, s, cs):
+        n = "E1" if s == 1 else "E3"; sl = S(2 * r + cs[0], 2 * r + cs[-1] + 1)
+        hist(s, cs, A(n, sl, S(0, 8)), A(n, sl, S(8, 16)), lambda c, g: A(n, 2 * r + c, S(8 + g, 9 + g)))
+
+    def back_event(r, cs):
+        sl = S(2 * r + cs[0], 2 * r + cs[-1] + 1)
+        event(A("EO", sl, S(0, 8)), A("EO", sl, S(8, 16)), cs, GO(r, 2, cs), MI(r, cs, 0), MI(r, cs, 16), MI(r, cs, 32), MI(r, cs, 40))
+        send(A("EO", sl, S(0, 16)), A("E1", sl, S(0, 16)), "a%d" % (2 * r + cs[-1]), -1, 1)
+
+    ts(W_("vw"), W_("vi"), 1023, ALU.bitwise_and); cp(C("l0", 0, 16), W_("vw"))
+    ts(both("VV", 3), W_("vi"), -PO, AD)
+    act(both("VV", 0), turn(A("VV", 3, S(0, 24)), 1), bias=-63.5); low(both("WW", 0), both("VV", 0), b2)
+
     for r in range(NR):
         last = r == NR - 1
-        for c in range(2): mm(C("msc", 8 * c, 8), C("XZ", 2048 + 128 * c, 128), W_("Wu"))
+        for c in range(2): mm(C("msc", 8 * c, 8), C("XA", 2048 + 128 * c, 128), W_("Wu"))
         h1, h2 = hp2(), hp2()
-        ts(H(h1, b2), C("msc", 0, 16), -OFF, AD, BIG2, AD); act(H(h2, b2), H(h1, b2), bias=-BIG2)
+        ts(H(h1), C("msc", 0, 16), -OFF, AD, BIG2, AD); act(H(h2), H(h1), bias=-BIG2)
         U = A("U", S(2 * r, 2 * r + 2), S(0, 8))
-        tt(U, C("msc", 0, 16), H(h2, b2), SU)
-        if r == 0:
-            seq[0] = 0
-            for c in range(2): send(1 - c, A("U", c, S(0, 8)), [(A("MI", c, S(16, 24)), "u%d" % c, 1)])
-            seq[0] = 99; ops[-1]["lift"] = ops[-3]["lift"] = OPT["lift"]
+        tt(U, C("msc", 0, 16), H(h2), SU); act(M(r, 1, b2, 48), U, bias=-1.0)
         station(r, 0, 0); station(r, 0, 1)
         for bk, n in (("ex0", 512), ("ex1", 512), ("pen", 128)):
-            mm(C(bk, 0, n), C("one", 256, 128), C("Rr", 0, n), True, False)
-        V0 = A("V0", S(2 * r, 2 * r + 2), S(0, 8)); h1, h2, alt = hp2(), hp2(), hp2()
-        tt(H(h1, b2), V0, U, AD); ts(H(h2, b2), H(h1, b2), 2048.0, GE, -2048.0, MU); tt(H(alt, b2), H(h1, b2), H(h2, b2), AD)
-        pre0 = hist_pre(r, 0)
+            mm(C(bk, 0, n), C("one", 128, 128), C("Rr", 0, n), True, False)
+        h1, h2, alt = hp2(), hp2(), hp2()
+        tt(H(h1), both("VV", r), U, AD); ts(H(h2), H(h1), 2048.0 - PO, GE, -2048.0, MU); tt(H(alt), H(h1), H(h2), AD)
+        diff(r, 0, b2)
         station(r, 1, 0)
-        mm(C("msc", 0, 256), W_("hI"), C("XZ", 2048, 256), True, False)
-        mm(C("msc", 0, 256), W_("hI"), C("zout", 768 * r, 256), False, True)
+        mm(C("msc", 0, 256), W_("hI"), C("XA", 2048, 256), True, False)
+        mm(C("msc", 0, 256), W_("hI"), C("zl", 768 * r, 256), False, True)
         ts(W_("zt"), C("msc", 0, 256), -0.25, AD, BIG0, AD)
-        act(C("XZ", 2048, 256), W_("zt"), bias=-BIG0)
-        if last: dma("Y", W_("yz"), C("XZ", 2048, 256), 65536)
+        act(C("XA", 2048, 256), W_("zt"), bias=-BIG0)
+        if last: dma("Y", W_("yz"), C("XA", 2048, 256), 65536)
+        if not O["e0"]: local_event(r, 0, (0,))
         station(r, 1, 1)
-        pre1 = hist_pre(r, 1)
-        if not OPT["b0"]: hist_post(r, 0, pre0, (0,), False)
+        local_event(r, 0, b2 if O["e0"] else (1,))
         station(r, 2, 0)
-        hist_post(r, 0, pre0, b2 if OPT["b0"] else (1,), False)
+        if not O["e1"]: back_event(r, (0,))
         station(r, 2, 1)
-        pre2 = hist_pre(r, 2)
-        if not OPT["b1"]: hist_post(r, 1, pre1, (0,), False)
-        station(r, 3, 0)
-        hist_post(r, 1, pre1, b2 if OPT["b1"] else (1,), False)
-        hist_post(r, 3, hist_pre(r, 3, (0,)), (0,), False)
-        station(r, 3, 1)
+        back_event(r, b2 if O["e1"] else (1,))
+        diff(r, 2, b2)
         if not last:
-            for s in range(3):
-                ts(C("fl", 16 * s, 16), A("MI", S(r * 6 + 2 * s, r * 6 + 2 * s + 2), S(8, 16)), 2.0 ** 29, LT)
-                act(C("fl", 48 + 16 * s, 16), A("MO", S(r * 8 + 2 * s, r * 8 + 2 * s + 2), S(0, 8)))
-            for s in range(6): mm(C("msc", 0, 16), C("one", 128 * (s // 3), 128), C("fl", 16 * s, 16), s == 0, s == 5)
-            tt(C("cn", 0, 16), C("msc", 0, 16), C("BM", 0, 16), MU)
+            h1 = hp2(); tt(H(h1), GO(r, 0, b2), GO(r, 1, b2), SU); tt(A("MO", r * 8 + 6, S(24, 40)), H(h1), GO(r, 2, b2), AD)
+        station(r, 3, 0)
+        if not O["e1"]: far_hist(r, 1, (0,))
+        local_event(r, 2, (0,))
+        station(r, 3, 1)
+        far_hist(r, 1, b2 if O["e1"] else (1,))
+        local_event(r, 2, (1,))
+        far_hist(r, 3, (0,))
+        if not last:
+            for k, (sg, x) in enumerate(((1, GO(r, 0, b2)), (0, MI(r, b2, 16)), (1, GO(r, 2, b2)), (0, A("E3", 2 * r, S(16, 32))))):
+                mm(C("msc", 0, 16), C("oneF", 128 * sg, 128), x, k == 0, k == 3)
+            tt(C("cn", 0, 16), C("msc", 0, 16), W_("BM"), MU)
             add("V", "red", [C("cn", 16, 1), C("cn", 0, 16), AxisListType.X, AD], [C("cn", 16, 1)], [C("cn", 0, 16)], 100)
             ts(C("cn", 17, 1), C("cn", 16, 1), -1.5, AD, BIG4, AD)
             ts(C("cn", 18, 1), C("cn", 17, 1), BIG4, SU, -28.5, AD)
             ts(C("cn", 19, 1), C("cn", 16, 1), C("cn", 18, 1), SU, 1 / 32.0, MU)
-            add("V", "rcp", [C("cn", 20, 1), C("cn", 19, 1)], [C("cn", 20, 1)], [C("cn", 19, 1)], 250)
-            ts(W_("sI"), W_("Ib"), C("cn", 20, 1), MU); ts(W_("nsI"), W_("Ib"), C("cn", 20, 1), MU, -1.0, MU)
-        for c in range(2):
-            hist_post(r, 2, pre2, (c,), c == 1)
-            if c == 0: hist_post(r, 3, hist_pre(r, 3, (1,)), (1,), False)
-            h1, h2 = hp2(), hp2(); cs = (c,)
-            vnew = A("V0", 2 * r + 2 + c, S(0, 8)); y = C("Yw", 8 * nxt("y", 24), 8)
-            tt(H(h1, cs), A("BFn", S(2 * r + c, 2 * r + c + 1), S(8, 16)), H(alt, cs), SU)
-            tt(H(h2, cs), H(h1, cs), A("MO", S(r * 8 + c, r * 8 + c + 1), S(0, 8)), MU)
-            tt(y, H(h2, cs), H(alt, cs), AD)
-            if not last:
-                act(vnew, y); h3 = hp2(); y0 = y; y = C("Yw", 8 * nxt("y", 24), 8)
-                ts(H(h3, cs), y0, 1024.0, GE, -1024.0, MU); tt(y, y0, H(h3, cs), AD)
-            cp(C("yvb", 8 * c, 8) if last else C("l0", 16 * (r + 1) + 8 * c, 8), turn(y, 1))
-        if last: dma("Y", W_("yv"), W_("yvb"), 8192)
-        for h in range(2): mm(W_("d%d" % h), W_("If"), C("OW", 512 * h, 512), True, False)["up"] = OPT["pre"]
+            sc = C("OWA", 1024, 1)
+            add("V", "rcp", [sc, C("cn", 19, 1)], [sc], [C("cn", 19, 1)], 250)
+            ts(C("sI", 256, 128), W_("Ib"), sc, MU); ts(C("sI", 384, 128), W_("Ib"), sc, MU, -1.0, MU)
+        for h in range(2): mm(W_("d%d" % h), W_("If"), C("OWA", 512 * h, 512), True, False)["up"] = O["pre"]
         cp(C("exs", 0, 512), W_("ex0")); act(C("exs", 512, 512), W_("ex1"))
-        t0 = len(ops)
+        for x in range(8): mm(C("d%d" % (x // 4), 128 * (x % 4), 128), A("exs", S(x, 1024, 8)), W_("Dm"), False, x % 4 == 3)
+        for h in range(2):
+            d = W_("d%d" % h); ow = C("OWA", 512 * h, 512)
+            ts(C("Rm", 512 * h, 512), d, BIG2, AD, BIG2, SU); tt(ow, d, C("Rm", 512 * h, 512), SU)
+        if last:
+            act(C("exs", 0, 512), C("OWA", 512, 512), bias=OFF * 2049, scale=2048.0)
+            for h in range(2):
+                tt(C("ynb", 256 * h, 256), C("exs", 256 * h, 256), C("OWA", 256 * h, 256), AD)
+                dma("Y", C("yn", 256 * h, 256), C("ynb", 256 * h, 256), 131072)
+        else:
+            copies(r + 1, "o")
+            sc = C("OWB%d" % (r + 1), 1024, 1)
+            ts(C("sI", 512, 128), W_("Ib"), sc, MU); ts(C("sI", 640, 128), W_("Ib"), sc, MU, -1.0, MU)
+        h1, h2 = hp2(), hp2()
+        tt(H(h1), A("FI", S(2 * r, 2 * r + 2), S(0, 8)), H(alt), SU); tt(H(h2), H(h1), GO(r, 0, b2), MU); tt(both("VV", r + 1), H(h2), H(alt), AD)
+        if last:
+            ts(W_("yvb"), turn(A("VV", r + 1, S(0, 24)), 1), 1024.0, AD); dma("Y", W_("yv"), W_("yvb"), 8192)
+        else:
+            low(both("WW", r + 1), both("VV", r + 1), b2)
+            ts(C("l0", 16 * (r + 1), 16), turn(A("WW", r + 1, S(0, 24)), 1), 1024.0, AD)
+        far_hist(r, 3, (1,))
         act(W_("hit"), C("pen", 0, 128))
         mm(C("pen", 128, 128), W_("hit"), W_("Dh")); ts(W_("hitT"), C("pen", 128, 128), 0.5, GT)
-        for x in ops[t0:]: x["up"] = 9000
-        for x in range(8):
-            o, a = C("d%d" % (x // 4), 128 * (x % 4), 128), A("exs", S(x, 1024, 8))
-            mm(o, a, W_("Dm"), False, x % 4 == 3)["up"] = OPT["tup"][x // 4]
-        for h in range(2):
-            d = W_("d%d" % h); ow = C("OW", 512 * h, 512)
-            ts(C("Rm", 512 * h, 512), d, BIG2, AD, BIG2, SU); tt(ow, d, C("Rm", 512 * h, 512), SU)
-            if not last: act(C("OW", 1024 + 512 * h, 512), ow)
-        if last:
-            act(C("exs", 0, 512), C("OW", 512, 512), bias=OFF * 2049, scale=2048.0)
-            for h in range(2):
-                tt(C("ynb", 256 * h, 256), C("exs", 256 * h, 256), C("OW", 256 * h, 256), AD)
-                dma("Y", C("yn", 256 * h, 256), C("ynb", 256 * h, 256), 131072)
-        for q, bk in enumerate(("key", "d2", "ex0", "ex1")):
-            xb = C("XZ", 512 * q, 512)
-            mm(W_(bk), W_("Ib"), xb, True, False)["up"] = 15000
-            for i in range(4): mm(C(bk, 128 * i, 128), C("Sel", 128 * (4 * q + i), 128), W_("hitT"), False, i == 3)["up"] = XUP[q]
-            if q in XV: ts(xb, W_(bk), 0.0, MX)["up"] = XUP[q]
-            else: add("S", "act", [xb, W_(bk), ACT.Relu], [xb], [W_(bk)], 60 + 512 * CY)
+        banks = ("key", "d2", "ex0", "ex1")
+        for q, bk in enumerate(banks): mm(W_(bk), W_("Ib"), C("XA", 512 * q, 512), True, False)
+        for q, bk in enumerate(banks):
+            xb = C("XA", 512 * q, 512)
+            for i in range(4): mm(C(bk, 128 * i, 128), C("Sel", 128 * (4 * q + i), 128), W_("hitT"), False, i == 3)
+            if q in O["xv"]: ts(xb, W_(bk), 0.0, MX)
+            else: act(xb, W_(bk), fn=ACT.Relu)
             if last: dma("Y", C("yx", 512 * q, 512), xb, 131072)
+        if not last: copies(r + 1, "x")
         cnt["d"] = 0
     return ops
 
 
-def plan_order(WIN=150, FILL=60, SEED=1, AMP=0.0):
-    ops = build_ops(); acc = {}
+def meet(a, b):
+    if a["hi"] <= b["lo"] or b["hi"] <= a["lo"]: return False
+    return a["set"] is None or not a["set"].isdisjoint(b["set"])
+
+
+def plan_order(K=COST, O=OPT, WIN=150, FILL=60):
+    ops = build_ops(K, O); acc = {}; SYNC = K["SYNC"]
     for op in ops:
         deps = {}
-        e = op["e"]; eng = e if op["call"] != "dma" else None
-        if "after" in op: deps[op["after"]] = "msg"
+        e = op["e"]; eng = e if "sem" not in op else None
+        for p in op.get("after", []): deps[p] = "msg"
         if op.get("behind") is not None: deps[op["behind"]] = "order"
-        for a, wr in [(a, False) for a in op["r"]] + [(a, True) for a in op["w"]]:
-            lo, hi = (0, 512) if a["ps"] else (a["lo"], a["hi"])
-            for (p, plo, phi, pwr, pe) in acc.get(a["n"], []):
-                if p == op["id"] or phi <= lo or hi <= plo: continue
+        uses = [(a, False) for a in op["r"]] + [(a, True) for a in op["w"]]
+        for a, wr in uses:
+            for (p, pa, pwr, pe) in acc.get(a["n"], []):
+                if p == op["id"] or not (a["ps"] or meet(a, pa)): continue
                 if a["n"] == "Rr" and wr and pwr: continue
                 same = pe is not None and pe == eng
                 if not (wr or pwr or (a["ps"] and not same)): continue
-                if same and eng == "P":
-                    deps.setdefault(p, "order")
-                else:
-                    deps[p] = "sem"
-        for a, wr in [(a, False) for a in op["r"]] + [(a, True) for a in op["w"]]:
-            lo, hi = (0, 512) if a["ps"] else (a["lo"], a["hi"])
+                if same and eng == "P": deps.setdefault(p, "order")
+                else: deps[p] = "sem"
+        for a, wr in uses:
             lst = acc.setdefault(a["n"], [])
-            if wr and not a["ps"] and a["k"] == hi - lo: lst[:] = [x for x in lst if x[0] == op["id"] or not (lo <= x[1] and x[2] <= hi)]
-            if a["ps"]:
-                lst[:] = ([x for x in lst if x[3]][-1:] + [x for x in lst if not x[3]][-1:]) if not wr else []
-            lst.append((op["id"], lo, hi, wr, eng))
+            if wr and a["ps"]: lst[:] = []
+            elif wr and a["set"] is not None: lst[:] = [x for x in lst if x[0] == op["id"] or not x[1]["set"] <= a["set"]]
+            elif wr and a["k"] == a["hi"] - a["lo"]: lst[:] = [x for x in lst if x[0] == op["id"] or not (a["lo"] <= x[1]["lo"] and x[1]["hi"] <= a["hi"])]
+            lst.append((op["id"], a, wr, eng))
         op["deps"] = deps
     n = len(ops); succ = [[] for _ in range(n)]
     for op in ops:
@@ -463,32 +471,24 @@ def plan_order(WIN=150, FILL=60, SEED=1, AMP=0.0):
     for op in reversed(ops):
         i = op["id"]; m = 0.0
         for s in succ[i]: m = max(m, lev[s] + (0 if ops[s]["deps"][i] == "order" else op["lat"] + SYNC))
-        lev[i] = m + op["busy"] + (op["lat"] if not succ[i] else 0) + op.get("lift", 0)
+        lev[i] = m + op["busy"] + (op["lat"] if not succ[i] else 0)
     sq = [op["seq"] for op in ops]
     for op in reversed(ops):
         for p in op["deps"]: sq[p] = min(sq[p], sq[op["id"]])
-    x = SEED
-    for i in range(n):
-        x = (x * 1103515245 + 12345) % 2147483648
-        lev[i] += ops[i].get("up", 0) - 1e6 * sq[i] + AMP * x / 2147483648.0
-    left = [len(op["deps"]) for op in ops]; ready = {}; rt = [0.0] * n; st = [0.0] * n; fin = [0.0] * n
+    for i in range(n): lev[i] += ops[i].get("up", 0) - 1e6 * sq[i]
+    left = [len(op["deps"]) for op in ops]; rt = [0.0] * n; st = [0.0] * n; fin = [0.0] * n
     free = {}; order = []
-    pool = [i for i in range(n) if left[i] == 0]
-    while pool:
-        best = None
-        tmin = {}
-        for i in pool:
-            e = ops[i]["e"]; t = max(rt[i], free.get(e, 0.0)) if e else rt[i]
-            tmin[e] = min(tmin.get(e, 1e18), t)
-        e0 = min(tmin, key=lambda k: tmin[k])
-        for i in pool:
-            if ops[i]["e"] != e0: continue
-            t = max(rt[i], free.get(e0, 0.0)) if e0 else rt[i]
-            if t <= tmin[e0] + WIN and (best is None or lev[i] > lev[best]): best = i
-        if e0 and rt[best] > tmin[e0]:
-            fill = [i for i in pool if ops[i]["e"] == e0 and max(rt[i], tmin[e0]) + ops[i]["busy"] <= rt[best] + FILL]
+    pool = {}
+    for i in range(n):
+        if left[i] == 0: pool.setdefault(ops[i]["e"], []).append(i)
+    while any(pool.values()):
+        tmin = {e: max(min(rt[i] for i in l), free.get(e, 0.0) if e else 0.0) for e, l in pool.items() if l}
+        e0 = min(tmin, key=lambda k: tmin[k]); t0 = tmin[e0]
+        best = max((i for i in pool[e0] if rt[i] <= t0 + WIN), key=lambda i: lev[i])
+        if e0 and rt[best] > t0:
+            fill = [i for i in pool[e0] if max(rt[i], t0) + ops[i]["busy"] <= rt[best] + FILL]
             if fill: best = max(fill, key=lambda i: lev[i])
-        i = best; pool.remove(i); op = ops[i]
+        i = best; pool[e0].remove(i); op = ops[i]
         st[i] = max(rt[i], free.get(e0, 0.0)) if e0 else rt[i]
         if e0: free[e0] = st[i] + op["busy"]
         fin[i] = st[i] + op["busy"] + op["lat"]; order.append(i)
@@ -496,8 +496,8 @@ def plan_order(WIN=150, FILL=60, SEED=1, AMP=0.0):
             k = ops[s]["deps"][i]
             rt[s] = max(rt[s], st[i] if k == "order" else fin[i] + (SYNC if k == "sem" else 0))
             left[s] -= 1
-            if left[s] == 0: pool.append(s)
-    pos = {}; cntq = {}
+            if left[s] == 0: pool.setdefault(ops[s]["e"], []).append(s)
+    cntq = {}
     for i in order:
         op = ops[i]
         if "sem" in op: op["clk"] = (op["sem"], 1)
@@ -529,22 +529,39 @@ PLAN = {}
 
 def view(T, a):
     if not isinstance(a, dict): return a
-    v = T[a["n"]][(slice(*a["p"]) if "p" in a else slice(None),) + tuple(a["i"])]
+    v = T[a["n"]][(slice(None),) + tuple(a["i"])]
     if a["ind"] is not None: v = v.indirect(view(T, a["ind"]))
     return v
 
 
 def helpers(T, topo, rank):
     me = T.cores[rank]; n = len(T.cores)
-    far = [T.cores[(rank + k) % n] for k in (1, -1, -3)]
+    far = [T.cores[(rank + k) % n] for k in (1, -1)]
     ok = [c for c in topo.cores_of(me) if c != me and T.rank_of(c) is None and all(topo.may_write(c, f) for f in far)]
     ok.sort(key=lambda c: topo.die(c) != topo.die(me))
     return [ok[k % len(ok)] for k in range(4)]
 
 
-def split_mask(engs, nout, k):
-    m = len(engs) // nout
-    return sum(1 << e for e in engs[k * m:(k + 1) * m]), m
+def first_hop(T, topo, rank, op):
+    me = T.cores[rank]; hs = helpers(T, topo, rank); out = []
+    for k, (via, _s, _d) in enumerate(op["pieces"]):
+        to = T.cores[(rank + op["dist"]) % len(T.cores)] if via is None else hs[via]
+        engs = topo.engines(me, to); m = len(engs) // len(op["pieces"])
+        out.append((to, engs[k * m:(k + 1) * m]))
+    return out
+
+
+def arrivals(T, topo, rank, ops, o):
+    n = len(T.cores); total = 0
+    for p in o["after"]:
+        frm = (rank - ops[p]["dist"]) % n
+        for (via, _s, _d), (to, engs) in zip(ops[p]["pieces"], first_hop(T, topo, frm, ops[p])):
+            total += len(engs) if via is None else len(topo.engines(to, T.cores[rank]))
+    return total
+
+
+def bits(engs):
+    return sum(1 << e for e in engs)
 
 
 def rank_program(g, core, T, topo):
@@ -553,44 +570,44 @@ def rank_program(g, core, T, topo):
     n = len(T.cores); rank = T.rank_of(core)
     if rank is None:
         for rk in range(n):
-            hs = helpers(T, topo, rk)
-            if core not in hs: continue
+            if core not in helpers(T, topo, rk): continue
             sent = 0
             for i in order:
                 op = ops[i]
-                if op["call"] != "send" or hs[op["stream"]] != core: continue
-                outs = op["outs"]; src = view(T, outs[0][0])
-                g.wait_ge(T.sem[outs[0][1]], len(topo.engines(T.cores[rk], core)))
-                trs = []; parts = op["parts"]
-                for k, (dst, sem, dist) in enumerate(outs):
-                    to = T.cores[(rk + dist) % n]; rid, pid = topo.addr(to, core)
-                    mask, m = split_mask(topo.engines(core, to), 1 if parts else len(outs), 0 if parts else k); sent += m
-                    if parts: src = view(T, parts[k])
-                    if parts or len(outs) == 1: g.remote_dma(view(T, dst), src, T.sem[sem], T.sem.sent, pid, rid, mask)
-                    else: trs.append(RemoteDMATransfer(dst_ids=[DstId(rid=rid, pnc=pid)], dma_engine_mask=mask, remote_sem=T.sem[sem], src=src, dst=view(T, dst)))
-                if trs: g.remote_dma_fused(trs, local_sem=T.sem.sent)
+                if op["call"] != "send": continue
+                for (via, _s, dst), (h, engs) in zip(op["pieces"], first_hop(T, topo, rk, op)):
+                    if via is None or h != core: continue
+                    to = T.cores[(rk + op["dist"]) % n]; rid, pid = topo.addr(to, core)
+                    g.wait_ge(T.sem[op["rsem"]], len(engs))
+                    g.remote_dma(view(T, dst), view(T, dst), T.sem[op["rsem"]], T.sem.sent, pid, rid, topo.mask(core, to))
+                    sent += len(topo.engines(core, to))
             g.wait_ge(T.sem.sent, sent)
         return
-    hs = helpers(T, topo, rank)
     Q = {"V": g.vector, "S": g.scalar, "P": g.tensor, "G": g, "Y": g.sync}
+
+    def wait(q, o):
+        if o["call"] == "arrive": q.wait_ge(T.sem[o["sem"]], arrivals(T, topo, rank, ops, o))
+        elif o["call"] == "send": q.wait_ge(T.sem[o["sem"]], sum(len(e) for _c, e in first_hop(T, topo, rank, o)))
+        elif o["call"] == "dma": q.wait_ge(T.sem[o["sem"]], 16)
+        else: q.wait_ge(T.sem[o["sig"][0]], o["sig"][1])
+
     sent = 0
     for i in order:
         op = ops[i]
         if op["e"] is None: continue
         q = Q[op["e"]]
-        for p in op["waits"]:
-            o = ops[p]
-            if o["call"] == "arrive":
-                frm = (rank - o["dist"]) % n
-                h = helpers(T, topo, frm)[ops[o["after"]]["stream"]]
-                q.wait_ge(T.sem[o["sem"]], len(topo.engines(h, core)) // o["nout"])
-            elif o["call"] == "dma": q.wait_ge(T.sem[o["sem"]], 16)
-            else: q.wait_ge(T.sem[o["sig"][0]], o["sig"][1])
+        for p in op["waits"]: wait(q, ops[p])
         a = [view(T, x) for x in op["args"]]; kw = {k: view(T, x) for k, x in op["kw"].items()}; c = op["call"]
         if c == "send":
-            h = hs[op["stream"]]; rid, pid = topo.addr(h, core); dst, sem, _d = op["outs"][0]
-            g.remote_dma(a[0] if op["parts"] else view(T, dst), a[0], T.sem[sem], T.sem.sent, pid, rid, topo.mask(core, h))
-            sent += len(topo.engines(core, h)); continue
+            loc = T.sem[op.get("sem", "sent")]; trs = []
+            for (_v, src, dst), (to, engs) in zip(op["pieces"], first_hop(T, topo, rank, op)):
+                rid, pid = topo.addr(to, core)
+                if "sem" not in op: sent += len(engs)
+                if len(op["pieces"]) == 1: g.remote_dma(view(T, dst), view(T, src), T.sem[op["rsem"]], loc, pid, rid, bits(engs))
+                else: trs.append(RemoteDMATransfer(dst_ids=[DstId(rid=rid, pnc=pid)], dma_engine_mask=bits(engs), remote_sem=T.sem[op["rsem"]],
+                                                   src=view(T, src), dst=view(T, dst)))
+            if trs: g.remote_dma_fused(trs, local_sem=loc)
+            continue
         if c == "dma":
             q.dma_start(a[0], a[1]).then_inc(T.sem[op["sem"]], 16); continue
         if c == "ts": ins = q.tensor_scalar(*a)
@@ -602,9 +619,9 @@ def rank_program(g, core, T, topo):
         elif c == "rcp": ins = q.reciprocal(*a)
         elif c == "act": ins = q.activation(*a, **kw)
         elif c == "mm": ins = q.matmul(*a)
-        elif c == "tr": ins = q.transpose(*a)
+        elif c == "sel": ins = q.affine_select(*a)
         else: ins = q.iota(*a, **kw)
         if "sig" in op: ins.then_inc(T.sem[op["sig"][0]], 1)
     g.wait_ge(T.sem.sent, sent)
     for i in order:
-        if ops[i]["call"] == "dma" and i not in PLAN["need"]: g.sync.wait_ge(T.sem[ops[i]["sem"]], 16)
+        if "sem" in ops[i] and i not in PLAN["need"]: wait(g.sync, ops[i])

@@ -18,23 +18,24 @@ def _sb(shape, dt):
 
 SCRATCH = {
     "XA": _sb([2304], BF), "XB0": _sb([2304], BF), "XB1": _sb([2304], BF),
-    "OWA": _sb([1280], F32), "OWB0": _sb([1280], F32), "OWB1": _sb([1280], F32),
-    "nbi": _sb([512], I32), "vi": _sb([16], I32), "vw": _sb([16], I32),
+    "OWA": _sb([2312], F32), "OWB0": _sb([2312], F32), "OWB1": _sb([2312], F32),
+    "nbi": _sb([512], I32), "nbB": _sb([512], I32), "vi": _sb([16], I32), "vw": _sb([16], I32),
     "Xg": _sb([4096], BF), "near": _sb([4096], BF), "Pu": _sb([256], U16), "Pf": _sb([256], F16), "zT": _sb([256], F16),
     "zl": _sb([12 * 128], BF), "zin": _sb([4 * 128], BF), "LS": _sb([12 * 16], U16), "lin": _sb([32], U16), "l0": _sb([32], U16),
-    "MO": _sb([16, 56], F32), "MI": _sb([4, 48], F32), "EO": _sb([4, 16], F32), "E1": _sb([4, 16], F32), "E3": _sb([4, 32], F32),
-    "FI": _sb([4, 8], F32), "Mx": _sb([272], F32), "Qs": _sb([272], F32), "r2": _sb([16, 8], F32),
-    "VV": _sb([4, 24], F32), "WW": _sb([2, 24], F32), "bt": _sb([4 * 128], F16), "U": _sb([4, 8], F32), "hp": _sb([512, 8], F32),
-    "OA": _sb([NOH * 128], BF), "OB": _sb([NOH * 144], F16),
+    "MO": _sb([16, 64], F32), "MI": _sb([4, 64], F32), "EO": _sb([4, 16], F32), "E1": _sb([4, 16], F32), "E3": _sb([4, 32], F32),
+    "FI": _sb([4, 8], F32), "Mx": _sb([272], F32), "Dq": _sb([272], F32), "Qs": _sb([272], F32), "r2": _sb([16, 8], F32),
+    "VV": _sb([4, 24], F32), "WW": _sb([2, 24], F32), "bt": _sb([4 * 128], F16), "U": _sb([4, 8], F32),
+    "hp": _sb([512, 8], F32), "hq": _sb([32, 16], F32), "OA": _sb([NOH * 128], BF), "OB": _sb([NOH * 144], F16),
     "exs": _sb([1024], F32), "Rm": _sb([1024], F32), "hit": _sb([128], F16), "hitT": _sb([128], BF),
     "zt": _sb([256], F32), "cn": _sb([32], F32), "ynb": _sb([512], F32), "yvb": _sb([16], F32),
     "iJ": _sb([240], F32), "pi": _sb([4], I32), "pf": _sb([24], F32), "it": _sb([152], F32), "ct": _sb([272], F32),
     "Ib": _sb([128], BF), "If": _sb([128], F32), "nBig": _sb([128], F32), "hI": _sb([128], BF),
     "sI": _sb([6 * 128], BF), "BTs": _sb([240], F16), "Perm": _sb([136], F16), "m8": _sb([8], F32), "M16": _sb([16], F32),
-    "seg": _sb([136], F32), "cm": _sb([408], BF), "Dq": _sb([272], F32), "BM": _sb([16], F32), "BL": _sb([8], U16),
+    "seg": _sb([136], BF), "cm": _sb([408], BF), "BM": _sb([16], F32),
+    "BL": _sb([8], U16), "BP": _sb([4], U16), "BR": _sb([8], U16), "B8": _sb([2], U16),
     "Sel": _sb([2048], BF), "Rr": _sb([2048], BF), "pw": _sb([64], F32), "W": _sb([8], BF), "Wu": _sb([8], BF), "cI0": _sb([16], F32),
-    "one": _sb([256], BF), "oneF": _sb([256], F32), "iA": _sb([128], BF), "nA": _sb([128], BF),
-    "Dt": _sb([128], F32), "Dm": _sb([128], F32), "Dh": _sb([128], F16), "iB": _sb([144], BF),
+    "one": _sb([256], BF), "oneF": _sb([256], F32), "iA": _sb([128], BF), "nA": _sb([128], BF), "iC": _sb([128], BF),
+    "Dt": _sb([128], F32), "Dm": _sb([128], F32), "Dh": _sb([128], BF), "iB": _sb([144], BF),
     "d0": ("psum", [128, 512], F32), "d1": ("psum", [128, 512], F32), "d2": ("psum", [128, 512], F32),
     "key": ("psum", [128, 512], F32), "msc": ("psum", [128, 512], F32),
     "ex0": ("psum", [128, 512], F32), "ex1": ("psum", [128, 512], F32), "pen": ("psum", [128, 512], F32),
@@ -46,12 +47,12 @@ SEMAPHORES = (["cV", "cS", "cP", "cG", "sent"] + ["dm%d" % i for i in range(NDMA
 IO = {"tracks": [128, 2048], "nb": [128, 512], "v": [128, 16], "z": [128, 256],
       "yx": [128, 2048], "yn": [128, 512], "yv": [128, 16], "yz": [128, 256]}
 
-COST = {"CY": 0.87, "PCY": 0.42, "GA": 1.56, "SYNC": 90.0, "RELAY": 4200.0, "DIRECT": 2200.0, "ISSUE": 900.0, "FIXV": 30.0, "FIXP": 15.0,
-        "BULK": 6500.0}
-OPT = {"vg": [512, 0, 256, 0, 512, 0, 0, 0],
-       "nsc": [2, 6, 2, 4, 5, 5, 4, 6],
-       "xv": [1, 3], "rs": 14, "e0": 1, "e1": 0, "pre": 0}
-BLK = [256, 512, 512, 512, 256]
+COST = {"CY": 0.87, "PCY": 0.42, "GA": 1.56, "SYNC": 90.0, "RELAY": 4200.0, "DIRECT": 2200.0, "ISSUE": 900.0, "FIXV": 50.0, "FIXP": 15.0,
+        "BULK": 6500.0, "FIRST": 3000.0}
+OPT = {"vg": [257, 1793, 1, 1, 1, 1, 1, 1],
+       "nsc": [1, 1, 1, 1, 1, 1, 1, 1],
+       "e0": 1, "e1": 0, "pre": 20000, "blk": 0, "pv": 1, "pp": 0, "pu": 0, "bv": 0, "tp": 0, "w": 2000, "pr": 500, "rs2": 1, "pa": 0, "pe": 0}
+BLK = ([256, 512, 512, 512, 256], [512, 512, 512, 512], [512, 512, 512, 256, 256])
 
 
 def A(name, *idx):
@@ -113,19 +114,30 @@ def build_ops(K, O):
     def ms(out, val):
         return add("V", "ms", [out, val], [out], [], FIXV + max(64, out["k"] * (0.5 if two(out) else 1)) * CY)
 
+    def red(out, a):
+        return add("V", "red", [out, a, AxisListType.X, ALU.add], [out], [a], FIXV + 64 * CY)
+
     def act(out, a, bias=None, scale=None, fn=None):
         kw = {}
         if bias is not None: kw["bias"] = bias
         if scale is not None: kw["scale"] = scale
-        c = 65 + a["k"] * GA * CY if a["ind"] is not None else 60 + max(64, a["k"]) * CY
+        c = 65 + a["k"] * GA * CY if a["ind"] is not None else 65 + max(64, a["k"]) * CY
         return add("S", "act", [out, a, fn if fn is not None else ACT.Identity if kw else ACT.Copy], [out], [a, bias, scale], c, kw=kw)
 
     def mm(out, l, r, start=True, stop=True):
         return add("P", "mm", [out, l, r, start, stop], [out], [l, r], FIXP + max(64, r["k"]) * PCY * (4 if l["dt"] == F32 else 1), lat=60)
 
+    def sel(out, a, pat, op, fill, base):
+        return add("G", "sel", [out, a, pat, op, fill, base, 1], [out], [a], 170 + 2 * out["k"] * CY)
+
     def iota(out, pat, base, cm):
         kw = {} if out["dt"] == I32 else {"allow_small_or_imprecise_dtypes": True}
         return add("G", "iota", [out, pat, base, cm], [out], [], 130 + 2 * out["k"] * CY, kw=kw)
+
+    def flex(first, second, pen=0.0):
+        a = first(); b = second(); ops.pop()
+        a["alt"] = {k: b[k] for k in ("e", "call", "args", "kw", "busy")}; a["r"] = a["r"] + b["r"]; a["pen"] = pen
+        return a
 
     nd = [0]; prev = [None]
 
@@ -140,15 +152,15 @@ def build_ops(K, O):
 
     def bulk(src, dst, a, n, vias, sem, loc):
         m = n // len(vias)
-        o = add("G", "send", [C(src, a, n)], [], [C(src, a, n)], K["ISSUE"], lat=2500, rsem=sem, dist=-1, sem=loc, behind=prev[0],
+        o = add("G", "send", [C(src, a, n)], [], [C(src, a, n)], K["ISSUE"], lat=2500, rsem=sem, dist=-1, sem=loc, behind=prev[0], up=1e7,
                 pieces=[(h, C(src, a + m * k, m), C(dst, a + m * k, m)) for k, h in enumerate(vias)])
         prev[0] = o["id"]
         return o["id"]
 
-    def landed(dst, n, sem, after):
-        add(None, "arrive", [], [C(dst, 0, n)], [], 0, lat=K["BULK"] - 2500, after=after, sem=sem)
+    def landed(dst, n, sem, after, more=0.0):
+        add(None, "arrive", [], [C(dst, 0, n)], [], 0, lat=K["BULK"] - 2500 + more, after=after, sem=sem)
 
-    E, GE, GT, LT = ALU.is_equal, ALU.is_ge, ALU.is_gt, ALU.is_lt
+    E, GE, GT, LT, NE = ALU.is_equal, ALU.is_ge, ALU.is_gt, ALU.is_lt, ALU.not_equal
     AD, SU, MU, MX, MN = ALU.add, ALU.subtract, ALU.mult, ALU.max, ALU.min
     W_ = lambda n: A(n, *[S(None, None)] * (len((SCRATCH[n][1] if n in SCRATCH else IO[n])) - 1))
 
@@ -165,6 +177,8 @@ def build_ops(K, O):
     iota(W_("cI0"), [[128, 2], [0, 8]], 960, 1)
     iota(C("iB", 0, 16), [[128, 16]], -1024, 0)
     iota(C("iB", 16, 128), [[-1024, 16], [128, 8]], 16384, 0)
+    iota(W_("iC"), [[0, 8], [128, 16]], -1024, 0)
+    iota(W_("iA"), [[1, 128]], -64, 0); iota(W_("nA"), [[-1, 128]], 64, 0)
     ts(C("pi", 1, 1), C("pi", 0, 1), 15, ALU.bitwise_and)
     ts(C("pi", 2, 1), C("pi", 0, 1), 4, ALU.logical_shift_right)
     ts(C("pi", 3, 1), C("pi", 0, 1), 7, ALU.bitwise_and)
@@ -173,13 +187,16 @@ def build_ops(K, O):
     pc, pm, pd, p8 = pf(0), pf(1), pf(2), pf(3)
     J = lambda n: C("iJ", 0, n)
     ts(W_("Ib"), J(128), pc, E)
-    ts(C("sI", 0, 128), W_("Ib"), 32 / 28.5, MU); ts(C("sI", 128, 128), W_("Ib"), -32 / 28.5, MU); ts(W_("hI"), W_("Ib"), 0.5, MU)
-    act(W_("If"), W_("Ib")); act(W_("nBig"), W_("Ib"), scale=-DEAD)
+    ts(C("sI", 0, 128), W_("Ib"), 32 / 28.5, MU); ts(C("sI", 128, 128), W_("Ib"), -32 / 28.5, MU)
+    zb, zf = C("one", 128, 128), W_("Dt")
+    iota(zb, [[0, 128]], 0, 0); iota(zf, [[0, 128]], 0, 0)
+    for n, z, val in (("If", zf, 1.0), ("nBig", zf, -DEAD), ("hI", zb, 0.5), ("Dm", zf, 1.0), ("Dh", zb, 1.0)): sel(W_(n), z, [[-1, 128]], NE, val, 0)
+    for n in ("Dm", "Dh"): sel(W_(n), W_(n), [[-1, 128]], NE, -1.0, -1)
     ts(pf(4), pd, 17.0, MU, 15.0, AD); tt(pf(5), pf(4), pm, SU); ts(W_("Perm"), J(136), pf(5), E)
     ts(W_("BTs"), J(240), -112.0, AD, pm, E)
     ts(W_("m8"), J(8), pd, E); ts(W_("M16"), J(16), pm, E)
     pos = C("it", 16, 136)
-    ts(W_("seg"), pos, 1.5, GT)
+    act(W_("seg"), pos, bias=-384.0, scale=256.0, fn=ACT.Sigmoid)["busy"] += 1300
     ts(C("cm", 0, 136), pos, 17.0, E, 34816.0 * KS / 128, MU); ts(C("cm", 272, 136), pos, 17.0, E, DEAD / 128, MU)
     ts(pf(6), pc, 0.0, E, 4096.0, MU); ts(pf(7), pc, 1.0, E, -1088.0, MU); ts(pf(8), pc, 2.0, E, 0.5, MU); tt(pf(9), pf(7), pf(8), AD)
     ts(C("ct", 0, 136), pos, 16.5, LT, pf(9), MU); ts(C("ct", 136, 136), pos, -18.0, AD, pf(6), MU)
@@ -187,40 +204,48 @@ def build_ops(K, O):
     ts(W_("cI0"), W_("cI0"), 0.5, AD)
     ts(W_("BM"), C("it", 0, 16), pd, E)
     tt(pf(10), p8, pd, E); ts(pf(11), pm, 8.0, GE, 8.0, MU); ts(pf(12), pf(11), 8.0, AD); ts(W_("BL"), J(8), pf(12), AD, pf(10), MU)
+    ts(pf(15), pm, 8.0, GE, 16.0, AD); ts(C("pf", 16, 4), J(4), 2.0, MU, pf(15), AD); ts(W_("BP"), C("pf", 16, 4), pf(10), MU)
     ms(C("pw", 0, 16), 0.5); ms(C("pw", 16, 16), 0.0)
     scan(C("pw", 32, 16), C("pw", 0, 16), C("pw", 16, 16), 65536.0 * KS, MU, AD)
-    tt(C("pw", 48, 16), C("pw", 32, 16), W_("M16"), MU)
-    add("V", "red", [pf(13), C("pw", 48, 16), AxisListType.X, AD], [pf(13)], [C("pw", 48, 16)], 100)
+    tt(C("pw", 48, 16), C("pw", 32, 16), W_("M16"), MU); red(pf(13), C("pw", 48, 16))
     ts(pf(14), pm, 2.0, MU, 1.0, AD)
     ts(W_("W"), W_("m8"), pf(13), MU); ts(W_("Wu"), W_("m8"), pf(14), MU)
-    ms(C("one", 0, 128), 1.0); ms(C("one", 128, 128), 0.0)
-    ms(C("oneF", 0, 128), 1.0); ms(C("oneF", 128, 128), -1.0)
-    ts(W_("iA"), J(128), -63.5, AD); ts(W_("nA"), J(128), -1.0, MU, 63.0, AD)
-    ts(W_("Dt"), J(128), -1.0, AD, pc, E); tt(W_("Dm"), W_("Dt"), W_("If"), SU)
-    ts(pf(15), pc, 127.0, E); tt(C("Dm", 0, 1), C("Dm", 0, 1), pf(15), SU); cp(W_("Dh"), W_("Dm"))
-    for k in range(16): (act if k < O["rs"] else cp)(A("Rr", S(k, 2048, 16)), W_("Ib"))
-    ms(A("MO", S(0, 16), S(0, 8)), -63.5); ms(A("VV", S(0, 4), S(0, 8)), -63.5); ms(A("WW", S(0, 2), S(0, 8)), -63.5)
-    ms(C("OWA", 1024, 256), -OFF)
+    iota(C("one", 0, 128), [[0, 128]], 1, 0); iota(W_("oneF"), [[-2, 2], [0, 128]], 1, 0)
+    cp(W_("BR"), J(8)); cp(C("B8", 0, 1), p8)
+    for k in range(16): flex(lambda: act(A("Rr", S(k, 2048, 16)), W_("Ib")), lambda: cp(A("Rr", S(k, 2048, 16)), W_("Ib")), O["pr"])
+    ms(A("MO", S(0, 16), S(0, 16)), -63.5); ms(A("VV", S(0, 4), S(0, 8)), -63.5); ms(A("WW", S(0, 2), S(0, 8)), -63.5)
+    iota(C("OWA", 0, 8), [[0, 8]], 1, 0); iota(C("OWA", 2056, 256), [[0, 256]], -1023, 0)
     for r in range(NR):
-        ms(C("OWB%d" % r, OWN, 1280 - OWN), -OFF); ms(C("XB%d" % r, 2048, 256), 0.0)
-    for h in range(2):
-        y, R = C("d0", 256 * h, 256), C("Rm", 256 * h, 256)
-        ts(y, C("nbi", 256 * h, 256), -OFF, AD); ts(R, y, BIG2, AD, BIG2, SU)
-        tt(C("OWA", 256 * h, 256), y, R, SU)
-        act(C("OWA", 512 + 256 * h, 256), R, bias=-OFF, scale=1 / 2048.0)
+        for a in (OWN, 2056): iota(C("OWB%d" % r, a, 256), [[0, 256]], -1023, 0)
+        iota(C("XB%d" % r, 2048, 256), [[0, 256]], 0, 0)
+
+    def unpack(src, dst, bank, n):
+        for a in range(0, 512, n):
+            y, R = C(bank, a, n), C("Rm", a, n)
+            ts(y, C(src, a, n), -OFF, AD); ts(R, y, BIG2, AD, BIG2, SU)
+            tt(C(dst, 8 + a, n), y, R, SU)
+            act(C(dst, 520 + a, n), R, bias=-OFF, scale=1 / 2048.0)
+
+    def twice(n):
+        o = dma("Y", C(n, OWN, 1024), C(n, 8, 1024), 524288)
+        if n == "OWA": o["left"] = prev[0]
 
     def copies(r, what):
         seq[0] = 8 * r + 2
-        if what == "o": landed("OWB%d" % r, OWN, "bo%d" % r, [bulk("OWA", "OWB%d" % r, 0, OWN, [0, 2, 1, 3], "bo%d" % r, "so%d" % r)])
+        if what == "o" and r == 0:
+            landed("nbB", 512, "bo0", [bulk("nbi", "nbB", 0, 512, [0, 2, 1, 3], "bo0", "so0")], K["FIRST"] - 1500)
+            unpack("nbB", "OWB0", "pen", 512)
+        elif what == "o": landed("OWB%d" % r, OWN, "bo%d" % r, [bulk("OWA", "OWB%d" % r, 0, OWN, [0, 2, 1, 3], "bo%d" % r, "so%d" % r)])
         else: landed("XB%d" % r, 2048, "bx%d" % r, [bulk("XA", "XB%d" % r, 0, 1024, [0, 2], "bx%d" % r, "sx%d" % r),
                                                       bulk("XA", "XB%d" % r, 1024, 1024, [1, 3], "bx%d" % r, "sy%d" % r)])
         seq[0] = 99
 
-    copies(0, "o"); copies(0, "x")
-    o = iota(W_("Sel"), [[0, 2048]], -33, 0); o["behind"] = prev[0]
-    add("G", "sel", [W_("Sel"), W_("Sel"), [[-1, 16], [-16, 8], [0, 16]], E, 0.0, 0, 1], [W_("Sel")], [W_("Sel")], 170 + 2 * 2048 * CY)
+    unpack("nbi", "OWA", "d0", 256)
+    copies(0, "o"); copies(0, "x"); twice("OWA")
+    iota(W_("Sel"), [[0, 2048]], -33, 0)["behind"] = prev[0]
+    sel(W_("Sel"), W_("Sel"), [[-1, 16], [-16, 8], [0, 16]], E, 0.0, 0)
 
-    cnt = {"d": 0, "bt": 0, "oh": 0, "hp": 0}
+    cnt = {"d": 0, "bt": 0, "oh": 0, "hp": 0, "hq": 0}
 
     def nxt(k, m, step=1):
         v = cnt[k]; cnt[k] = (v + step) % m
@@ -234,12 +259,14 @@ def build_ops(K, O):
 
     KEY = ("key", "msc")
 
-    def turn(win, c):
+    def turn(win, c, lst="BL", n=16):
         b = nxt("bt", 4)
-        act(C("bt", 128 * b, 128), IND(win, W_("BL")), bias=63.5)
+        x, y = C("bt", 128 * b, 8 * n), IND(win, W_(lst))
+        if O["bv"]: flex(lambda: act(x, y, bias=63.5), lambda: ts(x, y, 63.5, AD))
+        else: act(x, y, bias=63.5)
         for gi in range(8):
-            mm(C(KEY[c], 272, 16), C("BTs", 112 - 16 * gi, 128), C("bt", 128 * b + 16 * gi, 16), gi == 0, gi == 7)
-        return C(KEY[c], 272, 16)
+            mm(C(KEY[c], 272, n), C("BTs", 112 - 16 * gi, 128), C("bt", 128 * b + n * gi, n), gi == 0, gi == 7)
+        return C(KEY[c], 272, n)
 
     def low(out, v, cs):
         h = hp2(); ts(H(h, cs), v, 1024.0 - PO, GE, -1024.0, MU); tt(out, v, H(h, cs), AD)
@@ -247,7 +274,7 @@ def build_ops(K, O):
     M = lambda r, s, cs, a, n=8: A("MO", S(r * 8 + s * 2 + cs[0], r * 8 + s * 2 + cs[-1] + 1), S(a, a + n))
     MI = lambda r, cs, a, n=8: A("MI", S(r * 2 + cs[0], r * 2 + cs[-1] + 1), S(a, a + n))
     R2 = lambda r, s, cs: A("r2", S(r * 8 + s * 2 + cs[0], r * 8 + s * 2 + cs[-1] + 1), S(0, 8))
-    GO = lambda r, s, cs: M(r, s, cs, 16 if s == 3 else 24)
+    GO = lambda r, s, cs, n=8: M(r, s, cs, 48 if s == 3 else 24, n)
     b2 = (0, 1)
 
     def both(n, j, cs=b2):
@@ -256,17 +283,18 @@ def build_ops(K, O):
     def station(r, s, c):
         jo = r * 8 + s * 2 + c; j = r * 6 + s * 2 + c; seq[0] = jo; cs = (c,)
         tb = "B%d" % r if s % 2 else "A"; si = 2 * (1 + s % 2) if r else 0
-        L = C("l0", 16 * r + 8 * c, 8) if s == 0 else C("lin", 8 * (2 * r + c), 8) if s == 2 else C("LS", 16 * (j - 2) + 8, 8)
+        L = C("l0", 16 * r + 8 * c, 8) if s == 0 else C("lin", 8 * (2 * r + c), 8) if s == 2 else C("LS", 16 * (j - 2) + (8 if s == 3 else 0), 8)
         Z = C("XA", 2048 + 128 * c, 128) if s == 0 else C("zin", 128 * (2 * r + c), 128) if s == 2 else C("zl", 128 * (j - 2), 128)
         Pf, Pu = C("Pf", 128 * c, 128), C("Pu", 128 * c, 128)
-        act(Pf, IND(W_("OW" + tb) if s else C("OWA", 0, 1024), L), bias=OFF); cp(Pu, Pf)
+        ow = IND(C("OW" + tb, 8, (1024, 1280, 2304, 2304)[s]), L)
+        if O["pv"]: ts(Pu, ow, OFF, AD); flex(lambda: act(Pf, ow, bias=OFF), lambda: cp(Pf, Pu), O["pp"])["up"] = -O["pu"]
+        else: act(Pf, ow, bias=OFF); cp(Pu, Pf)
         d = "d%d" % nxt("d", 3)
         mm(C(d, 0, 128), Z, C("sI", 128 * si + 128, 128)); act(C("zT", 128 * c, 128), C(d, 0, 128))
         b = 0; vg = O["vg"][2 * s + c]
-        for n in BLK:
+        for n in BLK[O["blk"]]:
             o = 2048 * c + b
-            (cp if vg >= n else act)(C("Xg", o, n), IND(C("X" + tb, 0, 2048), C("Pu", o // 16, n // 16)))
-            if vg >= n: vg -= n
+            (cp if vg == b + 1 else act)(C("Xg", o, n), IND(C("X" + tb, 0, 2048), C("Pu", o // 16, n // 16)))
             d = C("d%d" % nxt("d", 3), 0, n)
             mm(d, C("zT", 128 * c, 128), C("Rr", b, n), True, False)
             mm(d, C("sI", 128 * si, 128), C("Xg", o, n), False, True)
@@ -277,74 +305,87 @@ def build_ops(K, O):
         Mx = A("Mx", S(o + 16, o + 136, 17))
         mm(C(key, 0, 272), C("one", 0, 128), C("cm", ko, 272), True, False)
         mm(pay, Pf, W_("Perm"), False, False)
-        mm(A(key, S(po + 16, po + 136, 17)), W_("If"), C("cI0", 8 * c, 8) if s == 0 else MI(r, cs, 0) if s == 2 else M(r, s - 1, cs, 8), False, False)
+        mm(A(key, S(po + 16, po + 136, 17)), W_("If"), C("cI0", 8 * c, 8) if s == 0 else MI(r, cs, 16) if s == 2 else M(r, s - 1, cs, 16), False, False)
         if s:
-            mm(mk, W_("If"), MI(r, cs, 24) if s == 2 else Mx, False, False)
-            mm(mk, W_("nBig"), MI(r, cs, 16) if s == 2 else GO(r, s - 1, cs), False, False)
-        for k in range(16):
-            mm(A(key, S(ko + 15 - k, ko + 136, 17)), A("near", S(2048 * c + k, 2048 * c + 2048, 16)), W_("W"), False, k == 15)
+            mm(mk, W_("If"), MI(r, cs, 40) if s == 2 else Mx, False, False)
+            mm(mk, W_("nBig"), MI(r, cs, 24) if s == 2 else GO(r, s - 1, cs), False, False)
+        for p0, p1 in ((0, 96), (96, 128)) if O["tp"] else ((0, 128),):
+            for k in range(16):
+                out = dict(A(key, S(ko + 15 - k, ko + 136, 17)), p=(p0, p1))
+                x = mm(out, A("near", S(2048 * c + 16 * p0 + k, 2048 * c + 16 * p1, 16)), W_("W"), False, k == 15 and p1 == 128)
+                x["busy"] = FIXP + min(64, p1 - p0) * PCY
         scan(C("Mx", o, 136), W_("seg"), kk, 0.0, MU, MX)
         tt(C("Dq", o, 136), kk, C("Mx", o, 136), SU)
         scan(C("Qs", o, 136), C("Dq", o, 136), pay, 0.0, MX, MN)
-        Q, P = A("Qs", S(o + 16, o + 136, 17)), M(r, s, cs, 8)
+        Q, P = A("Qs", S(o + 16, o + 136, 17)), M(r, s, cs, 16)
         ts(R2(r, s, cs), Q, BIGP, AD, BIGP, SU); tt(P, Q, R2(r, s, cs), SU)
+        go = lambda: act(A("MO", jo, S(48, 64) if s == 3 else S(24, 40)), IND(A("r2", jo, S(0, 8)), C("B8", 0, 1)), bias=-4096.0, scale=-1.0, fn=ACT.Sign)
         if s == 3:
-            ts(GO(r, s, cs), R2(r, s, cs), -5000.0, LT)
+            act(M(r, s, cs, 24), R2(r, s, cs), bias=8192.0, fn=ACT.Relu)
             n = 32 if c == 0 and r < NR - 1 else 16
-            send(A("MO", jo, S(8, 8 + n)), A("E3", 2 * r + c, S(0, n)), "b%d" % (2 * r + c), 1, 0)
-            send(A("MO", jo, S(8, 16)), A("FI", 2 * r + c, S(0, 8)), "f%d" % (2 * r + c), -2)
-            seq[0] = 99
+            send(A("MO", jo, S(16, 16 + n)), A("E3", 2 * r + c, S(0, n)), "b%d" % (2 * r + c), 1, 0)
+            send(A("MO", jo, S(16, 24)), A("FI", 2 * r + c, S(0, 8)), "f%d" % (2 * r + c), -2)
+            go(); seq[0] = 99
             return
-        low(M(r, s, cs, 16), P, cs)
-        ts(C("LS", 16 * j, 16), turn(A("MO", jo, S(0, 24)), c), 1024.0, AD)
-        ts(GO(r, s, cs), R2(r, s, cs), -5000.0, LT)
+        if s == 0:
+            low(M(r, s, cs, 8), P, cs)
+            ts(C("LS", 16 * j, 16), turn(A("MO", jo, S(0, 24)), c), 1024.0, AD)
+        else: ts(C("LS", 16 * j + 8, 8), turn(A("MO", jo, S(0, 24)), c, "BP", 8), 1024.0, AD)
         if s == 1: send(C("LS", 16 * j + 8, 8), C("lin", 8 * (2 * r + c), 8), "l%d" % (2 * r + c), 2)
-        act(C("zl", 128 * j, 128), IND(W_("X" + tb), C("LS", 16 * j, 8)))
+        act(C("zl", 128 * j, 128), IND(W_("X" + tb), C("LS", 16 * j + 8, 8)))
+        go()
         if s == 1:
             send(C("zl", 128 * j, 128), C("zin", 128 * (2 * r + c), 128), "z%d" % (2 * r + c), 2)
-            act(M(r, s, cs, 32), Mx); diff(r, s, cs)
-            send(A("MO", jo, S(8, 56)), A("MI", 2 * r + c, S(0, 48)), "m%d" % (2 * r + c), 2)
+            act(M(r, s, cs, 40), Mx); diff(r, s, cs)
+            send(A("MO", jo, S(16, 64)), A("MI", 2 * r + c, S(16, 64)), "m%d" % (2 * r + c), 2)
         seq[0] = 99
 
-    def diff(r, s, cs):
-        w = both("WW", r, cs) if s == 0 else M(r, 0, cs, 16) if s == 1 else MI(r, cs, 8)
-        e1, e2 = hp2(), hp2()
-        act(H(e1, cs), R2(r, s, cs), bias=19456.0, scale=0.25); tt(H(e2, cs), w, M(r, s, cs, 8), SU)
-        tt(M(r, s, cs, 40), H(e1, cs), H(e2, cs), AD)
+    def scales(sc, a):
+        x, y = C("sI", a, 128), C("sI", a + 128, 128)
+        flex(lambda: act(x, W_("Ib"), scale=sc), lambda: ts(x, W_("Ib"), sc, MU)); flex(lambda: act(y, x, scale=-1.0), lambda: ts(y, x, -1.0, MU))
 
-    def event(code, wt, cs, gon, P, go, d, um1):
-        t1, t2 = hp2(), hp2()
-        tt(H(t1, cs), gon, d, MU); tt(code, H(t1, cs), P, AD); tt(H(t2, cs), gon, um1, MU); tt(wt, H(t2, cs), go, AD)
+    def diff(r, s, cs):
+        w = both("WW", r, cs) if s == 0 else M(r, 0, cs, 8) if s == 1 else MI(r, cs, 8)
+        e1, e2 = hp2(), hp2()
+        act(H(e1, cs), R2(r, s, cs), bias=19456.0, scale=0.25); tt(H(e2, cs), w, M(r, s, cs, 16), SU)
+        tt(M(r, s, cs, 48), H(e1, cs), H(e2, cs), AD)
+
+    def event(out, cs, gon, pg, du):
+        t = nxt("hq", 32, 2); t = A("hq", S(t + cs[0], t + cs[-1] + 1), S(0, 16))
+        tt(t, gon, du, MU); tt(out, t, pg, AD)
 
     def local_event(r, s, cs):
-        code, wt = hp2(), hp2()
-        event(H(code, cs), H(wt, cs), cs, GO(r, s + 1, cs), M(r, s, cs, 8), GO(r, s, cs), M(r, s, cs, 40), M(r, 1, cs, 48) if s == 0 else MI(r, cs, 40))
-        hist(s, cs, H(code, cs), H(wt, cs), lambda c, g: A("hp", wt + c, S(g, g + 1)))
+        e = nxt("hq", 32, 2)
+        event(A("hq", S(e + cs[0], e + cs[-1] + 1), S(0, 16)), cs, GO(r, s + 1, cs, 16), M(r, s, cs, 16, 16), M(r, s, cs, 48, 16))
+        hist(s, cs, "hq", e)
 
-    def hist(s, cs, code, wt, wcol):
-        bR, a = hp2(), hp2()
-        ts(H(bR, cs), code, BIG3, AD, BIG3, SU); tt(H(a, cs), code, H(bR, cs), SU)
-        wh = hp2()
-        if any(O["nsc"][2 * s + c] for c in cs): act(H(wh, cs), wt, scale=0.5)
+    def hist(s, cs, n, j):
+        code = A(n, S(j + cs[0], j + cs[-1] + 1), S(0, 8))
+        bR, a, a2, bm = hp2(), hp2(), hp2(), hp2()
+        ts(H(bR, cs), code, BIG3, AD, BIG3, SU)
+        if any(O["nsc"][2 * s + c] for c in cs):
+            tt(H(a, cs), code, H(bR, cs), SU); act(H(a2, cs), H(a, cs), scale=256.0)
+        if s == 3: tt(H(bm, cs), H(bR, cs), A(n, S(j + cs[0], j + cs[-1] + 1), S(8, 16)), AD)
         for c in cs:
+            if s == 3:
+                o3 = nxt("oh", NOH); tt(C("OB", 144 * o3, 128), IND(A("hp", bm + c, S(0, 8)), W_("BR")), W_("iC"), E)
             for gi in range(8):
-                o = nxt("oh", NOH); col = S(gi, gi + 1); n = 16 if s == 3 else 144
-                oa, ac = C("OA", 128 * o, 128), A("hp", a + c, col)
-                if gi >= 8 - O["nsc"][2 * s + c]:
-                    act(oa, W_("nA"), bias=ac, fn=ACT.Sign); wc = A("hp", wh + c, col)
-                else:
-                    ts(oa, W_("iA"), ac, LT, 0.5, SU); wc = wcol(c, gi)
-                ts(C("OB", 144 * o, n), C("iB", 0, n), A("hp", bR + c, col), E, wc, MU)
-                if s < 3: mm(C("ex%d" % (gi // 4), 128 * (gi % 4), 128), oa, C("OB", 144 * o + 16, 128), False, (s, c, gi % 4) == (2, 1, 3))
-                mm(C("pen", 16 * gi, 16), oa, C("OB", 144 * o, 16), False, (s, c, gi) == (3, 1, 7))
+                o = nxt("oh", NOH); col = S(gi, gi + 1)
+                oa, bc = C("OA", 128 * o, 128), A("hp", bR + c, col)
+                on_v = lambda: ts(oa, W_("iA"), bc, AD, A(n, j + c, col), LT)
+                if O["nsc"][2 * s + c]: flex(lambda: act(oa, W_("nA"), bias=A("hp", a2 + c, col), scale=256.0, fn=ACT.Sigmoid), on_v, O["pa"])
+                else: on_v()
+                if s < 3:
+                    ts(C("OB", 144 * o, 144), W_("iB"), bc, E, A(n, j + c, S(8 + gi, 9 + gi)), MU)
+                    mm(C("ex%d" % (gi // 4), 128 * (gi % 4), 128), oa, C("OB", 144 * o + 16, 128), False, (s, c, gi % 4) == (2, 1, 3))
+                mm(C("pen", 16 * gi, 16), oa, C("OB", 144 * o3 + 16 * gi if s == 3 else 144 * o, 16), False, (s, c, gi) == (3, 1, 7))
 
     def far_hist(r, s, cs):
-        n = "E1" if s == 1 else "E3"; sl = S(2 * r + cs[0], 2 * r + cs[-1] + 1)
-        hist(s, cs, A(n, sl, S(0, 8)), A(n, sl, S(8, 16)), lambda c, g: A(n, 2 * r + c, S(8 + g, 9 + g)))
+        hist(s, cs, "E1" if s == 1 else "E3", 2 * r)
 
     def back_event(r, cs):
         sl = S(2 * r + cs[0], 2 * r + cs[-1] + 1)
-        event(A("EO", sl, S(0, 8)), A("EO", sl, S(8, 16)), cs, GO(r, 2, cs), MI(r, cs, 0), MI(r, cs, 16), MI(r, cs, 32), MI(r, cs, 40))
+        event(A("EO", sl, S(0, 16)), cs, GO(r, 2, cs, 16), MI(r, cs, 16, 16), MI(r, cs, 48, 16))
         send(A("EO", sl, S(0, 16)), A("E1", sl, S(0, 16)), "a%d" % (2 * r + cs[-1]), -1, 1)
 
     ts(W_("vw"), W_("vi"), 1023, ALU.bitwise_and); cp(C("l0", 0, 16), W_("vw"))
@@ -357,7 +398,7 @@ def build_ops(K, O):
         h1, h2 = hp2(), hp2()
         ts(H(h1), C("msc", 0, 16), -OFF, AD, BIG2, AD); act(H(h2), H(h1), bias=-BIG2)
         U = A("U", S(2 * r, 2 * r + 2), S(0, 8))
-        tt(U, C("msc", 0, 16), H(h2), SU); act(M(r, 1, b2, 48), U, bias=-1.0)
+        tt(U, C("msc", 0, 16), H(h2), SU); act(M(r, 0, b2, 56), U, bias=-1.0); act(M(r, 1, b2, 56), U, bias=-1.0)
         station(r, 0, 0); station(r, 0, 1)
         for bk, n in (("ex0", 512), ("ex1", 512), ("pen", 128)):
             mm(C(bk, 0, n), C("one", 128, 128), C("Rr", 0, n), True, False)
@@ -372,14 +413,15 @@ def build_ops(K, O):
         if last: dma("Y", W_("yz"), C("XA", 2048, 256), 65536)
         if not O["e0"]: local_event(r, 0, (0,))
         station(r, 1, 1)
+        twice("OWB%d" % r)
         local_event(r, 0, b2 if O["e0"] else (1,))
         station(r, 2, 0)
         if not O["e1"]: back_event(r, (0,))
         station(r, 2, 1)
         back_event(r, b2 if O["e1"] else (1,))
-        diff(r, 2, b2)
+        low(MI(r, b2, 8), MI(r, b2, 16), b2); diff(r, 2, b2); act(M(r, 2, b2, 56), MI(r, b2, 56))
         if not last:
-            h1 = hp2(); tt(H(h1), GO(r, 0, b2), GO(r, 1, b2), SU); tt(A("MO", r * 8 + 6, S(24, 40)), H(h1), GO(r, 2, b2), AD)
+            h1 = hp2(); tt(H(h1), GO(r, 0, b2), GO(r, 1, b2), SU); tt(A("MO", r * 8 + 6, S(32, 48)), H(h1), GO(r, 2, b2), AD)
         station(r, 3, 0)
         if not O["e1"]: far_hist(r, 1, (0,))
         local_event(r, 2, (0,))
@@ -388,31 +430,31 @@ def build_ops(K, O):
         local_event(r, 2, (1,))
         far_hist(r, 3, (0,))
         if not last:
-            for k, (sg, x) in enumerate(((1, GO(r, 0, b2)), (0, MI(r, b2, 16)), (1, GO(r, 2, b2)), (0, A("E3", 2 * r, S(16, 32))))):
+            for k, (sg, x) in enumerate(((1, GO(r, 0, b2)), (0, MI(r, b2, 24)), (1, GO(r, 2, b2)), (0, A("E3", 2 * r, S(16, 32))))):
                 mm(C("msc", 0, 16), C("oneF", 128 * sg, 128), x, k == 0, k == 3)
-            tt(C("cn", 0, 16), C("msc", 0, 16), W_("BM"), MU)
-            add("V", "red", [C("cn", 16, 1), C("cn", 0, 16), AxisListType.X, AD], [C("cn", 16, 1)], [C("cn", 0, 16)], 100)
+            tt(C("cn", 0, 16), C("msc", 0, 16), W_("BM"), MU); red(C("cn", 16, 1), C("cn", 0, 16))
             ts(C("cn", 17, 1), C("cn", 16, 1), -1.5, AD, BIG4, AD)
             ts(C("cn", 18, 1), C("cn", 17, 1), BIG4, SU, -28.5, AD)
             ts(C("cn", 19, 1), C("cn", 16, 1), C("cn", 18, 1), SU, 1 / 32.0, MU)
-            sc = C("OWA", 1024, 1)
+            sc = C("OWA", 0, 1)
             add("V", "rcp", [sc, C("cn", 19, 1)], [sc], [C("cn", 19, 1)], 250)
-            ts(C("sI", 256, 128), W_("Ib"), sc, MU); ts(C("sI", 384, 128), W_("Ib"), sc, MU, -1.0, MU)
-        for h in range(2): mm(W_("d%d" % h), W_("If"), C("OWA", 512 * h, 512), True, False)["up"] = O["pre"]
-        cp(C("exs", 0, 512), W_("ex0")); act(C("exs", 512, 512), W_("ex1"))
+            scales(sc, 256)
+        for h in range(2): mm(W_("d%d" % h), W_("If"), C("OWA", 8 + 512 * h, 512), True, False)["up"] = O["pre"]
+        for h in range(2): flex(lambda: act(C("exs", 512 * h, 512), W_("ex%d" % h)), lambda: cp(C("exs", 512 * h, 512), W_("ex%d" % h)), O["pe"])
         for x in range(8): mm(C("d%d" % (x // 4), 128 * (x % 4), 128), A("exs", S(x, 1024, 8)), W_("Dm"), False, x % 4 == 3)
         for h in range(2):
-            d = W_("d%d" % h); ow = C("OWA", 512 * h, 512)
-            ts(C("Rm", 512 * h, 512), d, BIG2, AD, BIG2, SU); tt(ow, d, C("Rm", 512 * h, 512), SU)
+            d = W_("d%d" % h); rm = C("Rm", 512 * h, 512)
+            if h < O["rs2"]: act(rm, d, bias=BIG2); act(rm, rm, bias=-BIG2)
+            else: ts(rm, d, BIG2, AD, BIG2, SU)
+            tt(C("OWA", 8 + 512 * h, 512), d, rm, SU)
         if last:
-            act(C("exs", 0, 512), C("OWA", 512, 512), bias=OFF * 2049, scale=2048.0)
+            act(W_("d1"), C("OWA", 520, 512), bias=OFF * 2049, scale=2048.0)
             for h in range(2):
-                tt(C("ynb", 256 * h, 256), C("exs", 256 * h, 256), C("OWA", 256 * h, 256), AD)
+                tt(C("ynb", 256 * h, 256), C("d1", 256 * h, 256), C("OWA", 8 + 256 * h, 256), AD)
                 dma("Y", C("yn", 256 * h, 256), C("ynb", 256 * h, 256), 131072)
         else:
             copies(r + 1, "o")
-            sc = C("OWB%d" % (r + 1), 1024, 1)
-            ts(C("sI", 512, 128), W_("Ib"), sc, MU); ts(C("sI", 640, 128), W_("Ib"), sc, MU, -1.0, MU)
+            scales(C("OWB%d" % (r + 1), 0, 1), 512)
         h1, h2 = hp2(), hp2()
         tt(H(h1), A("FI", S(2 * r, 2 * r + 2), S(0, 8)), H(alt), SU); tt(H(h2), H(h1), GO(r, 0, b2), MU); tt(both("VV", r + 1), H(h2), H(alt), AD)
         if last:
@@ -421,17 +463,17 @@ def build_ops(K, O):
             low(both("WW", r + 1), both("VV", r + 1), b2)
             ts(C("l0", 16 * (r + 1), 16), turn(A("WW", r + 1, S(0, 24)), 1), 1024.0, AD)
         far_hist(r, 3, (1,))
-        act(W_("hit"), C("pen", 0, 128))
-        mm(C("pen", 128, 128), W_("hit"), W_("Dh")); ts(W_("hitT"), C("pen", 128, 128), 0.5, GT)
+        flex(lambda: act(W_("hit"), C("pen", 0, 128)), lambda: cp(W_("hit"), C("pen", 0, 128)))
+        mm(C("pen", 128, 128), W_("hit"), W_("Dh"))
+        flex(lambda: act(W_("hitT"), C("pen", 128, 128), fn=ACT.Sign), lambda: ts(W_("hitT"), C("pen", 128, 128), 0.5, GT))
         banks = ("key", "d2", "ex0", "ex1")
         for q, bk in enumerate(banks): mm(W_(bk), W_("Ib"), C("XA", 512 * q, 512), True, False)
         for q, bk in enumerate(banks):
             xb = C("XA", 512 * q, 512)
             for i in range(4): mm(C(bk, 128 * i, 128), C("Sel", 128 * (4 * q + i), 128), W_("hitT"), False, i == 3)
-            if q in O["xv"]: ts(xb, W_(bk), 0.0, MX)
-            else: act(xb, W_(bk), fn=ACT.Relu)
+            flex(lambda: act(xb, W_(bk), fn=ACT.Relu), lambda: ts(xb, W_(bk), 0.0, MX))
             if last: dma("Y", C("yx", 512 * q, 512), xb, 131072)
-        if not last: copies(r + 1, "x")
+        if not last: copies(r + 1, "x"); twice("OWA")
         cnt["d"] = 0
     return ops
 
@@ -445,9 +487,10 @@ def plan_order(K=COST, O=OPT, WIN=150, FILL=60):
     ops = build_ops(K, O); acc = {}; SYNC = K["SYNC"]
     for op in ops:
         deps = {}
-        e = op["e"]; eng = e if "sem" not in op else None
+        e = op["e"]; eng = e if "sem" not in op and "alt" not in op else None
         for p in op.get("after", []): deps[p] = "msg"
         if op.get("behind") is not None: deps[op["behind"]] = "order"
+        if "left" in op: deps[op["left"]] = "sem"
         uses = [(a, False) for a in op["r"]] + [(a, True) for a in op["w"]]
         for a, wr in uses:
             for (p, pa, pwr, pe) in acc.get(a["n"], []):
@@ -475,20 +518,30 @@ def plan_order(K=COST, O=OPT, WIN=150, FILL=60):
     sq = [op["seq"] for op in ops]
     for op in reversed(ops):
         for p in op["deps"]: sq[p] = min(sq[p], sq[op["id"]])
-    for i in range(n): lev[i] += ops[i].get("up", 0) - 1e6 * sq[i]
+    for i in range(n): lev[i] += ops[i].get("up", 0) - O["w"] * sq[i]
     left = [len(op["deps"]) for op in ops]; rt = [0.0] * n; st = [0.0] * n; fin = [0.0] * n
-    free = {}; order = []
-    pool = {}
+    free = {}; order = []; pool = {}
+
+    def enter(i):
+        pool.setdefault(ops[i]["e"], []).append(i)
+        if "alt" in ops[i]: pool.setdefault(ops[i]["alt"]["e"], []).append(i)
+
     for i in range(n):
-        if left[i] == 0: pool.setdefault(ops[i]["e"], []).append(i)
+        if left[i] == 0: enter(i)
     while any(pool.values()):
-        tmin = {e: max(min(rt[i] for i in l), free.get(e, 0.0) if e else 0.0) for e, l in pool.items() if l}
+        late = lambda i, e: rt[i] + (ops[i].get("pen", 0.0) if ops[i]["e"] != e else 0.0)
+        tmin = {e: max(min(late(i, e) for i in l), free.get(e, 0.0) if e else 0.0) for e, l in pool.items() if l}
         e0 = min(tmin, key=lambda k: tmin[k]); t0 = tmin[e0]
-        best = max((i for i in pool[e0] if rt[i] <= t0 + WIN), key=lambda i: lev[i])
+        busy = lambda i: ops[i]["busy"] if ops[i]["e"] == e0 else ops[i]["alt"]["busy"]
+        best = max((i for i in pool[e0] if late(i, e0) <= t0 + WIN), key=lambda i: lev[i])
         if e0 and rt[best] > t0:
-            fill = [i for i in pool[e0] if max(rt[i], t0) + ops[i]["busy"] <= rt[best] + FILL]
+            fill = [i for i in pool[e0] if max(late(i, e0), t0) + busy(i) <= rt[best] + FILL]
             if fill: best = max(fill, key=lambda i: lev[i])
-        i = best; pool[e0].remove(i); op = ops[i]
+        i = best; op = ops[i]
+        pool[op["e"]].remove(i)
+        if "alt" in op:
+            pool[op["alt"]["e"]].remove(i)
+            if op["e"] != e0: op.update(op["alt"]); op["swapped"] = True
         st[i] = max(rt[i], free.get(e0, 0.0)) if e0 else rt[i]
         if e0: free[e0] = st[i] + op["busy"]
         fin[i] = st[i] + op["busy"] + op["lat"]; order.append(i)
@@ -496,7 +549,7 @@ def plan_order(K=COST, O=OPT, WIN=150, FILL=60):
             k = ops[s]["deps"][i]
             rt[s] = max(rt[s], st[i] if k == "order" else fin[i] + (SYNC if k == "sem" else 0))
             left[s] -= 1
-            if left[s] == 0: pool.setdefault(ops[s]["e"], []).append(s)
+            if left[s] == 0: enter(s)
     cntq = {}
     for i in order:
         op = ops[i]
@@ -529,7 +582,7 @@ PLAN = {}
 
 def view(T, a):
     if not isinstance(a, dict): return a
-    v = T[a["n"]][(slice(None),) + tuple(a["i"])]
+    v = T[a["n"]][(slice(*a.get("p", (None,))),) + tuple(a["i"])]
     if a["ind"] is not None: v = v.indirect(view(T, a["ind"]))
     return v
 

import numpy as np
from concourse.bass import DstId, RemoteDMATransfer
from concourse.mybir import AluOpType, AxisListType, ActivationFunctionType

ALU, ACT = AluOpType, ActivationFunctionType
NR, NS = 2, 4
BIGN, BIG2, BIG3, BIG4, BIG0, BIGP = 1.5 * 2.0 ** 29, 1.5 * 2.0 ** 34, 1.5 * 2.0 ** 30, 1.5 * 2.0 ** 25, 1.5 * 2.0 ** 23, 1.5 * 2.0 ** 35
OFF, PO = 1023.5, 1087.5
KS, DEAD = 2.0 ** 17, 2.0 ** 34
NOH = 16
OWN = 1032
F32, BF, F16, I32, U16 = "float32", "bfloat16", "float16", "int32", "uint16"


def _sb(shape, dt):
    return ("sbuf", [128] + list(shape), dt)


SCRATCH = {
    "XA": _sb([2304], BF), "XB0": _sb([2304], BF), "XB1": _sb([2304], BF),
    "OWA": _sb([2312], F32), "OWB0": _sb([2312], F32), "OWB1": _sb([2312], F32),
    "nbi": _sb([512], I32), "nbB": _sb([512], I32), "vi": _sb([16], I32), "vw": _sb([16], I32),
    "Xg": _sb([4096], BF), "near": _sb([4096], BF), "Pu": _sb([256], U16), "Pf": _sb([256], F16), "zT": _sb([256], F16),
    "zl": _sb([12 * 128], BF), "zin": _sb([4 * 128], BF), "LS": _sb([12 * 16], U16), "lin": _sb([32], U16), "l0": _sb([32], U16),
    "MO": _sb([16, 64], F32), "MI": _sb([4, 64], F32), "EO": _sb([4, 16], F32), "E1": _sb([4, 16], F32), "E3": _sb([4, 32], F32),
    "FI": _sb([4, 8], F32), "Mx": _sb([272], F32), "Dq": _sb([272], F32), "Qs": _sb([272], F32), "r2": _sb([16, 8], F32),
    "VV": _sb([4, 24], F32), "WW": _sb([2, 24], F32), "bt": _sb([4 * 128], F16), "U": _sb([4, 8], F32),
    "hp": _sb([512, 8], F32), "hq": _sb([32, 16], F32), "OA": _sb([NOH * 128], BF), "OB": _sb([NOH * 144], F16),
    "exs": _sb([1024], F32), "Rm": _sb([1024], F32), "hit": _sb([128], F16), "hitT": _sb([128], BF),
    "zt": _sb([256], F32), "cn": _sb([32], F32), "ynb": _sb([512], F32), "yvb": _sb([16], F32),
    "iJ": _sb([240], F32), "pi": _sb([4], I32), "pf": _sb([24], F32), "it": _sb([152], F32), "ct": _sb([272], F32),
    "Ib": _sb([128], BF), "If": _sb([128], F32), "nBig": _sb([128], F32), "hI": _sb([128], BF),
    "sI": _sb([6 * 128], BF), "BTs": _sb([240], F16), "Perm": _sb([136], F16), "m8": _sb([8], F32), "M16": _sb([16], F32),
    "seg": _sb([136], BF), "cm": _sb([408], BF), "BM": _sb([16], F32),
    "BL": _sb([8], U16), "BP": _sb([4], U16), "BR": _sb([8], U16), "B8": _sb([2], U16),
    "Sel": _sb([2048], BF), "Rr": _sb([2048], BF), "pw": _sb([64], F32), "W": _sb([8], BF), "Wu": _sb([8], BF), "cI0": _sb([16], F32),
    "one": _sb([256], BF), "oneF": _sb([256], F32), "iA": _sb([128], BF), "nA": _sb([128], BF), "iC": _sb([128], BF),
    "Dt": _sb([128], F32), "Dm": _sb([128], F32), "Dh": _sb([128], BF), "iB": _sb([144], BF),
    "d0": ("psum", [128, 512], F32), "d1": ("psum", [128, 512], F32), "d2": ("psum", [128, 512], F32),
    "key": ("psum", [128, 512], F32), "msc": ("psum", [128, 512], F32),
    "ex0": ("psum", [128, 512], F32), "ex1": ("psum", [128, 512], F32), "pen": ("psum", [128, 512], F32),
}
NDMA = 20
SEMAPHORES = (["cV", "cS", "cP", "cG", "sent"] + ["dm%d" % i for i in range(NDMA)]
              + ["%s%d" % (k, j) for k in "zlmabf" for j in range(4)]
              + ["%s%d" % (k, j) for k in ("bo", "bx", "so", "sx", "sy") for j in range(2)])
IO = {"tracks": [128, 2048], "nb": [128, 512], "v": [128, 16], "z": [128, 256],
      "yx": [128, 2048], "yn": [128, 512], "yv": [128, 16], "yz": [128, 256]}

COST = {"CY": 0.87, "PCY": 0.42, "GA": 1.56, "SYNC": 90.0, "RELAY": 4200.0, "DIRECT": 2200.0, "ISSUE": 900.0, "FIXV": 50.0, "FIXP": 15.0,
        "BULK": 6500.0, "FIRST": 3000.0}
OPT = {"vg": [257, 1793, 1, 1, 1, 1, 1, 1],
       "nsc": [1, 1, 1, 1, 1, 1, 1, 1],
       "e0": 1, "e1": 0, "pre": 20000, "blk": 0, "pv": 1, "pp": 0, "pu": 0, "bv": 0, "tp": 0, "w": 2000, "pr": 500, "rs2": 1, "pa": 0, "pe": 0}
BLK = ([256, 512, 512, 512, 256], [512, 512, 512, 512], [512, 512, 512, 256, 256])


def A(name, *idx):
    shape = (SCRATCH[name][1] if name in SCRATCH else IO[name])[1:]
    cols = np.arange(int(np.prod(shape))).reshape(shape)[idx]
    psum = name in SCRATCH and SCRATCH[name][0] == "psum"
    dt = SCRATCH[name][2] if name in SCRATCH else None
    return {"n": name, "i": idx, "lo": int(np.min(cols)), "hi": int(np.max(cols)) + 1, "k": int(np.size(cols)), "ps": psum, "dt": dt,
            "ind": None, "set": frozenset(np.ravel(cols).tolist()) if len(shape) > 1 else None}


def S(a, b, c=None):
    return slice(a, b, c)


def C(name, a, n):
    return A(name, S(a, a + n))


def IND(win, off):
    d = dict(win); d["ind"] = off; d["k"] = off["k"] * 16
    return d


def build_ops(K, O):
    ops = []; seq = [99]
    CY, PCY, GA, FIXV, FIXP = K["CY"], K["PCY"], K["GA"], K["FIXV"], K["FIXP"]

    def add(e, call, args, w, r, busy, lat=0.0, kw=None, **x):
        rr = []
        for a in r:
            if isinstance(a, dict):
                rr.append(a)
                if a["ind"] is not None: rr.append(a["ind"])
        op = {"e": e, "call": call, "args": args, "kw": kw or {}, "w": w, "r": rr, "busy": busy, "lat": lat, "id": len(ops), "seq": seq[0]}
        op.update(x); ops.append(op)
        return op

    def two(*a):
        return all(x["dt"] in (BF, F16, U16) for x in a)

    def vcost(out, in0, per):
        if in0["ind"] is not None: return 50 + in0["k"] * GA * CY
        return FIXV + max(64, out["k"] * per) * CY

    def ts(out, in0, s1, op0, s2=None, op1=None):
        args = [out, in0, s1, s2, op0] + ([op1] if op1 is not None else [])
        return add("V", "ts", args, [out], [in0, s1, s2], vcost(out, in0, 0.5 if two(out, in0) else 1))

    def tt(out, a, b, op):
        return add("V", "tt", [out, a, b, op], [out], [a, b], vcost(out, a, 1 if a["ps"] or b["ps"] else 2))

    def cp(out, a):
        return add("V", "cp", [out, a], [out], [a], vcost(out, a, 0.5 if two(out, a) else 1))

    def scan(out, d0, d1, init, op0, op1):
        return add("V", "scan", [out, d0, d1, init, op0, op1], [out], [d0, d1], vcost(out, d0, 1))

    def ms(out, val):
        return add("V", "ms", [out, val], [out], [], FIXV + max(64, out["k"] * (0.5 if two(out) else 1)) * CY)

    def red(out, a):
        return add("V", "red", [out, a, AxisListType.X, ALU.add], [out], [a], FIXV + 64 * CY)

    def act(out, a, bias=None, scale=None, fn=None):
        kw = {}
        if bias is not None: kw["bias"] = bias
        if scale is not None: kw["scale"] = scale
        c = 65 + a["k"] * GA * CY if a["ind"] is not None else 65 + max(64, a["k"]) * CY
        return add("S", "act", [out, a, fn if fn is not None else ACT.Identity if kw else ACT.Copy], [out], [a, bias, scale], c, kw=kw)

    def mm(out, l, r, start=True, stop=True):
        return add("P", "mm", [out, l, r, start, stop], [out], [l, r], FIXP + max(64, r["k"]) * PCY * (4 if l["dt"] == F32 else 1), lat=60)

    def sel(out, a, pat, op, fill, base):
        return add("G", "sel", [out, a, pat, op, fill, base, 1], [out], [a], 170 + 2 * out["k"] * CY)

    def iota(out, pat, base, cm):
        kw = {} if out["dt"] == I32 else {"allow_small_or_imprecise_dtypes": True}
        return add("G", "iota", [out, pat, base, cm], [out], [], 130 + 2 * out["k"] * CY, kw=kw)

    def flex(first, second, pen=0.0):
        a = first(); b = second(); ops.pop()
        a["alt"] = {k: b[k] for k in ("e", "call", "args", "kw", "busy")}; a["r"] = a["r"] + b["r"]; a["pen"] = pen
        return a

    nd = [0]; prev = [None]

    def dma(q, out, a, nbytes):
        nd[0] += 1
        return add(q, "dma", [out, a], [out], [a], 80, lat=1800 + nbytes / 150.0, sem="dm%d" % (nd[0] - 1), cnt=16)

    def send(src, dst, sem, dist, via=None):
        o = add("G", "send", [src], [], [src], K["ISSUE"], pieces=[(via, src, dst)], rsem=sem, dist=dist, behind=prev[0])
        prev[0] = o["id"]
        add(None, "arrive", [], [dst], [], 0, lat=K["DIRECT" if via is None else "RELAY"] + src["k"] * 3, after=[o["id"]], sem=sem)

    def bulk(src, dst, a, n, vias, sem, loc):
        m = n // len(vias)
        o = add("G", "send", [C(src, a, n)], [], [C(src, a, n)], K["ISSUE"], lat=2500, rsem=sem, dist=-1, sem=loc, behind=prev[0], up=1e7,
                pieces=[(h, C(src, a + m * k, m), C(dst, a + m * k, m)) for k, h in enumerate(vias)])
        prev[0] = o["id"]
        return o["id"]

    def landed(dst, n, sem, after, more=0.0):
        add(None, "arrive", [], [C(dst, 0, n)], [], 0, lat=K["BULK"] - 2500 + more, after=after, sem=sem)

    E, GE, GT, LT, NE = ALU.is_equal, ALU.is_ge, ALU.is_gt, ALU.is_lt, ALU.not_equal
    AD, SU, MU, MX, MN = ALU.add, ALU.subtract, ALU.mult, ALU.max, ALU.min
    W_ = lambda n: A(n, *[S(None, None)] * (len((SCRATCH[n][1] if n in SCRATCH else IO[n])) - 1))

    dma("Y", C("nbi", 0, 256), C("nb", 0, 256), 131072)
    dma("S", C("nbi", 256, 256), C("nb", 256, 256), 262144)
    dma("Y", W_("vi"), W_("v"), 8192)
    dma("S", C("XA", 2048, 256), W_("z"), 65536)
    dma("Y", C("XA", 0, 1024), C("tracks", 0, 1024), 500000)
    dma("S", C("XA", 1024, 1024), C("tracks", 1024, 1024), 600000)
    iota(C("pi", 0, 1), [[0, 1]], 0, 1)
    iota(W_("iJ"), [[1, 240]], 0, 0)
    iota(C("it", 0, 16), [[0, 2], [1, 8]], 0, 0)
    iota(C("it", 16, 136), [[0, 8], [1, 17]], 1, 0)
    iota(W_("cI0"), [[128, 2], [0, 8]], 960, 1)
    iota(C("iB", 0, 16), [[128, 16]], -1024, 0)
    iota(C("iB", 16, 128), [[-1024, 16], [128, 8]], 16384, 0)
    iota(W_("iC"), [[0, 8], [128, 16]], -1024, 0)
    iota(W_("iA"), [[1, 128]], -64, 0); iota(W_("nA"), [[-1, 128]], 64, 0)
    ts(C("pi", 1, 1), C("pi", 0, 1), 15, ALU.bitwise_and)
    ts(C("pi", 2, 1), C("pi", 0, 1), 4, ALU.logical_shift_right)
    ts(C("pi", 3, 1), C("pi", 0, 1), 7, ALU.bitwise_and)
    cp(C("pf", 0, 4), C("pi", 0, 4))
    pf = lambda j: C("pf", j, 1)
    pc, pm, pd, p8 = pf(0), pf(1), pf(2), pf(3)
    J = lambda n: C("iJ", 0, n)
    ts(W_("Ib"), J(128), pc, E)
    ts(C("sI", 0, 128), W_("Ib"), 32 / 28.5, MU); ts(C("sI", 128, 128), W_("Ib"), -32 / 28.5, MU)
    zb, zf = C("one", 128, 128), W_("Dt")
    iota(zb, [[0, 128]], 0, 0); iota(zf, [[0, 128]], 0, 0)
    for n, z, val in (("If", zf, 1.0), ("nBig", zf, -DEAD), ("hI", zb, 0.5), ("Dm", zf, 1.0), ("Dh", zb, 1.0)): sel(W_(n), z, [[-1, 128]], NE, val, 0)
    for n in ("Dm", "Dh"): sel(W_(n), W_(n), [[-1, 128]], NE, -1.0, -1)
    ts(pf(4), pd, 17.0, MU, 15.0, AD); tt(pf(5), pf(4), pm, SU); ts(W_("Perm"), J(136), pf(5), E)
    ts(W_("BTs"), J(240), -112.0, AD, pm, E)
    ts(W_("m8"), J(8), pd, E); ts(W_("M16"), J(16), pm, E)
    pos = C("it", 16, 136)
    act(W_("seg"), pos, bias=-384.0, scale=256.0, fn=ACT.Sigmoid)["busy"] += 1300
    ts(C("cm", 0, 136), pos, 17.0, E, 34816.0 * KS / 128, MU); ts(C("cm", 272, 136), pos, 17.0, E, DEAD / 128, MU)
    ts(pf(6), pc, 0.0, E, 4096.0, MU); ts(pf(7), pc, 1.0, E, -1088.0, MU); ts(pf(8), pc, 2.0, E, 0.5, MU); tt(pf(9), pf(7), pf(8), AD)
    ts(C("ct", 0, 136), pos, 16.5, LT, pf(9), MU); ts(C("ct", 136, 136), pos, -18.0, AD, pf(6), MU)
    tt(C("cm", 136, 136), C("ct", 0, 136), C("ct", 136, 136), AD)
    ts(W_("cI0"), W_("cI0"), 0.5, AD)
    ts(W_("BM"), C("it", 0, 16), pd, E)
    tt(pf(10), p8, pd, E); ts(pf(11), pm, 8.0, GE, 8.0, MU); ts(pf(12), pf(11), 8.0, AD); ts(W_("BL"), J(8), pf(12), AD, pf(10), MU)
    ts(pf(15), pm, 8.0, GE, 16.0, AD); ts(C("pf", 16, 4), J(4), 2.0, MU, pf(15), AD); ts(W_("BP"), C("pf", 16, 4), pf(10), MU)
    ms(C("pw", 0, 16), 0.5); ms(C("pw", 16, 16), 0.0)
    scan(C("pw", 32, 16), C("pw", 0, 16), C("pw", 16, 16), 65536.0 * KS, MU, AD)
    tt(C("pw", 48, 16), C("pw", 32, 16), W_("M16"), MU); red(pf(13), C("pw", 48, 16))
    ts(pf(14), pm, 2.0, MU, 1.0, AD)
    ts(W_("W"), W_("m8"), pf(13), MU); ts(W_("Wu"), W_("m8"), pf(14), MU)
    iota(C("one", 0, 128), [[0, 128]], 1, 0); iota(W_("oneF"), [[-2, 2], [0, 128]], 1, 0)
    cp(W_("BR"), J(8)); cp(C("B8", 0, 1), p8)
    for k in range(16): flex(lambda: act(A("Rr", S(k, 2048, 16)), W_("Ib")), lambda: cp(A("Rr", S(k, 2048, 16)), W_("Ib")), O["pr"])
    ms(A("MO", S(0, 16), S(0, 16)), -63.5); ms(A("VV", S(0, 4), S(0, 8)), -63.5); ms(A("WW", S(0, 2), S(0, 8)), -63.5)
    iota(C("OWA", 0, 8), [[0, 8]], 1, 0); iota(C("OWA", 2056, 256), [[0, 256]], -1023, 0)
    for r in range(NR):
        for a in (OWN, 2056): iota(C("OWB%d" % r, a, 256), [[0, 256]], -1023, 0)
        iota(C("XB%d" % r, 2048, 256), [[0, 256]], 0, 0)

    def unpack(src, dst, bank, n):
        for a in range(0, 512, n):
            y, R = C(bank, a, n), C("Rm", a, n)
            ts(y, C(src, a, n), -OFF, AD); ts(R, y, BIG2, AD, BIG2, SU)
            tt(C(dst, 8 + a, n), y, R, SU)
            act(C(dst, 520 + a, n), R, bias=-OFF, scale=1 / 2048.0)

    def twice(n):
        o = dma("Y", C(n, OWN, 1024), C(n, 8, 1024), 524288)
        if n == "OWA": o["left"] = prev[0]

    def copies(r, what):
        seq[0] = 8 * r + 2
        if what == "o" and r == 0:
            landed("nbB", 512, "bo0", [bulk("nbi", "nbB", 0, 512, [0, 2, 1, 3], "bo0", "so0")], K["FIRST"] - 1500)
            unpack("nbB", "OWB0", "pen", 512)
        elif what == "o": landed("OWB%d" % r, OWN, "bo%d" % r, [bulk("OWA", "OWB%d" % r, 0, OWN, [0, 2, 1, 3], "bo%d" % r, "so%d" % r)])
        else: landed("XB%d" % r, 2048, "bx%d" % r, [bulk("XA", "XB%d" % r, 0, 1024, [0, 2], "bx%d" % r, "sx%d" % r),
                                                      bulk("XA", "XB%d" % r, 1024, 1024, [1, 3], "bx%d" % r, "sy%d" % r)])
        seq[0] = 99

    unpack("nbi", "OWA", "d0", 256)
    copies(0, "o"); copies(0, "x"); twice("OWA")
    iota(W_("Sel"), [[0, 2048]], -33, 0)["behind"] = prev[0]
    sel(W_("Sel"), W_("Sel"), [[-1, 16], [-16, 8], [0, 16]], E, 0.0, 0)

    cnt = {"d": 0, "bt": 0, "oh": 0, "hp": 0, "hq": 0}

    def nxt(k, m, step=1):
        v = cnt[k]; cnt[k] = (v + step) % m
        return v

    def hp2():
        return nxt("hp", 512, 2)

    def H(h, cs=(0, 1)):
        return A("hp", S(h + cs[0], h + cs[-1] + 1), S(0, 8))

    KEY = ("key", "msc")

    def turn(win, c, lst="BL", n=16):
        b = nxt("bt", 4)
        x, y = C("bt", 128 * b, 8 * n), IND(win, W_(lst))
        if O["bv"]: flex(lambda: act(x, y, bias=63.5), lambda: ts(x, y, 63.5, AD))
        else: act(x, y, bias=63.5)
        for gi in range(8):
            mm(C(KEY[c], 272, n), C("BTs", 112 - 16 * gi, 128), C("bt", 128 * b + n * gi, n), gi == 0, gi == 7)
        return C(KEY[c], 272, n)

    def low(out, v, cs):
        h = hp2(); ts(H(h, cs), v, 1024.0 - PO, GE, -1024.0, MU); tt(out, v, H(h, cs), AD)

    M = lambda r, s, cs, a, n=8: A("MO", S(r * 8 + s * 2 + cs[0], r * 8 + s * 2 + cs[-1] + 1), S(a, a + n))
    MI = lambda r, cs, a, n=8: A("MI", S(r * 2 + cs[0], r * 2 + cs[-1] + 1), S(a, a + n))
    R2 = lambda r, s, cs: A("r2", S(r * 8 + s * 2 + cs[0], r * 8 + s * 2 + cs[-1] + 1), S(0, 8))
    GO = lambda r, s, cs, n=8: M(r, s, cs, 48 if s == 3 else 24, n)
    b2 = (0, 1)

    def both(n, j, cs=b2):
        return A(n, j, S(8 + 8 * cs[0], 16 + 8 * cs[-1]))

    def station(r, s, c):
        jo = r * 8 + s * 2 + c; j = r * 6 + s * 2 + c; seq[0] = jo; cs = (c,)
        tb = "B%d" % r if s % 2 else "A"; si = 2 * (1 + s % 2) if r else 0
        L = C("l0", 16 * r + 8 * c, 8) if s == 0 else C("lin", 8 * (2 * r + c), 8) if s == 2 else C("LS", 16 * (j - 2) + (8 if s == 3 else 0), 8)
        Z = C("XA", 2048 + 128 * c, 128) if s == 0 else C("zin", 128 * (2 * r + c), 128) if s == 2 else C("zl", 128 * (j - 2), 128)
        Pf, Pu = C("Pf", 128 * c, 128), C("Pu", 128 * c, 128)
        ow = IND(C("OW" + tb, 8, (1024, 1280, 2304, 2304)[s]), L)
        if O["pv"]: ts(Pu, ow, OFF, AD); flex(lambda: act(Pf, ow, bias=OFF), lambda: cp(Pf, Pu), O["pp"])["up"] = -O["pu"]
        else: act(Pf, ow, bias=OFF); cp(Pu, Pf)
        d = "d%d" % nxt("d", 3)
        mm(C(d, 0, 128), Z, C("sI", 128 * si + 128, 128)); act(C("zT", 128 * c, 128), C(d, 0, 128))
        b = 0; vg = O["vg"][2 * s + c]
        for n in BLK[O["blk"]]:
            o = 2048 * c + b
            (cp if vg == b + 1 else act)(C("Xg", o, n), IND(C("X" + tb, 0, 2048), C("Pu", o // 16, n // 16)))
            d = C("d%d" % nxt("d", 3), 0, n)
            mm(d, C("zT", 128 * c, 128), C("Rr", b, n), True, False)
            mm(d, C("sI", 128 * si, 128), C("Xg", o, n), False, True)
            ts(C("near", o, n), d, BIGN, AD, BIGN, E)
            b += n
        key = KEY[c]; ko = 136 if s else 0; po = 136 - ko; o = 136 * c
        kk, mk, pay = C(key, ko, 136), A(key, S(ko + 16, ko + 136, 17)), C(key, po, 136)
        Mx = A("Mx", S(o + 16, o + 136, 17))
        mm(C(key, 0, 272), C("one", 0, 128), C("cm", ko, 272), True, False)
        mm(pay, Pf, W_("Perm"), False, False)
        mm(A(key, S(po + 16, po + 136, 17)), W_("If"), C("cI0", 8 * c, 8) if s == 0 else MI(r, cs, 16) if s == 2 else M(r, s - 1, cs, 16), False, False)
        if s:
            mm(mk, W_("If"), MI(r, cs, 40) if s == 2 else Mx, False, False)
            mm(mk, W_("nBig"), MI(r, cs, 24) if s == 2 else GO(r, s - 1, cs), False, False)
        for p0, p1 in ((0, 96), (96, 128)) if O["tp"] else ((0, 128),):
            for k in range(16):
                out = dict(A(key, S(ko + 15 - k, ko + 136, 17)), p=(p0, p1))
                x = mm(out, A("near", S(2048 * c + 16 * p0 + k, 2048 * c + 16 * p1, 16)), W_("W"), False, k == 15 and p1 == 128)
                x["busy"] = FIXP + min(64, p1 - p0) * PCY
        scan(C("Mx", o, 136), W_("seg"), kk, 0.0, MU, MX)
        tt(C("Dq", o, 136), kk, C("Mx", o, 136), SU)
        scan(C("Qs", o, 136), C("Dq", o, 136), pay, 0.0, MX, MN)
        Q, P = A("Qs", S(o + 16, o + 136, 17)), M(r, s, cs, 16)
        ts(R2(r, s, cs), Q, BIGP, AD, BIGP, SU); tt(P, Q, R2(r, s, cs), SU)
        go = lambda: act(A("MO", jo, S(48, 64) if s == 3 else S(24, 40)), IND(A("r2", jo, S(0, 8)), C("B8", 0, 1)), bias=-4096.0, scale=-1.0, fn=ACT.Sign)
        if s == 3:
            act(M(r, s, cs, 24), R2(r, s, cs), bias=8192.0, fn=ACT.Relu)
            n = 32 if c == 0 and r < NR - 1 else 16
            send(A("MO", jo, S(16, 16 + n)), A("E3", 2 * r + c, S(0, n)), "b%d" % (2 * r + c), 1, 0)
            send(A("MO", jo, S(16, 24)), A("FI", 2 * r + c, S(0, 8)), "f%d" % (2 * r + c), -2)
            go(); seq[0] = 99
            return
        if s == 0:
            low(M(r, s, cs, 8), P, cs)
            ts(C("LS", 16 * j, 16), turn(A("MO", jo, S(0, 24)), c), 1024.0, AD)
        else: ts(C("LS", 16 * j + 8, 8), turn(A("MO", jo, S(0, 24)), c, "BP", 8), 1024.0, AD)
        if s == 1: send(C("LS", 16 * j + 8, 8), C("lin", 8 * (2 * r + c), 8), "l%d" % (2 * r + c), 2)
        act(C("zl", 128 * j, 128), IND(W_("X" + tb), C("LS", 16 * j + 8, 8)))
        go()
        if s == 1:
            send(C("zl", 128 * j, 128), C("zin", 128 * (2 * r + c), 128), "z%d" % (2 * r + c), 2)
            act(M(r, s, cs, 40), Mx); diff(r, s, cs)
            send(A("MO", jo, S(16, 64)), A("MI", 2 * r + c, S(16, 64)), "m%d" % (2 * r + c), 2)
        seq[0] = 99

    def scales(sc, a):
        x, y = C("sI", a, 128), C("sI", a + 128, 128)
        flex(lambda: act(x, W_("Ib"), scale=sc), lambda: ts(x, W_("Ib"), sc, MU)); flex(lambda: act(y, x, scale=-1.0), lambda: ts(y, x, -1.0, MU))

    def diff(r, s, cs):
        w = both("WW", r, cs) if s == 0 else M(r, 0, cs, 8) if s == 1 else MI(r, cs, 8)
        e1, e2 = hp2(), hp2()
        act(H(e1, cs), R2(r, s, cs), bias=19456.0, scale=0.25); tt(H(e2, cs), w, M(r, s, cs, 16), SU)
        tt(M(r, s, cs, 48), H(e1, cs), H(e2, cs), AD)

    def event(out, cs, gon, pg, du):
        t = nxt("hq", 32, 2); t = A("hq", S(t + cs[0], t + cs[-1] + 1), S(0, 16))
        tt(t, gon, du, MU); tt(out, t, pg, AD)

    def local_event(r, s, cs):
        e = nxt("hq", 32, 2)
        event(A("hq", S(e + cs[0], e + cs[-1] + 1), S(0, 16)), cs, GO(r, s + 1, cs, 16), M(r, s, cs, 16, 16), M(r, s, cs, 48, 16))
        hist(s, cs, "hq", e)

    def hist(s, cs, n, j):
        code = A(n, S(j + cs[0], j + cs[-1] + 1), S(0, 8))
        bR, a, a2, bm = hp2(), hp2(), hp2(), hp2()
        ts(H(bR, cs), code, BIG3, AD, BIG3, SU)
        if any(O["nsc"][2 * s + c] for c in cs):
            tt(H(a, cs), code, H(bR, cs), SU); act(H(a2, cs), H(a, cs), scale=256.0)
        if s == 3: tt(H(bm, cs), H(bR, cs), A(n, S(j + cs[0], j + cs[-1] + 1), S(8, 16)), AD)
        for c in cs:
            if s == 3:
                o3 = nxt("oh", NOH); tt(C("OB", 144 * o3, 128), IND(A("hp", bm + c, S(0, 8)), W_("BR")), W_("iC"), E)
            for gi in range(8):
                o = nxt("oh", NOH); col = S(gi, gi + 1)
                oa, bc = C("OA", 128 * o, 128), A("hp", bR + c, col)
                on_v = lambda: ts(oa, W_("iA"), bc, AD, A(n, j + c, col), LT)
                if O["nsc"][2 * s + c]: flex(lambda: act(oa, W_("nA"), bias=A("hp", a2 + c, col), scale=256.0, fn=ACT.Sigmoid), on_v, O["pa"])
                else: on_v()
                if s < 3:
                    ts(C("OB", 144 * o, 144), W_("iB"), bc, E, A(n, j + c, S(8 + gi, 9 + gi)), MU)
                    mm(C("ex%d" % (gi // 4), 128 * (gi % 4), 128), oa, C("OB", 144 * o + 16, 128), False, (s, c, gi % 4) == (2, 1, 3))
                mm(C("pen", 16 * gi, 16), oa, C("OB", 144 * o3 + 16 * gi if s == 3 else 144 * o, 16), False, (s, c, gi) == (3, 1, 7))

    def far_hist(r, s, cs):
        hist(s, cs, "E1" if s == 1 else "E3", 2 * r)

    def back_event(r, cs):
        sl = S(2 * r + cs[0], 2 * r + cs[-1] + 1)
        event(A("EO", sl, S(0, 16)), cs, GO(r, 2, cs, 16), MI(r, cs, 16, 16), MI(r, cs, 48, 16))
        send(A("EO", sl, S(0, 16)), A("E1", sl, S(0, 16)), "a%d" % (2 * r + cs[-1]), -1, 1)

    ts(W_("vw"), W_("vi"), 1023, ALU.bitwise_and); cp(C("l0", 0, 16), W_("vw"))
    ts(both("VV", 3), W_("vi"), -PO, AD)
    act(both("VV", 0), turn(A("VV", 3, S(0, 24)), 1), bias=-63.5); low(both("WW", 0), both("VV", 0), b2)

    for r in range(NR):
        last = r == NR - 1
        for c in range(2): mm(C("msc", 8 * c, 8), C("XA", 2048 + 128 * c, 128), W_("Wu"))
        h1, h2 = hp2(), hp2()
        ts(H(h1), C("msc", 0, 16), -OFF, AD, BIG2, AD); act(H(h2), H(h1), bias=-BIG2)
        U = A("U", S(2 * r, 2 * r + 2), S(0, 8))
        tt(U, C("msc", 0, 16), H(h2), SU); act(M(r, 0, b2, 56), U, bias=-1.0); act(M(r, 1, b2, 56), U, bias=-1.0)
        station(r, 0, 0); station(r, 0, 1)
        for bk, n in (("ex0", 512), ("ex1", 512), ("pen", 128)):
            mm(C(bk, 0, n), C("one", 128, 128), C("Rr", 0, n), True, False)
        h1, h2, alt = hp2(), hp2(), hp2()
        tt(H(h1), both("VV", r), U, AD); ts(H(h2), H(h1), 2048.0 - PO, GE, -2048.0, MU); tt(H(alt), H(h1), H(h2), AD)
        diff(r, 0, b2)
        station(r, 1, 0)
        mm(C("msc", 0, 256), W_("hI"), C("XA", 2048, 256), True, False)
        mm(C("msc", 0, 256), W_("hI"), C("zl", 768 * r, 256), False, True)
        ts(W_("zt"), C("msc", 0, 256), -0.25, AD, BIG0, AD)
        act(C("XA", 2048, 256), W_("zt"), bias=-BIG0)
        if last: dma("Y", W_("yz"), C("XA", 2048, 256), 65536)
        if not O["e0"]: local_event(r, 0, (0,))
        station(r, 1, 1)
        twice("OWB%d" % r)
        local_event(r, 0, b2 if O["e0"] else (1,))
        station(r, 2, 0)
        if not O["e1"]: back_event(r, (0,))
        station(r, 2, 1)
        back_event(r, b2 if O["e1"] else (1,))
        low(MI(r, b2, 8), MI(r, b2, 16), b2); diff(r, 2, b2); act(M(r, 2, b2, 56), MI(r, b2, 56))
        if not last:
            h1 = hp2(); tt(H(h1), GO(r, 0, b2), GO(r, 1, b2), SU); tt(A("MO", r * 8 + 6, S(32, 48)), H(h1), GO(r, 2, b2), AD)
        station(r, 3, 0)
        if not O["e1"]: far_hist(r, 1, (0,))
        local_event(r, 2, (0,))
        station(r, 3, 1)
        far_hist(r, 1, b2 if O["e1"] else (1,))
        local_event(r, 2, (1,))
        far_hist(r, 3, (0,))
        if not last:
            for k, (sg, x) in enumerate(((1, GO(r, 0, b2)), (0, MI(r, b2, 24)), (1, GO(r, 2, b2)), (0, A("E3", 2 * r, S(16, 32))))):
                mm(C("msc", 0, 16), C("oneF", 128 * sg, 128), x, k == 0, k == 3)
            tt(C("cn", 0, 16), C("msc", 0, 16), W_("BM"), MU); red(C("cn", 16, 1), C("cn", 0, 16))
            ts(C("cn", 17, 1), C("cn", 16, 1), -1.5, AD, BIG4, AD)
            ts(C("cn", 18, 1), C("cn", 17, 1), BIG4, SU, -28.5, AD)
            ts(C("cn", 19, 1), C("cn", 16, 1), C("cn", 18, 1), SU, 1 / 32.0, MU)
            sc = C("OWA", 0, 1)
            add("V", "rcp", [sc, C("cn", 19, 1)], [sc], [C("cn", 19, 1)], 250)
            scales(sc, 256)
        for h in range(2): mm(W_("d%d" % h), W_("If"), C("OWA", 8 + 512 * h, 512), True, False)["up"] = O["pre"]
        for h in range(2): flex(lambda: act(C("exs", 512 * h, 512), W_("ex%d" % h)), lambda: cp(C("exs", 512 * h, 512), W_("ex%d" % h)), O["pe"])
        for x in range(8): mm(C("d%d" % (x // 4), 128 * (x % 4), 128), A("exs", S(x, 1024, 8)), W_("Dm"), False, x % 4 == 3)
        for h in range(2):
            d = W_("d%d" % h); rm = C("Rm", 512 * h, 512)
            if h < O["rs2"]: act(rm, d, bias=BIG2); act(rm, rm, bias=-BIG2)
            else: ts(rm, d, BIG2, AD, BIG2, SU)
            tt(C("OWA", 8 + 512 * h, 512), d, rm, SU)
        if last:
            act(W_("d1"), C("OWA", 520, 512), bias=OFF * 2049, scale=2048.0)
            for h in range(2):
                tt(C("ynb", 256 * h, 256), C("d1", 256 * h, 256), C("OWA", 8 + 256 * h, 256), AD)
                dma("Y", C("yn", 256 * h, 256), C("ynb", 256 * h, 256), 131072)
        else:
            copies(r + 1, "o")
            scales(C("OWB%d" % (r + 1), 0, 1), 512)
        h1, h2 = hp2(), hp2()
        tt(H(h1), A("FI", S(2 * r, 2 * r + 2), S(0, 8)), H(alt), SU); tt(H(h2), H(h1), GO(r, 0, b2), MU); tt(both("VV", r + 1), H(h2), H(alt), AD)
        if last:
            ts(W_("yvb"), turn(A("VV", r + 1, S(0, 24)), 1), 1024.0, AD); dma("Y", W_("yv"), W_("yvb"), 8192)
        else:
            low(both("WW", r + 1), both("VV", r + 1), b2)
            ts(C("l0", 16 * (r + 1), 16), turn(A("WW", r + 1, S(0, 24)), 1), 1024.0, AD)
        far_hist(r, 3, (1,))
        flex(lambda: act(W_("hit"), C("pen", 0, 128)), lambda: cp(W_("hit"), C("pen", 0, 128)))
        mm(C("pen", 128, 128), W_("hit"), W_("Dh"))
        flex(lambda: act(W_("hitT"), C("pen", 128, 128), fn=ACT.Sign), lambda: ts(W_("hitT"), C("pen", 128, 128), 0.5, GT))
        banks = ("key", "d2", "ex0", "ex1")
        for q, bk in enumerate(banks): mm(W_(bk), W_("Ib"), C("XA", 512 * q, 512), True, False)
        for q, bk in enumerate(banks):
            xb = C("XA", 512 * q, 512)
            for i in range(4): mm(C(bk, 128 * i, 128), C("Sel", 128 * (4 * q + i), 128), W_("hitT"), False, i == 3)
            flex(lambda: act(xb, W_(bk), fn=ACT.Relu), lambda: ts(xb, W_(bk), 0.0, MX))
            if last: dma("Y", C("yx", 512 * q, 512), xb, 131072)
        if not last: copies(r + 1, "x"); twice("OWA")
        cnt["d"] = 0
    return ops


def meet(a, b):
    if a["hi"] <= b["lo"] or b["hi"] <= a["lo"]: return False
    return a["set"] is None or not a["set"].isdisjoint(b["set"])


def plan_order(K=COST, O=OPT, WIN=150, FILL=60):
    ops = build_ops(K, O); acc = {}; SYNC = K["SYNC"]
    for op in ops:
        deps = {}
        e = op["e"]; eng = e if "sem" not in op and "alt" not in op else None
        for p in op.get("after", []): deps[p] = "msg"
        if op.get("behind") is not None: deps[op["behind"]] = "order"
        if "left" in op: deps[op["left"]] = "sem"
        uses = [(a, False) for a in op["r"]] + [(a, True) for a in op["w"]]
        for a, wr in uses:
            for (p, pa, pwr, pe) in acc.get(a["n"], []):
                if p == op["id"] or not (a["ps"] or meet(a, pa)): continue
                if a["n"] == "Rr" and wr and pwr: continue
                same = pe is not None and pe == eng
                if not (wr or pwr or (a["ps"] and not same)): continue
                if same and eng == "P": deps.setdefault(p, "order")
                else: deps[p] = "sem"
        for a, wr in uses:
            lst = acc.setdefault(a["n"], [])
            if wr and a["ps"]: lst[:] = []
            elif wr and a["set"] is not None: lst[:] = [x for x in lst if x[0] == op["id"] or not x[1]["set"] <= a["set"]]
            elif wr and a["k"] == a["hi"] - a["lo"]: lst[:] = [x for x in lst if x[0] == op["id"] or not (a["lo"] <= x[1]["lo"] and x[1]["hi"] <= a["hi"])]
            lst.append((op["id"], a, wr, eng))
        op["deps"] = deps
    n = len(ops); succ = [[] for _ in range(n)]
    for op in ops:
        for p in op["deps"]: succ[p].append(op["id"])
    lev = [0.0] * n
    for op in reversed(ops):
        i = op["id"]; m = 0.0
        for s in succ[i]: m = max(m, lev[s] + (0 if ops[s]["deps"][i] == "order" else op["lat"] + SYNC))
        lev[i] = m + op["busy"] + (op["lat"] if not succ[i] else 0)
    sq = [op["seq"] for op in ops]
    for op in reversed(ops):
        for p in op["deps"]: sq[p] = min(sq[p], sq[op["id"]])
    for i in range(n): lev[i] += ops[i].get("up", 0) - O["w"] * sq[i]
    left = [len(op["deps"]) for op in ops]; rt = [0.0] * n; st = [0.0] * n; fin = [0.0] * n
    free = {}; order = []; pool = {}

    def enter(i):
        pool.setdefault(ops[i]["e"], []).append(i)
        if "alt" in ops[i]: pool.setdefault(ops[i]["alt"]["e"], []).append(i)

    for i in range(n):
        if left[i] == 0: enter(i)
    while any(pool.values()):
        late = lambda i, e: rt[i] + (ops[i].get("pen", 0.0) if ops[i]["e"] != e else 0.0)
        tmin = {e: max(min(late(i, e) for i in l), free.get(e, 0.0) if e else 0.0) for e, l in pool.items() if l}
        e0 = min(tmin, key=lambda k: tmin[k]); t0 = tmin[e0]
        busy = lambda i: ops[i]["busy"] if ops[i]["e"] == e0 else ops[i]["alt"]["busy"]
        best = max((i for i in pool[e0] if late(i, e0) <= t0 + WIN), key=lambda i: lev[i])
        if e0 and rt[best] > t0:
            fill = [i for i in pool[e0] if max(late(i, e0), t0) + busy(i) <= rt[best] + FILL]
            if fill: best = max(fill, key=lambda i: lev[i])
        i = best; op = ops[i]
        pool[op["e"]].remove(i)
        if "alt" in op:
            pool[op["alt"]["e"]].remove(i)
            if op["e"] != e0: op.update(op["alt"]); op["swapped"] = True
        st[i] = max(rt[i], free.get(e0, 0.0)) if e0 else rt[i]
        if e0: free[e0] = st[i] + op["busy"]
        fin[i] = st[i] + op["busy"] + op["lat"]; order.append(i)
        for s in succ[i]:
            k = ops[s]["deps"][i]
            rt[s] = max(rt[s], st[i] if k == "order" else fin[i] + (SYNC if k == "sem" else 0))
            left[s] -= 1
            if left[s] == 0: enter(s)
    cntq = {}
    for i in order:
        op = ops[i]
        if "sem" in op: op["clk"] = (op["sem"], 1)
        else:
            cntq[op["e"]] = cntq.get(op["e"], 0) + 1; op["clk"] = (op["e"], cntq[op["e"]])
    know = {}; need = set()
    for i in order:
        op = ops[i]; op["waits"] = []
        if op["e"] is None:
            op["know"] = {}; continue
        kn = know.setdefault(op["e"], {})
        for p in sorted((p for p, k in op["deps"].items() if k == "sem"), key=lambda p: -fin[p]):
            key, val = ops[p]["clk"]
            if kn.get(key, 0) >= val: continue
            op["waits"].append(p); need.add(p); kn[key] = val
            for a, b in ops[p]["know"].items():
                if kn.get(a, 0) < b: kn[a] = b
        op["know"] = dict(kn)
    num = {}
    for i in order:
        op = ops[i]
        if "sem" not in op and i in need:
            num[op["e"]] = num.get(op["e"], 0) + 1; op["sig"] = ("c" + op["e"], num[op["e"]])
    return {"ops": ops, "order": order, "need": need, "span": max(fin), "st": st, "fin": fin}


PLAN = {}


def view(T, a):
    if not isinstance(a, dict): return a
    v = T[a["n"]][(slice(*a.get("p", (None,))),) + tuple(a["i"])]
    if a["ind"] is not None: v = v.indirect(view(T, a["ind"]))
    return v


def helpers(T, topo, rank):
    me = T.cores[rank]; n = len(T.cores)
    far = [T.cores[(rank + k) % n] for k in (1, -1)]
    ok = [c for c in topo.cores_of(me) if c != me and T.rank_of(c) is None and all(topo.may_write(c, f) for f in far)]
    ok.sort(key=lambda c: topo.die(c) != topo.die(me))
    return [ok[k % len(ok)] for k in range(4)]


def first_hop(T, topo, rank, op):
    me = T.cores[rank]; hs = helpers(T, topo, rank); out = []
    for k, (via, _s, _d) in enumerate(op["pieces"]):
        to = T.cores[(rank + op["dist"]) % len(T.cores)] if via is None else hs[via]
        engs = topo.engines(me, to); m = len(engs) // len(op["pieces"])
        out.append((to, engs[k * m:(k + 1) * m]))
    return out


def arrivals(T, topo, rank, ops, o):
    n = len(T.cores); total = 0
    for p in o["after"]:
        frm = (rank - ops[p]["dist"]) % n
        for (via, _s, _d), (to, engs) in zip(ops[p]["pieces"], first_hop(T, topo, frm, ops[p])):
            total += len(engs) if via is None else len(topo.engines(to, T.cores[rank]))
    return total


def bits(engs):
    return sum(1 << e for e in engs)


def rank_program(g, core, T, topo):
    if not PLAN: PLAN.update(plan_order())
    ops, order = PLAN["ops"], PLAN["order"]
    n = len(T.cores); rank = T.rank_of(core)
    if rank is None:
        for rk in range(n):
            if core not in helpers(T, topo, rk): continue
            sent = 0
            for i in order:
                op = ops[i]
                if op["call"] != "send": continue
                for (via, _s, dst), (h, engs) in zip(op["pieces"], first_hop(T, topo, rk, op)):
                    if via is None or h != core: continue
                    to = T.cores[(rk + op["dist"]) % n]; rid, pid = topo.addr(to, core)
                    g.wait_ge(T.sem[op["rsem"]], len(engs))
                    g.remote_dma(view(T, dst), view(T, dst), T.sem[op["rsem"]], T.sem.sent, pid, rid, topo.mask(core, to))
                    sent += len(topo.engines(core, to))
            g.wait_ge(T.sem.sent, sent)
        return
    Q = {"V": g.vector, "S": g.scalar, "P": g.tensor, "G": g, "Y": g.sync}

    def wait(q, o):
        if o["call"] == "arrive": q.wait_ge(T.sem[o["sem"]], arrivals(T, topo, rank, ops, o))
        elif o["call"] == "send": q.wait_ge(T.sem[o["sem"]], sum(len(e) for _c, e in first_hop(T, topo, rank, o)))
        elif o["call"] == "dma": q.wait_ge(T.sem[o["sem"]], 16)
        else: q.wait_ge(T.sem[o["sig"][0]], o["sig"][1])

    sent = 0
    for i in order:
        op = ops[i]
        if op["e"] is None: continue
        q = Q[op["e"]]
        for p in op["waits"]: wait(q, ops[p])
        a = [view(T, x) for x in op["args"]]; kw = {k: view(T, x) for k, x in op["kw"].items()}; c = op["call"]
        if c == "send":
            loc = T.sem[op.get("sem", "sent")]; trs = []
            for (_v, src, dst), (to, engs) in zip(op["pieces"], first_hop(T, topo, rank, op)):
                rid, pid = topo.addr(to, core)
                if "sem" not in op: sent += len(engs)
                if len(op["pieces"]) == 1: g.remote_dma(view(T, dst), view(T, src), T.sem[op["rsem"]], loc, pid, rid, bits(engs))
                else: trs.append(RemoteDMATransfer(dst_ids=[DstId(rid=rid, pnc=pid)], dma_engine_mask=bits(engs), remote_sem=T.sem[op["rsem"]],
                                                   src=view(T, src), dst=view(T, dst)))
            if trs: g.remote_dma_fused(trs, local_sem=loc)
            continue
        if c == "dma":
            q.dma_start(a[0], a[1]).then_inc(T.sem[op["sem"]], 16); continue
        if c == "ts": ins = q.tensor_scalar(*a)
        elif c == "tt": ins = q.tensor_tensor(*a)
        elif c == "cp": ins = q.tensor_copy(*a)
        elif c == "scan": ins = q.tensor_tensor_scan(*a)
        elif c == "ms": ins = q.memset(*a)
        elif c == "red": ins = q.tensor_reduce(*a)
        elif c == "rcp": ins = q.reciprocal(*a)
        elif c == "act": ins = q.activation(*a, **kw)
        elif c == "mm": ins = q.matmul(*a)
        elif c == "sel": ins = q.affine_select(*a)
        else: ins = q.iota(*a, **kw)
        if "sig" in op: ins.then_inc(T.sem[op["sig"][0]], 1)
    g.wait_ge(T.sem.sent, sent)
    for i in order:
        if "sem" in ops[i] and i not in PLAN["need"]: wait(g.sync, ops[i])
